import numpy as np
import ml_dtypes


def mxq(x, axis, fmt="e4m3"):
    dtype, down = {"e4m3": (ml_dtypes.float8_e4m3fn, 7), "e5m2": (ml_dtypes.float8_e5m2, 14)}[fmt]
    v = np.moveaxis(np.asarray(x, np.float32).astype(ml_dtypes.bfloat16).astype(np.float64), axis, -1)
    blocks = v.reshape(v.shape[:-1] + (-1, 32))
    amax = np.abs(blocks).max(-1, keepdims=True)
    byte = np.maximum(np.where(amax > 0, np.frexp(amax)[1] - 1 + 127, 0) - down, 1)
    scale = np.exp2(byte - 127.0)
    codes = (blocks / scale).astype(np.float32).astype(dtype).astype(np.float64)
    return np.moveaxis((codes * scale).reshape(v.shape), -1, axis)


WIDE = False


def mx_kscale(k):
    if not WIDE:
        return np.ones(k)
    levels = np.array([10, -10, 5, -5, 0])
    if k % 512:
        return np.exp2(np.random.permutation(np.resize(levels, k // 32))).repeat(32)
    a = np.empty((k // 512, 16))
    for p in range(k // 512):
        a[p, :8] = np.random.permutation(np.resize(levels, 8))
        for g in range(8):
            far = levels[np.abs(levels - a[p, g]) >= 10]
            a[p, g + 8] = far[np.random.randint(len(far))]
    return np.exp2(a.ravel()).repeat(32)


def f64(x):
    return np.asarray(x).astype(np.float64)


def striped(idx):
    return np.tile(idx.reshape(-1, 16).T, (8, 1)).astype(np.uint16)


def unstriped(offs):
    return offs[:16].T.reshape(-1).astype(np.int64)


E2M1 = np.array([0.0, 0.5, 1.0, 1.5, 2.0, 3.0, 4.0, 6.0, -0.0, -0.5, -1.0, -1.5, -2.0, -3.0, -4.0, -6.0])


def pack_weight(w, fmt):
    k, n = w.shape
    w = f64(np.asarray(w, np.float32).astype(ml_dtypes.bfloat16)).reshape(k // 32, 32, n)
    amax = np.abs(w).max(1)
    if fmt == "e4m3":
        byte = np.frexp(amax)[1] - 1 + 127 - 7
    else:
        mant, ex = np.frexp(amax / 6.0)
        byte = np.where(mant > 0.5, ex, ex - 1) + 127
    byte = np.clip(np.where(amax > 0, byte, 1), 1, 254)
    scaled = (w * np.exp2(127.0 - byte)[:, None, :]).reshape(k, n).astype(np.float32)
    by_word = np.ascontiguousarray(scaled.reshape(k // 512, 128, 4, n).transpose(0, 1, 3, 2))
    if fmt == "e4m3":
        words = by_word.astype(ml_dtypes.float8_e4m3fn).view(np.uint8)
    else:
        c = by_word.astype(ml_dtypes.float4_e2m1fn).view(np.uint8) & 0xF
        words = (c[..., 0::2] | (c[..., 1::2] << 4)).reshape(k // 512, 128, 2 * n)
    return np.ascontiguousarray(words), np.ascontiguousarray(byte.astype(np.uint8).reshape(k // 512, 16, n))


def unpack_weight(words, scales, fmt):
    g, _, n = scales.shape
    words = np.ascontiguousarray(words).reshape(g, 128, n, -1)
    if fmt == "e4m3":
        vals = words.view(ml_dtypes.float8_e4m3fn).astype(np.float64)
    else:
        nib = np.empty((g, 128, n, 4), np.uint8)
        nib[..., 0::2] = words & 0xF
        nib[..., 1::2] = words >> 4
        vals = E2M1[nib]
    vals = vals * np.repeat(np.exp2(scales.astype(np.float64) - 127.0), 8, axis=1)[..., None]
    return vals.transpose(0, 1, 3, 2).reshape(g * 512, n)


def gelu(v):
    return 0.5 * v * (1.0 + np.tanh(np.sqrt(2.0 / np.pi) * (v + 0.044715 * v**3)))


def striped8(idx):
    return np.concatenate([v.reshape(-1, 16).T for v in idx]).astype(np.uint16)


def unstriped8(offs):
    return np.stack([offs[16 * g:16 * g + 16].T.reshape(-1) for g in range(8)]).astype(np.int64)


def runs(v, idx8):
    k = np.arange(v.shape[0])
    return v[k[:, None], idx8[k % 512 // 64]]


K, T, S, H, N = 1536, 2048, 1024, 512, 384


def setup_inputs():
    n = np.random.standard_normal
    s = mx_kscale(K)[:, None]
    u = mx_kscale(H)[:, None]
    tab_words, tab_scales = pack_weight(n((K, T)) * s, "e4m3")
    offs = striped8(np.stack([np.random.permutation(T)[:S] for _ in range(8)]))
    w1_words, w1_scales = pack_weight(1.5 * n((K, H)) / np.sqrt(K) / s, "e2m1")
    w2 = (n((K, H)) / np.sqrt(K) / s * u.T).astype(np.float32)
    w3_words, w3_scales = pack_weight(0.6 * n((K, H)) / np.sqrt(K) / s * u.T, "e4m3")
    w4 = (1.5 * n((H, N)) / np.sqrt(H) / u).astype(np.float32)
    drift = (0.4 * n(N)).astype(np.float32)
    return {"tab_words": tab_words, "tab_scales": tab_scales, "offs": offs,
            "w1_words": w1_words, "w1_scales": w1_scales, "w2": w2,
            "w3_words": w3_words, "w3_scales": w3_scales,
            "w4": w4, "drift": drift}


def reference(tab_words, tab_scales, offs, w1_words, w1_scales, w2,
              w3_words, w3_scales, w4, drift):
    v = runs(unpack_weight(tab_words, tab_scales, "e4m3"), unstriped8(offs))
    a = unpack_weight(w1_words, w1_scales, "e2m1").T @ v
    b = mxq(f64(w2), 0, "e4m3").T @ v
    c = unpack_weight(w3_words, w3_scales, "e4m3").T @ v
    h = a / (1.0 + np.abs(a)) * b - c
    y = mxq(f64(w4), 0, "e4m3").T @ mxq(h, 0, "e4m3")
    return y + f64(drift)[:, None]

@@ -1,0 +1,300 @@
+from contextlib import ExitStack
+
+import concourse.mybir as mybir
+
+K, T, S, H, N = 1536, 2048, 1024, 512, 384
+FLOPS = 2 * (3 * K * H * S + H * N * S)
+
+F32 = mybir.dt.float32
+BF16 = mybir.dt.bfloat16
+I32 = mybir.dt.int32
+U32 = mybir.dt.uint32
+U16 = mybir.dt.uint16
+U8 = mybir.dt.uint8
+FP8X4 = mybir.dt.float8_e4m3fn_x4
+FP4X4 = mybir.dt.float4_e2m1fn_x4
+ACT = mybir.ActivationFunctionType
+ALU = mybir.AluOpType
+
+P = 128
+PASSES = K // 512
+HALF = 512
+SLICE = 128
+TILES = 4
+NT = N // P
+LANE_BYTES = 4 * T
+W1_BYTES = PASSES * 2 * H
+
+
+def tile_list_plankton_tendency_kernel(
+    tc, tab_words, tab_scales, offs, w1_words, w1_scales, w2, w3_words, w3_scales, w4, drift, out
+):
+    nc = tc.nc
+    with ExitStack() as ctx:
+        keep = ctx.enter_context(tc.tile_pool(name="keep", bufs=1))
+        shared = ctx.enter_context(tc.tile_pool(name="shared", bufs=1))
+        ring = ctx.enter_context(tc.tile_pool(name="ring", bufs=2))
+        psum = ctx.enter_context(tc.psum_pool(name="psum", bufs=4))
+
+        def held(name, shape, dtype):
+            return keep.tile(shape, dtype, name=name, align_bytes=64)
+
+        offsets = keep.tile([P, S // 16], U16, name="offsets")
+        nc.sync.dma_start(offsets[:], offs)
+
+        scale_window = shared.tile([P, T], U8, name="scale_window", offset=W1_BYTES + 2 * LANE_BYTES)
+        w_scales_raw = held("w_scales_raw", [P, PASSES, H], U8)
+        v_scales = held("v_scales", [P, 2, S], U8)
+        last_scales = held("last_scales", [P, S], U8)
+        warm = shared.tile([P, 16], F32, name="warm", offset=W1_BYTES - 32)
+        warm_out = shared.tile([P, 16], F32, name="warm_out", offset=W1_BYTES + LANE_BYTES)
+        nc.vector.memset(warm[:], 1.0)
+        nc.scalar.activation(warm_out[:], warm[:], ACT.Abs_reciprocal_sqrt)
+        nc.vector.memset(scale_window[:].bitcast(I32), 0)
+        nc.gpsimd.memset(w_scales_raw[:].bitcast(I32), 0)
+        nc.vector.memset(v_scales[:].bitcast(I32), 0)
+
+        def staged(lane, shape, dtype):
+            if lane >= 1:
+                return shared.tile(shape, dtype, name=f"lane{lane}", tag=f"lane{lane}", offset=W1_BYTES + LANE_BYTES * (lane - 1))
+            return keep.tile(shape, dtype, name=f"lane{lane}", tag=f"lane{lane}", align_bytes=64)
+
+        tab = {}
+
+        def load_tab(a):
+            tab[a] = staged(a, [P, T], I32)
+            nc.sync.dma_start(tab[a][:], tab_words[a].rearrange("p t i -> p (t i)").bitcast(I32))
+
+        load_tab(0)
+        tab_scale_words = tab_scales.bitcast(I32)
+        for a in range(2):
+            nc.sync.dma_start(scale_window[2 + 4 * a : P : 8, :].bitcast(I32), tab_scale_words[a])
+        for r in range(2):
+            nc.sync.dma_start(scale_window[r:P:16, :].bitcast(I32), tab_scale_words[2, r:16:2, :])
+        w1_raw = shared.tile([P, PASSES, 2 * H], U8, name="w1_raw", offset=0)
+        nc.sync.dma_start(w1_raw[:].bitcast(I32), w1_words.bitcast(I32).rearrange("a p n -> p a n"))
+        load_tab(1)
+        load_tab(2)
+
+        for d in range(4):
+            nc.gpsimd.dma_start(
+                w_scales_raw[32 * d : 32 * d + 4, :, :].bitcast(I32),
+                w1_scales.bitcast(I32)[:, 4 * d : 4 * d + 4, :].rearrange("a r n -> r a n"),
+            )
+
+        drift_cols = held("drift_cols", [P, NT], F32)
+        with nc.allow_non_contiguous_dma(reason="one drift value for each partition and tile of out"):
+            nc.gpsimd.dma_start(drift_cols[:], drift.rearrange("(m p) -> p m", p=P))
+
+        gathered_scales = shared.tile(
+            [P, S], U8, name="gathered_scales", offset=W1_BYTES + 4 * LANE_BYTES - S // 2
+        )
+        nc.vector.tensor_copy(gathered_scales[:], scale_window[:].indirect(offsets[:]))
+
+        for d in range(4):
+            nc.scalar.dma_start(
+                v_scales[32 * d : 32 * d + 4, :, :].bitcast(I32),
+                gathered_scales[32 * d + 2 : 32 * d + 32 : 4, :].bitcast(I32),
+            )
+        nc.vector.tensor_copy(last_scales[:].bitcast(I32), gathered_scales[:].bitcast(I32))
+        for r in range(2):
+            nc.scalar.dma_start(
+                last_scales[2 + r : P : 32, :].bitcast(I32), gathered_scales[16 + r : P : 32, :].bitcast(I32)
+            )
+        w2_raw = {}
+
+        def load_w2(a):
+            w2_raw[a] = staged(a + 3, [P, 4, H], F32)
+            nc.sync.dma_start(w2_raw[a][:], w2[512 * a : 512 * (a + 1), :].rearrange("(p j) c -> p j c", j=4))
+
+        load_w2(0)
+        load_w2(1)
+        load_w2(2)
+
+        v_words = {}
+
+        def gather_words(a, half):
+            v_words[a, half] = held(f"v_words{a}_{half}", [P, HALF], U32)
+            cols = offsets[:, half * (HALF // 16) : (half + 1) * (HALF // 16)]
+            nc.vector.tensor_copy(v_words[a, half][:], tab[a][:].bitcast(U32).indirect(cols))
+
+        def permute_columns(name, raw, dtype):
+            done = held(name, list(raw.shape), dtype)
+            nc.vector.tensor_copy(
+                done[:].bitcast(I32).rearrange("p a (t q w) -> p a t q w", t=TILES, q=16),
+                raw[:].bitcast(I32).rearrange("p a (q t w) -> p a t q w", t=TILES, q=16),
+            )
+            return done
+
+        gather_words(0, 0)
+        w1_codes = permute_columns("w1_codes", w1_raw, U8)
+        w1_scale_rows = permute_columns("w1_scale_rows", w_scales_raw, U8)
+        for d in range(4):
+            nc.gpsimd.dma_start(
+                w_scales_raw[32 * d + 4 : 32 * d + 16, 0, :].bitcast(I32),
+                w3_scales.bitcast(I32)[:, 4 * d : 4 * d + 4, :],
+            )
+        gather_words(1, 0)
+        gather_words(0, 1)
+        gather_words(2, 0)
+        gather_words(1, 1)
+        gather_words(2, 1)
+
+        w2_codes = [held(f"w2_codes{a}", [P, H], U32) for a in range(PASSES)]
+        w2_scales = [held(f"w2_scales{a}", [P, H], U8) for a in range(PASSES)]
+        w2_bf = [held(f"w2_bf{a}", [P, 4 * H], BF16) for a in range(PASSES)]
+
+        def round_w2(a):
+            nc.vector.tensor_copy(
+                w2_bf[a][:].rearrange("p (t q i j) -> p t q j i", t=TILES, q=16, j=4),
+                w2_raw[a][:].rearrange("p j (q t i) -> p t q j i", t=TILES, q=16),
+            )
+
+        def quantise_w2(a):
+            nc.vector.quantize_mx(out=w2_codes[a][:].bitcast(FP8X4), scales=w2_scales[a][:], in_=w2_bf[a][:])
+
+        def mx_pass(acc, codes, scales, a, lo, width):
+            half, at = divmod(lo, HALF)
+            nc.tensor.matmul_mx(
+                out=acc,
+                lhsT=codes,
+                lhsT_scale=scales,
+                rhs=v_words[a, half][:, at : at + width].bitcast(FP8X4),
+                rhs_scale=(v_scales[:, a, :] if a < 2 else last_scales[:])[:, lo : lo + width],
+                start=(a == 0),
+                stop=(a == PASSES - 1),
+            )
+
+        def a_pass(acc, a, half, t):
+            mx_pass(acc[:], w1_codes[:, a, 2 * P * t : 2 * P * (t + 1)].bitcast(FP4X4),
+                    w1_scale_rows[:, a, P * t : P * (t + 1)], a, HALF * half, HALF)
+
+        def b_pass(acc, a, half, t):
+            mx_pass(acc[:], w2_codes[a][:, P * t : P * (t + 1)].bitcast(FP8X4),
+                    w2_scales[a][:, P * t : P * (t + 1)], a, HALF * half, HALF)
+
+        soft = {}
+
+        def saturate_uptake(acc, half, t):
+            mag = ring.tile([P, HALF], F32, name="mag")
+            root = ring.tile([P, HALF], F32, name="root")
+            inv = ring.tile([P, HALF], F32, name="inv")
+            nc.scalar.activation(mag[:], acc[:], ACT.Abs)
+            nc.scalar.activation(root[:], mag[:], ACT.Abs_reciprocal_sqrt, bias=1.0)
+            nc.scalar.activation(inv[:], root[:], ACT.Square)
+            soft[half, t] = held(f"soft{half}_{t}", [P, HALF], F32)
+            nc.vector.tensor_tensor(soft[half, t][:], acc[:], inv[:], ALU.mult)
+
+        def bank(tag):
+            return psum.tile([P, HALF], F32, name=tag, tag=tag)
+
+        a_banks = [bank("first") for t in range(TILES)]
+        for t in range(TILES):
+            for a in range(PASSES):
+                a_pass(a_banks[t], a, 0, t)
+
+        def uptake(half, t):
+            acc = bank("first")
+            for a in range(PASSES):
+                a_pass(acc, a, half, t)
+            return acc
+
+        b_banks = [bank("second") for t in range(TILES)]
+        later = {}
+        for a in range(PASSES):
+            round_w2(a)
+            if a == 0:
+                w3_raw = staged(3, [P, PASSES, H], I32)
+                nc.sync.dma_start(w3_raw[:], w3_words.rearrange("a p e i -> p a (e i)").bitcast(I32))
+            if a == 1:
+                w4_raw = staged(4, [P, TILES, N], F32)
+                w4_rows = w4.rearrange("(q t i) n -> t q i n", t=TILES, i=8)
+                for t in range(TILES):
+                    nc.sync.dma_start(w4_raw[:, t, :], w4_rows[t])
+            saturate_uptake(a_banks[a], 0, a)
+            quantise_w2(a)
+            later[a] = uptake(1, a)
+            for t in range(TILES):
+                b_pass(b_banks[t], a, 0, t)
+        saturate_uptake(a_banks[3], 0, 3)
+        later[3] = uptake(1, 3)
+        w3_scale_rows = permute_columns("w3_scale_rows", w_scales_raw[:, 0:1, :], U8)
+        w3_codes = permute_columns("w3_codes", w3_raw, U32)
+
+        growth = [held(f"growth{half}", [P, TILES, HALF], F32) for half in range(2)]
+
+        def grow(acc, half, t):
+            nc.vector.tensor_tensor(growth[half][:, t, :], acc[:], soft[half, t][:], ALU.mult)
+
+        b_later = {}
+        for t in range(TILES):
+            grow(b_banks[t], 0, t)
+            saturate_uptake(later[t], 1, t)
+            b_later[t] = bank("second")
+            for a in range(PASSES):
+                b_pass(b_later[t], a, 1, t)
+
+        w4_bf = held("w4_bf", [P, 4 * N], BF16)
+        w4_codes = held("w4_codes", [P, N], U32)
+        w4_scales = held("w4_scales", [P, N], U8)
+        nc.scalar.copy(
+            w4_bf[:].rearrange("p (c i t) -> p c t i", t=TILES, i=4),
+            w4_raw[:].rearrange("p t (c i) -> p c t i", i=4),
+        )
+        for lo, hi in ((0, 256), (256, N)):
+            nc.vector.quantize_mx(out=w4_codes[:, lo:hi].bitcast(FP8X4), scales=w4_scales[:, lo:hi],
+                                  in_=w4_bf[:, 4 * lo : 4 * hi])
+
+        def mortality(j):
+            acc = bank("first")
+            for t in range(TILES):
+                for a in range(PASSES):
+                    mx_pass(acc[:, SLICE * t : SLICE * (t + 1)],
+                            w3_codes[:, a, P * t : P * (t + 1)].bitcast(FP8X4),
+                            w3_scale_rows[4 * (a + 1) : P, 0, P * t : P * (t + 1)], a, SLICE * j, SLICE)
+            return acc
+
+        def net_growth(acc, j):
+            half, at = divmod(SLICE * j, HALF)
+            h_bf = ring.tile([P, 4 * SLICE], BF16, name="h_bf", align_bytes=64)
+            nc.vector.tensor_tensor(
+                h_bf[:].rearrange("p (c i t) -> p c t i", t=TILES, i=4),
+                growth[half][:, :, at : at + SLICE].rearrange("p t (c i) -> p c t i", i=4),
+                acc[:].rearrange("p (t c i) -> p c t i", t=TILES, i=4),
+                ALU.subtract,
+            )
+            return h_bf
+
+        def tendencies(h_bf, j):
+            h_codes = ring.tile([P, SLICE], U32, name="h_codes", align_bytes=64)
+            h_scales = ring.tile([P, SLICE], U8, name="h_scales", align_bytes=64)
+            nc.vector.quantize_mx(out=h_codes[:].bitcast(FP8X4), scales=h_scales[:], in_=h_bf[:])
+            acc = bank("second")
+            result = ring.tile([P, NT, SLICE], F32, name="result", bufs=4)
+            for m in range(NT):
+                nc.tensor.matmul_mx(
+                    out=acc[:, SLICE * m : SLICE * (m + 1)],
+                    lhsT=w4_codes[:, P * m : P * (m + 1)].bitcast(FP8X4),
+                    lhsT_scale=w4_scales[:, P * m : P * (m + 1)],
+                    rhs=h_codes[:].bitcast(FP8X4),
+                    rhs_scale=h_scales[:],
+                    start=True,
+                    stop=True,
+                )
+            for m in range(NT):
+                nc.scalar.activation(result[:, m, :], acc[:, SLICE * m : SLICE * (m + 1)], ACT.Identity,
+                                     bias=drift_cols[:, m : m + 1])
+            nc.sync.dma_start(
+                out[:, SLICE * j : SLICE * (j + 1)].rearrange("(m p) s -> p m s", p=P), result[:]
+            )
+
+        pending = None
+        for j in range(S // SLICE):
+            acc = mortality(j)
+            h_bf = net_growth(acc, j)
+            if j < TILES:
+                grow(b_later[j], 1, j)
+            if pending is not None:
+                tendencies(*pending)
+            pending = (h_bf, j)
+        tendencies(*pending)

@@ -22,8 +22,39 @@ HALF = 512
 SLICE = 128
 TILES = 4
 NT = N // P
-LANE_BYTES = 4 * T
-W1_BYTES = PASSES * 2 * H
+AT = {
+    "w3_codes": 0,
+    "w2_bf0": 2048,
+    "w2_bf2": 2048,
+    "scale_window": 6016,
+    "w1_codes": 7936,
+    "v_words0_0": 11008,
+    "w1_raw": 12928,
+    "w1_scales_first": 13056,
+    "v_words0_1": 13824,
+    "w2_raw1": 15872,
+    "w4_raw": 15872,
+    "gathered_scales": 24064,
+    "drift_cols": 24064,
+    "w2_raw2": 24128,
+    "v_words1_0": 32320,
+    "tab0": 33344,
+    "v_words1_1": 34368,
+    "w2_codes0": 36416,
+    "v_words2_0": 38464,
+    "v_words2_1": 40512,
+    "w2_raw0": 42560,
+    "warm": 50720,
+    "tab1": 50752,
+    "w3_raw": 50752,
+    "tab2": 58944,
+    "warm_out": 58944,
+    "w3_scale_rows": 58944,
+    "w1_scales_rest": 59456,
+    "w2_bf1": 60224,
+    "root1_1": 67136,
+    "w4_bf": 67136,
+}
 
 
 def tile_list_plankton_tendency_kernel(
@@ -37,42 +68,48 @@ def tile_list_plankton_tendency_kernel(
         psum = ctx.enter_context(tc.psum_pool(name="psum", bufs=4))
 
         def held(name, shape, dtype):
+            if name in AT:
+                return shared.tile(shape, dtype, name=name, align_bytes=32 if name == "warm" else 64, offset=AT[name])
             return keep.tile(shape, dtype, name=name, align_bytes=64)
 
         offsets = keep.tile([P, S // 16], U16, name="offsets")
         nc.sync.dma_start(offsets[:], offs)
 
-        scale_window = shared.tile([P, T], U8, name="scale_window", offset=W1_BYTES + 2 * LANE_BYTES)
+        scale_window = held("scale_window", [P, T], U8)
         w_scales_raw = held("w_scales_raw", [P, PASSES, H], U8)
-        v_scales = held("v_scales", [P, 2, S], U8)
-        last_scales = held("last_scales", [P, S], U8)
-        warm = shared.tile([P, 16], F32, name="warm", offset=W1_BYTES - 32)
-        warm_out = shared.tile([P, 16], F32, name="warm_out", offset=W1_BYTES + LANE_BYTES)
-        nc.vector.memset(warm[:], 1.0)
-        nc.scalar.activation(warm_out[:], warm[:], ACT.Abs_reciprocal_sqrt)
+        v_scales = held("v_scales", [P, PASSES, S], U8)
+        warm = held("warm", [P, 16], F32)
+        warm_out = held("warm_out", [P, 16], F32)
         nc.vector.memset(scale_window[:].bitcast(I32), 0)
         nc.gpsimd.memset(w_scales_raw[:].bitcast(I32), 0)
+        nc.vector.memset(warm[:], 1.0)
+        nc.scalar.activation(warm_out[:], warm[:], ACT.Abs_reciprocal_sqrt)
         nc.vector.memset(v_scales[:].bitcast(I32), 0)
-
-        def staged(lane, shape, dtype):
-            if lane >= 1:
-                return shared.tile(shape, dtype, name=f"lane{lane}", tag=f"lane{lane}", offset=W1_BYTES + LANE_BYTES * (lane - 1))
-            return keep.tile(shape, dtype, name=f"lane{lane}", tag=f"lane{lane}", align_bytes=64)
+        w3_scales_raw = held("w3_scales_raw", [P, 1, H], U8)
+        nc.vector.memset(w3_scales_raw[:].bitcast(I32), 0)
 
         tab = {}
 
         def load_tab(a):
-            tab[a] = staged(a, [P, T], I32)
+            tab[a] = held(f"tab{a}", [P, T], I32)
             nc.sync.dma_start(tab[a][:], tab_words[a].rearrange("p t i -> p (t i)").bitcast(I32))
 
         load_tab(0)
         tab_scale_words = tab_scales.bitcast(I32)
-        for a in range(2):
-            nc.sync.dma_start(scale_window[2 + 4 * a : P : 8, :].bitcast(I32), tab_scale_words[a])
-        for r in range(2):
-            nc.sync.dma_start(scale_window[r:P:16, :].bitcast(I32), tab_scale_words[2, r:16:2, :])
-        w1_raw = shared.tile([P, PASSES, 2 * H], U8, name="w1_raw", offset=0)
+        for d in range(4):
+            (nc.scalar, nc.sync)[d % 2].dma_start(
+                scale_window[32 * d + 4 : 32 * d + 28 : 2, :].bitcast(I32),
+                tab_scale_words[:, 4 * d : 4 * d + 4, :].rearrange("a r n -> r a n"),
+            )
+        w1_raw = held("w1_raw", [P, PASSES, 2 * H], U8)
         nc.sync.dma_start(w1_raw[:].bitcast(I32), w1_words.bitcast(I32).rearrange("a p n -> p a n"))
+        w2_raw = {}
+
+        def load_w2(a):
+            w2_raw[a] = held(f"w2_raw{a}", [P, 4, H], F32)
+            nc.sync.dma_start(w2_raw[a][:], w2[512 * a : 512 * (a + 1), :].rearrange("(p j) c -> p j c", j=4))
+
+        load_w2(0)
         load_tab(1)
         load_tab(2)
 
@@ -81,35 +118,24 @@ def tile_list_plankton_tendency_kernel(
                 w_scales_raw[32 * d : 32 * d + 4, :, :].bitcast(I32),
                 w1_scales.bitcast(I32)[:, 4 * d : 4 * d + 4, :].rearrange("a r n -> r a n"),
             )
+        for d in range(4):
+            nc.gpsimd.dma_start(
+                w3_scales_raw[32 * d + 4 : 32 * d + 16, 0, :].bitcast(I32),
+                w3_scales.bitcast(I32)[:, 4 * d : 4 * d + 4, :],
+            )
 
-        drift_cols = held("drift_cols", [P, NT], F32)
-        with nc.allow_non_contiguous_dma(reason="one drift value for each partition and tile of out"):
-            nc.gpsimd.dma_start(drift_cols[:], drift.rearrange("(m p) -> p m", p=P))
-
-        gathered_scales = shared.tile(
-            [P, S], U8, name="gathered_scales", offset=W1_BYTES + 4 * LANE_BYTES - S // 2
-        )
+        gathered_scales = held("gathered_scales", [P, S], U8)
         nc.vector.tensor_copy(gathered_scales[:], scale_window[:].indirect(offsets[:]))
 
         for d in range(4):
             nc.scalar.dma_start(
                 v_scales[32 * d : 32 * d + 4, :, :].bitcast(I32),
-                gathered_scales[32 * d + 2 : 32 * d + 32 : 4, :].bitcast(I32),
+                gathered_scales[32 * d + 4 : 32 * d + 28 : 2, :].bitcast(I32),
             )
-        nc.vector.tensor_copy(last_scales[:].bitcast(I32), gathered_scales[:].bitcast(I32))
-        for r in range(2):
-            nc.scalar.dma_start(
-                last_scales[2 + r : P : 32, :].bitcast(I32), gathered_scales[16 + r : P : 32, :].bitcast(I32)
-            )
-        w2_raw = {}
-
-        def load_w2(a):
-            w2_raw[a] = staged(a + 3, [P, 4, H], F32)
-            nc.sync.dma_start(w2_raw[a][:], w2[512 * a : 512 * (a + 1), :].rearrange("(p j) c -> p j c", j=4))
-
-        load_w2(0)
-        load_w2(1)
         load_w2(2)
+        drift_cols = held("drift_cols", [P, NT], F32)
+        with nc.allow_non_contiguous_dma(reason="one drift value for each partition and tile of out"):
+            nc.gpsimd.dma_start(drift_cols[:], drift.rearrange("(m p) -> p m", p=P))
 
         v_words = {}
 
@@ -118,34 +144,34 @@ def tile_list_plankton_tendency_kernel(
             cols = offsets[:, half * (HALF // 16) : (half + 1) * (HALF // 16)]
             nc.vector.tensor_copy(v_words[a, half][:], tab[a][:].bitcast(U32).indirect(cols))
 
-        def permute_columns(name, raw, dtype):
-            done = held(name, list(raw.shape), dtype)
+        def permute_columns(name, raw, dtype, first=0, count=TILES):
+            done = held(name, [P, raw.shape[1], raw.shape[2] * count // TILES], dtype)
             nc.vector.tensor_copy(
-                done[:].bitcast(I32).rearrange("p a (t q w) -> p a t q w", t=TILES, q=16),
-                raw[:].bitcast(I32).rearrange("p a (q t w) -> p a t q w", t=TILES, q=16),
+                done[:].bitcast(I32).rearrange("p a (t q w) -> p a t q w", t=count, q=16),
+                raw[:].bitcast(I32).rearrange("p a (q t w) -> p a t q w", t=TILES, q=16)[:, :, first : first + count],
             )
             return done
 
-        gather_words(0, 0)
         w1_codes = permute_columns("w1_codes", w1_raw, U8)
-        w1_scale_rows = permute_columns("w1_scale_rows", w_scales_raw, U8)
-        for d in range(4):
-            nc.gpsimd.dma_start(
-                w_scales_raw[32 * d + 4 : 32 * d + 16, 0, :].bitcast(I32),
-                w3_scales.bitcast(I32)[:, 4 * d : 4 * d + 4, :],
-            )
-        gather_words(1, 0)
+        load_w2(1)
+        gather_words(0, 0)
+        w1_scales_first = permute_columns("w1_scales_first", w_scales_raw, U8, 0, 2)
         gather_words(0, 1)
-        gather_words(2, 0)
+        gather_words(1, 0)
         gather_words(1, 1)
+        w3_raw = held("w3_raw", [P, PASSES, H], I32)
+        nc.sync.dma_start(w3_raw[:], w3_words.rearrange("a p e i -> p a (e i)").bitcast(I32))
+        gather_words(2, 0)
         gather_words(2, 1)
+        w1_scales_rest = permute_columns("w1_scales_rest", w_scales_raw, U8, 2, 2)
 
         w2_codes = [held(f"w2_codes{a}", [P, H], U32) for a in range(PASSES)]
         w2_scales = [held(f"w2_scales{a}", [P, H], U8) for a in range(PASSES)]
-        w2_bf = [held(f"w2_bf{a}", [P, 4 * H], BF16) for a in range(PASSES)]
+        w2_bf = {}
 
         def round_w2(a):
-            nc.vector.tensor_copy(
+            w2_bf[a] = held(f"w2_bf{a}", [P, 4 * H], BF16)
+            (nc.scalar.copy if a < 2 else nc.vector.tensor_copy)(
                 w2_bf[a][:].rearrange("p (t q i j) -> p t q j i", t=TILES, q=16, j=4),
                 w2_raw[a][:].rearrange("p j (q t i) -> p t q j i", t=TILES, q=16),
             )
@@ -160,14 +186,14 @@ def tile_list_plankton_tendency_kernel(
                 lhsT=codes,
                 lhsT_scale=scales,
                 rhs=v_words[a, half][:, at : at + width].bitcast(FP8X4),
-                rhs_scale=(v_scales[:, a, :] if a < 2 else last_scales[:])[:, lo : lo + width],
+                rhs_scale=v_scales[:, a, lo : lo + width],
                 start=(a == 0),
                 stop=(a == PASSES - 1),
             )
 
         def a_pass(acc, a, half, t):
             mx_pass(acc[:], w1_codes[:, a, 2 * P * t : 2 * P * (t + 1)].bitcast(FP4X4),
-                    w1_scale_rows[:, a, P * t : P * (t + 1)], a, HALF * half, HALF)
+                    (w1_scales_first, w1_scales_rest)[t // 2][:, a, P * (t % 2) : P * (t % 2 + 1)], a, HALF * half, HALF)
 
         def b_pass(acc, a, half, t):
             mx_pass(acc[:], w2_codes[a][:, P * t : P * (t + 1)].bitcast(FP8X4),
@@ -177,7 +203,7 @@ def tile_list_plankton_tendency_kernel(
 
         def saturate_uptake(acc, half, t):
             mag = ring.tile([P, HALF], F32, name="mag")
-            root = ring.tile([P, HALF], F32, name="root")
+            root = held(f"root{half}_{t}", [P, HALF], F32)
             inv = ring.tile([P, HALF], F32, name="inv")
             nc.scalar.activation(mag[:], acc[:], ACT.Abs)
             nc.scalar.activation(root[:], mag[:], ACT.Abs_reciprocal_sqrt, bias=1.0)
@@ -199,51 +225,18 @@ def tile_list_plankton_tendency_kernel(
                 a_pass(acc, a, half, t)
             return acc
 
-        b_banks = [bank("second") for t in range(TILES)]
-        later = {}
-        for a in range(PASSES):
-            round_w2(a)
-            if a == 0:
-                w3_raw = staged(3, [P, PASSES, H], I32)
-                nc.sync.dma_start(w3_raw[:], w3_words.rearrange("a p e i -> p a (e i)").bitcast(I32))
-            if a == 1:
-                w4_raw = staged(4, [P, TILES, N], F32)
-                w4_rows = w4.rearrange("(q t i) n -> t q i n", t=TILES, i=8)
-                for t in range(TILES):
-                    nc.sync.dma_start(w4_raw[:, t, :], w4_rows[t])
-            saturate_uptake(a_banks[a], 0, a)
-            quantise_w2(a)
-            later[a] = uptake(1, a)
-            for t in range(TILES):
-                b_pass(b_banks[t], a, 0, t)
-        saturate_uptake(a_banks[3], 0, 3)
-        later[3] = uptake(1, 3)
-        w3_scale_rows = permute_columns("w3_scale_rows", w_scales_raw[:, 0:1, :], U8)
-        w3_codes = permute_columns("w3_codes", w3_raw, U32)
-
         growth = [held(f"growth{half}", [P, TILES, HALF], F32) for half in range(2)]
+        w4_codes = held("w4_codes", [P, N], U32)
+        w4_scales = held("w4_scales", [P, N], U8)
 
         def grow(acc, half, t):
             nc.vector.tensor_tensor(growth[half][:, t, :], acc[:], soft[half, t][:], ALU.mult)
 
-        b_later = {}
-        for t in range(TILES):
-            grow(b_banks[t], 0, t)
-            saturate_uptake(later[t], 1, t)
-            b_later[t] = bank("second")
+        def growth_rate(t):
+            acc = bank("second")
             for a in range(PASSES):
-                b_pass(b_later[t], a, 1, t)
-
-        w4_bf = held("w4_bf", [P, 4 * N], BF16)
-        w4_codes = held("w4_codes", [P, N], U32)
-        w4_scales = held("w4_scales", [P, N], U8)
-        nc.scalar.copy(
-            w4_bf[:].rearrange("p (c i t) -> p c t i", t=TILES, i=4),
-            w4_raw[:].rearrange("p t (c i) -> p c t i", i=4),
-        )
-        for lo, hi in ((0, 256), (256, N)):
-            nc.vector.quantize_mx(out=w4_codes[:, lo:hi].bitcast(FP8X4), scales=w4_scales[:, lo:hi],
-                                  in_=w4_bf[:, 4 * lo : 4 * hi])
+                b_pass(acc, a, 1, t)
+            return acc
 
         def mortality(j):
             acc = bank("first")
@@ -266,8 +259,8 @@ def tile_list_plankton_tendency_kernel(
             return h_bf
 
         def tendencies(h_bf, j):
-            h_codes = ring.tile([P, SLICE], U32, name="h_codes", align_bytes=64)
-            h_scales = ring.tile([P, SLICE], U8, name="h_scales", align_bytes=64)
+            h_codes = ring.tile([P, SLICE], U32, name="h_codes", align_bytes=64, bufs=4)
+            h_scales = ring.tile([P, SLICE], U8, name="h_scales", align_bytes=64, bufs=4)
             nc.vector.quantize_mx(out=h_codes[:].bitcast(FP8X4), scales=h_scales[:], in_=h_bf[:])
             acc = bank("second")
             result = ring.tile([P, NT, SLICE], F32, name="result", bufs=4)
@@ -288,10 +281,57 @@ def tile_list_plankton_tendency_kernel(
                 out[:, SLICE * j : SLICE * (j + 1)].rearrange("(m p) s -> p m s", p=P), result[:]
             )
 
+        b_banks = [bank("second") for t in range(TILES)]
+        later = {}
+        for a in range(PASSES):
+            round_w2(a)
+            if a == 1:
+                w4_raw = held("w4_raw", [P, TILES, N], F32)
+                w4_rows = w4.rearrange("(q t i) n -> t q i n", t=TILES, i=8)
+                for t in range(TILES):
+                    nc.sync.dma_start(w4_raw[:, t, :], w4_rows[t])
+            saturate_uptake(a_banks[a], 0, a)
+            quantise_w2(a)
+            if a < 2:
+                later[a] = uptake(1, a)
+            for t in range(TILES):
+                b_pass(b_banks[t], a, 0, t)
+        w3_scale_rows = permute_columns("w3_scale_rows", w3_scales_raw, U8)
+        w3_codes = permute_columns("w3_codes", w3_raw, U32)
+        loss = {0: mortality(0)}
+        saturate_uptake(a_banks[3], 0, 3)
+        later[2] = uptake(1, 2)
+
+        b_later = {}
+        grow(b_banks[0], 0, 0)
+        b_later[0] = growth_rate(0)
+        saturate_uptake(later[0], 1, 0)
+        loss[1] = mortality(1)
+        grow(b_banks[1], 0, 1)
+        b_later[1] = growth_rate(1)
+        grow(b_banks[2], 0, 2)
+        b_later[2] = growth_rate(2)
+        saturate_uptake(later[1], 1, 1)
+        later[3] = uptake(1, 3)
+        grow(b_banks[3], 0, 3)
+        b_later[3] = growth_rate(3)
+
+        w4_bf = held("w4_bf", [P, 4 * N], BF16)
+        nc.scalar.copy(
+            w4_bf[:].rearrange("p (c i t) -> p c t i", t=TILES, i=4),
+            w4_raw[:].rearrange("p t (c i) -> p c t i", i=4),
+        )
+        for lo, hi in ((0, 256), (256, N)):
+            nc.vector.quantize_mx(out=w4_codes[:, lo:hi].bitcast(FP8X4), scales=w4_scales[:, lo:hi],
+                                  in_=w4_bf[:, 4 * lo : 4 * hi])
+
         pending = None
         for j in range(S // SLICE):
-            acc = mortality(j)
-            h_bf = net_growth(acc, j)
+            if j not in loss:
+                loss[j] = mortality(j)
+            h_bf = net_growth(loss[j], j)
+            if j < 2:
+                saturate_uptake(later[j + 2], 1, j + 2)
             if j < TILES:
                 grow(b_later[j], 1, j)
             if pending is not None:

@@ -34,26 +34,27 @@ AT = {
     "v_words0_1": 13824,
     "w2_raw1": 15872,
     "w4_raw": 15872,
+    "mag0_0": 22016,
     "gathered_scales": 24064,
     "drift_cols": 24064,
-    "w2_raw2": 24128,
-    "v_words1_0": 32320,
-    "tab0": 33344,
-    "v_words1_1": 34368,
-    "w2_codes0": 36416,
-    "v_words2_0": 38464,
-    "v_words2_1": 40512,
-    "w2_raw0": 42560,
-    "warm": 50720,
-    "tab1": 50752,
-    "w3_raw": 50752,
-    "tab2": 58944,
-    "warm_out": 58944,
-    "w3_scale_rows": 58944,
-    "w1_scales_rest": 59456,
-    "w2_bf1": 60224,
-    "root1_1": 67136,
-    "w4_bf": 67136,
+    "w2_raw2": 25088,
+    "tab0": 33152,
+    "v_words1_0": 33280,
+    "v_words1_1": 35328,
+    "v_words2_0": 37376,
+    "v_words2_1": 39424,
+    "w2_raw0": 41472,
+    "warm": 49632,
+    "tab1": 49664,
+    "w2_codes0": 49664,
+    "tab2": 57856,
+    "warm_out": 57856,
+    "w3_scale_rows": 57856,
+    "w1_scales_rest": 58368,
+    "w2_bf1": 59136,
+    "w3_raw": 63232,
+    "root1_1": 69376,
+    "w4_bf": 69376,
 }
 
 
@@ -132,7 +133,6 @@ def tile_list_plankton_tendency_kernel(
                 v_scales[32 * d : 32 * d + 4, :, :].bitcast(I32),
                 gathered_scales[32 * d + 4 : 32 * d + 28 : 2, :].bitcast(I32),
             )
-        load_w2(2)
         drift_cols = held("drift_cols", [P, NT], F32)
         with nc.allow_non_contiguous_dma(reason="one drift value for each partition and tile of out"):
             nc.gpsimd.dma_start(drift_cols[:], drift.rearrange("(m p) -> p m", p=P))
@@ -157,12 +157,13 @@ def tile_list_plankton_tendency_kernel(
         gather_words(0, 0)
         w1_scales_first = permute_columns("w1_scales_first", w_scales_raw, U8, 0, 2)
         gather_words(0, 1)
+        load_w2(2)
         gather_words(1, 0)
         gather_words(1, 1)
-        w3_raw = held("w3_raw", [P, PASSES, H], I32)
-        nc.sync.dma_start(w3_raw[:], w3_words.rearrange("a p e i -> p a (e i)").bitcast(I32))
         gather_words(2, 0)
         gather_words(2, 1)
+        w3_raw = held("w3_raw", [P, PASSES, H], I32)
+        nc.sync.dma_start(w3_raw[:], w3_words.rearrange("a p e i -> p a (e i)").bitcast(I32))
         w1_scales_rest = permute_columns("w1_scales_rest", w_scales_raw, U8, 2, 2)
 
         w2_codes = [held(f"w2_codes{a}", [P, H], U32) for a in range(PASSES)]
@@ -171,13 +172,17 @@ def tile_list_plankton_tendency_kernel(
 
         def round_w2(a):
             w2_bf[a] = held(f"w2_bf{a}", [P, 4 * H], BF16)
-            (nc.scalar.copy if a < 2 else nc.vector.tensor_copy)(
-                w2_bf[a][:].rearrange("p (t q i j) -> p t q j i", t=TILES, q=16, j=4),
-                w2_raw[a][:].rearrange("p j (q t i) -> p t q j i", t=TILES, q=16),
-            )
+            dst = w2_bf[a][:].rearrange("p (t q i j) -> p t q j i", t=TILES, q=16, j=4)
+            src = w2_raw[a][:].rearrange("p j (q t i) -> p t q j i", t=TILES, q=16)
+            for pair in range(2):
+                copy = nc.scalar.copy if 2 * a + pair < 3 else nc.vector.tensor_copy
+                copy(dst[:, 2 * pair : 2 * pair + 2], src[:, 2 * pair : 2 * pair + 2])
 
         def quantise_w2(a):
-            nc.vector.quantize_mx(out=w2_codes[a][:].bitcast(FP8X4), scales=w2_scales[a][:], in_=w2_bf[a][:])
+            for lo in (0, H // 2):
+                hi = lo + H // 2
+                nc.vector.quantize_mx(out=w2_codes[a][:, lo:hi].bitcast(FP8X4), scales=w2_scales[a][:, lo:hi],
+                                      in_=w2_bf[a][:, 4 * lo : 4 * hi])
 
         def mx_pass(acc, codes, scales, a, lo, width):
             half, at = divmod(lo, HALF)
@@ -202,7 +207,7 @@ def tile_list_plankton_tendency_kernel(
         soft = {}
 
         def saturate_uptake(acc, half, t):
-            mag = ring.tile([P, HALF], F32, name="mag")
+            mag = held(f"mag{half}_{t}", [P, HALF], F32)
             root = held(f"root{half}_{t}", [P, HALF], F32)
             inv = ring.tile([P, HALF], F32, name="inv")
             nc.scalar.activation(mag[:], acc[:], ACT.Abs)

@@ -17,44 +17,61 @@ ACT = mybir.ActivationFunctionType
 ALU = mybir.AluOpType
 
 P = 128
-PASSES = K // 512
+PACK = 4
+PASSES = K // (P * PACK)
+QUADS = 4
+BLOCKS = 16
 HALF = 512
 SLICE = 128
-TILES = 4
-NT = N // P
-AT = {
-    "w3_codes": 0,
-    "w2_bf0": 2048,
-    "w2_bf2": 2048,
-    "scale_window": 6016,
-    "w1_codes": 7936,
-    "v_words0_0": 11008,
-    "w1_raw": 12928,
-    "w1_scales_first": 13056,
-    "v_words0_1": 13824,
-    "w2_raw1": 15872,
-    "w4_raw": 15872,
-    "mag0_0": 22016,
-    "gathered_scales": 24064,
-    "drift_cols": 24064,
-    "w2_raw2": 25088,
-    "tab0": 33152,
-    "v_words1_0": 33280,
-    "v_words1_1": 35328,
-    "v_words2_0": 37376,
-    "v_words2_1": 39424,
-    "w2_raw0": 41472,
-    "warm": 49632,
-    "tab1": 49664,
-    "w2_codes0": 49664,
-    "tab2": 57856,
-    "warm_out": 57856,
-    "w3_scale_rows": 57856,
-    "w1_scales_rest": 58368,
-    "w2_bf1": 59136,
-    "w3_raw": 63232,
-    "root1_1": 69376,
-    "w4_bf": 69376,
+TILES = H // P
+OUT_TILES = N // P
+
+REACH = 128
+WORDS = 4 * HALF
+STAGE = 4 * T
+W1_BYTES = PASSES * 2 * H
+PAIR_SCALES = PASSES * 2 * P
+SCALE_WINDOW = 0
+W1_CODES = SCALE_WINDOW + T - REACH
+W1_RAW = W1_CODES + W1_BYTES + WORDS - REACH
+W2_RAW = W1_RAW + W1_BYTES - REACH
+DRIFT = W2_RAW + 2 * STAGE
+TAB = DRIFT + 64 + STAGE
+LAST_TAB = TAB + 2 * STAGE
+W2_BF = LAST_TAB + 2 * WORDS + H + PAIR_SCALES + 8 * H
+W4_BF = W2_BF + 4 * PASSES * H
+OFFSET = {
+    "scale_window": SCALE_WINDOW,
+    "w1_codes": W1_CODES,
+    "w1_raw": W1_RAW,
+    "v_words0_0": W1_RAW + REACH - WORDS,
+    "w1_scales_first": W1_RAW + REACH,
+    "v_words0_1": W1_RAW + REACH + PAIR_SCALES,
+    "w2_raw0": W2_RAW,
+    "warm_out": W1_RAW + REACH,
+    "w3_raw": W2_RAW,
+    "gathered_scales": DRIFT - S // 2,
+    "w2_raw1": W2_RAW + STAGE,
+    "drift_cols": DRIFT,
+    "w2_raw2": DRIFT + 64,
+    "w4_raw": W2_RAW + STAGE,
+    "tab0": TAB,
+    "v_words2_0": TAB,
+    "v_words2_1": TAB + WORDS,
+    "v_words1_0": TAB + 2 * WORDS,
+    "warm_in": LAST_TAB - 32,
+    "tab1": TAB + STAGE,
+    "tab2": LAST_TAB,
+    "v_words1_1": LAST_TAB,
+    "w2_codes0": LAST_TAB + WORDS,
+    "w3_scale_rows": LAST_TAB + 2 * WORDS,
+    "w1_scales_rest": LAST_TAB + 2 * WORDS + H,
+    "w2_bf1": LAST_TAB + 2 * WORDS + H + PAIR_SCALES,
+    "w2_bf0": W2_BF,
+    "w2_bf2": W2_BF,
+    "w3_codes": W2_BF,
+    "root1_1": W4_BF,
+    "w4_bf": W4_BF,
 }
 
 
@@ -68,23 +85,26 @@ def tile_list_plankton_tendency_kernel(
         ring = ctx.enter_context(tc.tile_pool(name="ring", bufs=2))
         psum = ctx.enter_context(tc.psum_pool(name="psum", bufs=4))
 
-        def held(name, shape, dtype):
-            if name in AT:
-                return shared.tile(shape, dtype, name=name, align_bytes=32 if name == "warm" else 64, offset=AT[name])
-            return keep.tile(shape, dtype, name=name, align_bytes=64)
+        def held(name, shape, dtype, align=64):
+            if name in OFFSET:
+                return shared.tile(shape, dtype, name=name, align_bytes=align, offset=OFFSET[name])
+            return keep.tile(shape, dtype, name=name, align_bytes=align)
+
+        def bank(tag):
+            return psum.tile([P, HALF], F32, name=tag, tag=tag)
 
         offsets = keep.tile([P, S // 16], U16, name="offsets")
         nc.sync.dma_start(offsets[:], offs)
 
         scale_window = held("scale_window", [P, T], U8)
-        w_scales_raw = held("w_scales_raw", [P, PASSES, H], U8)
+        w1_scales_raw = held("w1_scales_raw", [P, PASSES, H], U8)
         v_scales = held("v_scales", [P, PASSES, S], U8)
-        warm = held("warm", [P, 16], F32)
+        warm_in = held("warm_in", [P, 16], F32, align=32)
         warm_out = held("warm_out", [P, 16], F32)
         nc.vector.memset(scale_window[:].bitcast(I32), 0)
-        nc.gpsimd.memset(w_scales_raw[:].bitcast(I32), 0)
-        nc.vector.memset(warm[:], 1.0)
-        nc.scalar.activation(warm_out[:], warm[:], ACT.Abs_reciprocal_sqrt)
+        nc.gpsimd.memset(w1_scales_raw[:].bitcast(I32), 0)
+        nc.vector.memset(warm_in[:], 1.0)
+        nc.scalar.activation(warm_out[:], warm_in[:], ACT.Abs_reciprocal_sqrt)
         nc.vector.memset(v_scales[:].bitcast(I32), 0)
         w3_scales_raw = held("w3_scales_raw", [P, 1, H], U8)
         nc.vector.memset(w3_scales_raw[:].bitcast(I32), 0)
@@ -95,45 +115,45 @@ def tile_list_plankton_tendency_kernel(
             tab[a] = held(f"tab{a}", [P, T], I32)
             nc.sync.dma_start(tab[a][:], tab_words[a].rearrange("p t i -> p (t i)").bitcast(I32))
 
+        def scale_rows(tile, d):
+            return tile[32 * d + 4 : 32 * d + 28 : 2, :].bitcast(I32)
+
+        def quadrant_rows(scales, d):
+            return scales.bitcast(I32)[:, 4 * d : 4 * d + 4, :]
+
         load_tab(0)
-        tab_scale_words = tab_scales.bitcast(I32)
-        for d in range(4):
+        for d in range(QUADS):
             (nc.scalar, nc.sync)[d % 2].dma_start(
-                scale_window[32 * d + 4 : 32 * d + 28 : 2, :].bitcast(I32),
-                tab_scale_words[:, 4 * d : 4 * d + 4, :].rearrange("a r n -> r a n"),
+                scale_rows(scale_window, d), quadrant_rows(tab_scales, d).rearrange("a s n -> s a n")
             )
         w1_raw = held("w1_raw", [P, PASSES, 2 * H], U8)
         nc.sync.dma_start(w1_raw[:].bitcast(I32), w1_words.bitcast(I32).rearrange("a p n -> p a n"))
-        w2_raw = {}
-
-        def load_w2(a):
-            w2_raw[a] = held(f"w2_raw{a}", [P, 4, H], F32)
-            nc.sync.dma_start(w2_raw[a][:], w2[512 * a : 512 * (a + 1), :].rearrange("(p j) c -> p j c", j=4))
-
-        load_w2(0)
         load_tab(1)
         load_tab(2)
 
-        for d in range(4):
+        for d in range(QUADS):
             nc.gpsimd.dma_start(
-                w_scales_raw[32 * d : 32 * d + 4, :, :].bitcast(I32),
-                w1_scales.bitcast(I32)[:, 4 * d : 4 * d + 4, :].rearrange("a r n -> r a n"),
+                w1_scales_raw[32 * d : 32 * d + 4, :, :].bitcast(I32),
+                quadrant_rows(w1_scales, d).rearrange("a s n -> s a n"),
             )
-        for d in range(4):
+        for d in range(QUADS):
             nc.gpsimd.dma_start(
-                w3_scales_raw[32 * d + 4 : 32 * d + 16, 0, :].bitcast(I32),
-                w3_scales.bitcast(I32)[:, 4 * d : 4 * d + 4, :],
+                w3_scales_raw[32 * d + 4 : 32 * d + 16, 0, :].bitcast(I32), quadrant_rows(w3_scales, d)
             )
 
         gathered_scales = held("gathered_scales", [P, S], U8)
         nc.vector.tensor_copy(gathered_scales[:], scale_window[:].indirect(offsets[:]))
-
-        for d in range(4):
-            nc.scalar.dma_start(
-                v_scales[32 * d : 32 * d + 4, :, :].bitcast(I32),
-                gathered_scales[32 * d + 4 : 32 * d + 28 : 2, :].bitcast(I32),
+        for d in range(QUADS):
+            (nc.scalar, nc.sync)[d % 2].dma_start(
+                v_scales[32 * d : 32 * d + 4, :, :].bitcast(I32), scale_rows(gathered_scales, d)
             )
-        drift_cols = held("drift_cols", [P, NT], F32)
+
+        w2_raw = {}
+        for a in range(PASSES):
+            w2_raw[a] = held(f"w2_raw{a}", [P, PACK, H], F32)
+            rows = w2[P * PACK * a : P * PACK * (a + 1), :]
+            nc.sync.dma_start(w2_raw[a][:], rows.rearrange("(p j) c -> p j c", j=PACK))
+        drift_cols = held("drift_cols", [P, OUT_TILES], F32)
         with nc.allow_non_contiguous_dma(reason="one drift value for each partition and tile of out"):
             nc.gpsimd.dma_start(drift_cols[:], drift.rearrange("(m p) -> p m", p=P))
 
@@ -141,50 +161,44 @@ def tile_list_plankton_tendency_kernel(
 
         def gather_words(a, half):
             v_words[a, half] = held(f"v_words{a}_{half}", [P, HALF], U32)
-            cols = offsets[:, half * (HALF // 16) : (half + 1) * (HALF // 16)]
-            nc.vector.tensor_copy(v_words[a, half][:], tab[a][:].bitcast(U32).indirect(cols))
+            entries = offsets[:, half * (HALF // 16) : (half + 1) * (HALF // 16)]
+            nc.vector.tensor_copy(v_words[a, half][:], tab[a][:].bitcast(U32).indirect(entries))
 
-        def permute_columns(name, raw, dtype, first=0, count=TILES):
+        def order_columns(name, raw, dtype, first=0, count=TILES):
             done = held(name, [P, raw.shape[1], raw.shape[2] * count // TILES], dtype)
+            source = raw[:].bitcast(I32).rearrange("p a (q t w) -> p a t q w", t=TILES, q=BLOCKS)
             nc.vector.tensor_copy(
-                done[:].bitcast(I32).rearrange("p a (t q w) -> p a t q w", t=count, q=16),
-                raw[:].bitcast(I32).rearrange("p a (q t w) -> p a t q w", t=TILES, q=16)[:, :, first : first + count],
+                done[:].bitcast(I32).rearrange("p a (t q w) -> p a t q w", t=count, q=BLOCKS),
+                source[:, :, first : first + count],
             )
             return done
 
-        w1_codes = permute_columns("w1_codes", w1_raw, U8)
-        load_w2(1)
+        w1_codes = order_columns("w1_codes", w1_raw, U8)
         gather_words(0, 0)
-        w1_scales_first = permute_columns("w1_scales_first", w_scales_raw, U8, 0, 2)
+        w1_scales_first = order_columns("w1_scales_first", w1_scales_raw, U8, 0, 2)
         gather_words(0, 1)
-        load_w2(2)
         gather_words(1, 0)
-        gather_words(1, 1)
         gather_words(2, 0)
         gather_words(2, 1)
-        w3_raw = held("w3_raw", [P, PASSES, H], I32)
-        nc.sync.dma_start(w3_raw[:], w3_words.rearrange("a p e i -> p a (e i)").bitcast(I32))
-        w1_scales_rest = permute_columns("w1_scales_rest", w_scales_raw, U8, 2, 2)
+        w1_scales_rest = order_columns("w1_scales_rest", w1_scales_raw, U8, 2, 2)
+        gather_words(1, 1)
 
         w2_codes = [held(f"w2_codes{a}", [P, H], U32) for a in range(PASSES)]
         w2_scales = [held(f"w2_scales{a}", [P, H], U8) for a in range(PASSES)]
         w2_bf = {}
 
         def round_w2(a):
-            w2_bf[a] = held(f"w2_bf{a}", [P, 4 * H], BF16)
-            dst = w2_bf[a][:].rearrange("p (t q i j) -> p t q j i", t=TILES, q=16, j=4)
-            src = w2_raw[a][:].rearrange("p j (q t i) -> p t q j i", t=TILES, q=16)
+            w2_bf[a] = held(f"w2_bf{a}", [P, PACK * H], BF16)
+            rounded = w2_bf[a][:].rearrange("p (t q i j) -> p t q j i", t=TILES, q=BLOCKS, j=PACK)
+            source = w2_raw[a][:].rearrange("p j (q t i) -> p t q j i", t=TILES, q=BLOCKS)
             for pair in range(2):
-                copy = nc.scalar.copy if 2 * a + pair < 3 else nc.vector.tensor_copy
-                copy(dst[:, 2 * pair : 2 * pair + 2], src[:, 2 * pair : 2 * pair + 2])
+                copy = nc.scalar.copy if 2 * a + pair < PASSES else nc.vector.tensor_copy
+                copy(rounded[:, 2 * pair : 2 * pair + 2], source[:, 2 * pair : 2 * pair + 2])
 
-        def quantise_w2(a):
-            for lo in (0, H // 2):
-                hi = lo + H // 2
-                nc.vector.quantize_mx(out=w2_codes[a][:, lo:hi].bitcast(FP8X4), scales=w2_scales[a][:, lo:hi],
-                                      in_=w2_bf[a][:, 4 * lo : 4 * hi])
+        def quantise(codes, scales, values):
+            nc.vector.quantize_mx(out=codes.bitcast(FP8X4), scales=scales, in_=values)
 
-        def mx_pass(acc, codes, scales, a, lo, width):
+        def table_pass(acc, codes, scales, a, lo, width):
             half, at = divmod(lo, HALF)
             nc.tensor.matmul_mx(
                 out=acc,
@@ -196,80 +210,71 @@ def tile_list_plankton_tendency_kernel(
                 stop=(a == PASSES - 1),
             )
 
-        def a_pass(acc, a, half, t):
-            mx_pass(acc[:], w1_codes[:, a, 2 * P * t : 2 * P * (t + 1)].bitcast(FP4X4),
-                    (w1_scales_first, w1_scales_rest)[t // 2][:, a, P * (t % 2) : P * (t % 2 + 1)], a, HALF * half, HALF)
-
-        def b_pass(acc, a, half, t):
-            mx_pass(acc[:], w2_codes[a][:, P * t : P * (t + 1)].bitcast(FP8X4),
-                    w2_scales[a][:, P * t : P * (t + 1)], a, HALF * half, HALF)
-
-        soft = {}
-
-        def saturate_uptake(acc, half, t):
-            mag = held(f"mag{half}_{t}", [P, HALF], F32)
-            root = held(f"root{half}_{t}", [P, HALF], F32)
-            inv = ring.tile([P, HALF], F32, name="inv")
-            nc.scalar.activation(mag[:], acc[:], ACT.Abs)
-            nc.scalar.activation(root[:], mag[:], ACT.Abs_reciprocal_sqrt, bias=1.0)
-            nc.scalar.activation(inv[:], root[:], ACT.Square)
-            soft[half, t] = held(f"soft{half}_{t}", [P, HALF], F32)
-            nc.vector.tensor_tensor(soft[half, t][:], acc[:], inv[:], ALU.mult)
-
-        def bank(tag):
-            return psum.tile([P, HALF], F32, name=tag, tag=tag)
-
-        a_banks = [bank("first") for t in range(TILES)]
-        for t in range(TILES):
-            for a in range(PASSES):
-                a_pass(a_banks[t], a, 0, t)
-
         def uptake(half, t):
             acc = bank("first")
+            pair_scales = (w1_scales_first, w1_scales_rest)[t // 2]
             for a in range(PASSES):
-                a_pass(acc, a, half, t)
+                table_pass(acc[:], w1_codes[:, a, 2 * P * t : 2 * P * (t + 1)].bitcast(FP4X4),
+                           pair_scales[:, a, P * (t % 2) : P * (t % 2 + 1)], a, HALF * half, HALF)
             return acc
 
-        growth = [held(f"growth{half}", [P, TILES, HALF], F32) for half in range(2)]
-        w4_codes = held("w4_codes", [P, N], U32)
-        w4_scales = held("w4_scales", [P, N], U8)
+        def growth_pass(acc, a, half, t):
+            table_pass(acc[:], w2_codes[a][:, P * t : P * (t + 1)].bitcast(FP8X4),
+                       w2_scales[a][:, P * t : P * (t + 1)], a, HALF * half, HALF)
 
-        def grow(acc, half, t):
-            nc.vector.tensor_tensor(growth[half][:, t, :], acc[:], soft[half, t][:], ALU.mult)
-
-        def growth_rate(t):
+        def late_growth(t):
             acc = bank("second")
             for a in range(PASSES):
-                b_pass(acc, a, 1, t)
+                growth_pass(acc, a, 1, t)
             return acc
 
         def mortality(j):
             acc = bank("first")
             for t in range(TILES):
                 for a in range(PASSES):
-                    mx_pass(acc[:, SLICE * t : SLICE * (t + 1)],
-                            w3_codes[:, a, P * t : P * (t + 1)].bitcast(FP8X4),
-                            w3_scale_rows[4 * (a + 1) : P, 0, P * t : P * (t + 1)], a, SLICE * j, SLICE)
+                    table_pass(acc[:, SLICE * t : SLICE * (t + 1)],
+                               w3_codes[:, a, P * t : P * (t + 1)].bitcast(FP8X4),
+                               w3_scale_rows[4 * (a + 1) : P, 0, P * t : P * (t + 1)], a, SLICE * j, SLICE)
             return acc
+
+        saturated = {}
+
+        def saturate(acc, half, t):
+            magnitude = ring.tile([P, HALF], F32, name="magnitude")
+            root = held(f"root{half}_{t}", [P, HALF], F32)
+            inverse = ring.tile([P, HALF], F32, name="inverse", bufs=4)
+            nc.scalar.activation(magnitude[:], acc[:], ACT.Abs)
+            nc.scalar.activation(root[:], magnitude[:], ACT.Abs_reciprocal_sqrt, bias=1.0)
+            nc.scalar.activation(inverse[:], root[:], ACT.Square)
+            saturated[half, t] = held(f"saturated{half}_{t}", [P, HALF], F32)
+            nc.vector.tensor_tensor(saturated[half, t][:], acc[:], inverse[:], ALU.mult)
+
+        gain = [held(f"gain{half}", [P, TILES, HALF], F32) for half in range(2)]
+
+        def multiply_growth(acc, half, t):
+            nc.vector.tensor_tensor(gain[half][:, t, :], acc[:], saturated[half, t][:], ALU.mult)
 
         def net_growth(acc, j):
             half, at = divmod(SLICE * j, HALF)
-            h_bf = ring.tile([P, 4 * SLICE], BF16, name="h_bf", align_bytes=64)
+            h_bf = ring.tile([P, TILES * SLICE], BF16, name="h_bf", align_bytes=64)
             nc.vector.tensor_tensor(
                 h_bf[:].rearrange("p (c i t) -> p c t i", t=TILES, i=4),
-                growth[half][:, :, at : at + SLICE].rearrange("p t (c i) -> p c t i", i=4),
+                gain[half][:, :, at : at + SLICE].rearrange("p t (c i) -> p c t i", i=4),
                 acc[:].rearrange("p (t c i) -> p c t i", t=TILES, i=4),
                 ALU.subtract,
             )
             return h_bf
 
+        w4_codes = held("w4_codes", [P, N], U32)
+        w4_scales = held("w4_scales", [P, N], U8)
+
         def tendencies(h_bf, j):
             h_codes = ring.tile([P, SLICE], U32, name="h_codes", align_bytes=64, bufs=4)
             h_scales = ring.tile([P, SLICE], U8, name="h_scales", align_bytes=64, bufs=4)
-            nc.vector.quantize_mx(out=h_codes[:].bitcast(FP8X4), scales=h_scales[:], in_=h_bf[:])
+            quantise(h_codes[:], h_scales[:], h_bf[:])
             acc = bank("second")
-            result = ring.tile([P, NT, SLICE], F32, name="result", bufs=4)
-            for m in range(NT):
+            result = ring.tile([P, OUT_TILES, SLICE], F32, name="result", bufs=4)
+            for m in range(OUT_TILES):
                 nc.tensor.matmul_mx(
                     out=acc[:, SLICE * m : SLICE * (m + 1)],
                     lhsT=w4_codes[:, P * m : P * (m + 1)].bitcast(FP8X4),
@@ -279,66 +284,66 @@ def tile_list_plankton_tendency_kernel(
                     start=True,
                     stop=True,
                 )
-            for m in range(NT):
+            for m in range(OUT_TILES):
                 nc.scalar.activation(result[:, m, :], acc[:, SLICE * m : SLICE * (m + 1)], ACT.Identity,
                                      bias=drift_cols[:, m : m + 1])
-            nc.sync.dma_start(
-                out[:, SLICE * j : SLICE * (j + 1)].rearrange("(m p) s -> p m s", p=P), result[:]
-            )
+            nc.sync.dma_start(out[:, SLICE * j : SLICE * (j + 1)].rearrange("(m p) s -> p m s", p=P), result[:])
 
-        b_banks = [bank("second") for t in range(TILES)]
-        later = {}
+        early_a = [uptake(0, t) for t in range(TILES)]
+        early_b = [bank("second") for t in range(TILES)]
+        late_a, late_b, loss = {}, {}, {}
         for a in range(PASSES):
             round_w2(a)
+            if a == 0:
+                w3_raw = held("w3_raw", [P, PASSES, H], I32)
+                nc.sync.dma_start(w3_raw[:], w3_words.rearrange("a p e i -> p a (e i)").bitcast(I32))
             if a == 1:
                 w4_raw = held("w4_raw", [P, TILES, N], F32)
                 w4_rows = w4.rearrange("(q t i) n -> t q i n", t=TILES, i=8)
                 for t in range(TILES):
                     nc.sync.dma_start(w4_raw[:, t, :], w4_rows[t])
-            saturate_uptake(a_banks[a], 0, a)
-            quantise_w2(a)
-            if a < 2:
-                later[a] = uptake(1, a)
+            saturate(early_a[a], 0, a)
+            quantise(w2_codes[a][:], w2_scales[a][:], w2_bf[a][:])
+            if a < PASSES - 1:
+                late_a[a] = uptake(1, a)
             for t in range(TILES):
-                b_pass(b_banks[t], a, 0, t)
-        w3_scale_rows = permute_columns("w3_scale_rows", w3_scales_raw, U8)
-        w3_codes = permute_columns("w3_codes", w3_raw, U32)
-        loss = {0: mortality(0)}
-        saturate_uptake(a_banks[3], 0, 3)
-        later[2] = uptake(1, 2)
+                growth_pass(early_b[t], a, 0, t)
+        w3_scale_rows = order_columns("w3_scale_rows", w3_scales_raw, U8)
+        w3_codes = order_columns("w3_codes", w3_raw, U32)
+        loss[0] = mortality(0)
+        saturate(early_a[3], 0, 3)
+        late_a[2] = uptake(1, 2)
 
-        b_later = {}
-        grow(b_banks[0], 0, 0)
-        b_later[0] = growth_rate(0)
-        saturate_uptake(later[0], 1, 0)
+        def hand_over_growth(t):
+            multiply_growth(early_b[t], 0, t)
+            late_b[t] = late_growth(t)
+
+        hand_over_growth(0)
+        saturate(late_a[0], 1, 0)
         loss[1] = mortality(1)
-        grow(b_banks[1], 0, 1)
-        b_later[1] = growth_rate(1)
-        grow(b_banks[2], 0, 2)
-        b_later[2] = growth_rate(2)
-        saturate_uptake(later[1], 1, 1)
-        later[3] = uptake(1, 3)
-        grow(b_banks[3], 0, 3)
-        b_later[3] = growth_rate(3)
+        hand_over_growth(1)
+        hand_over_growth(2)
+        saturate(late_a[1], 1, 1)
+        late_a[3] = uptake(1, 3)
+        hand_over_growth(3)
 
-        w4_bf = held("w4_bf", [P, 4 * N], BF16)
+        w4_bf = held("w4_bf", [P, TILES * N], BF16)
         nc.scalar.copy(
             w4_bf[:].rearrange("p (c i t) -> p c t i", t=TILES, i=4),
             w4_raw[:].rearrange("p t (c i) -> p c t i", i=4),
         )
-        for lo, hi in ((0, 256), (256, N)):
-            nc.vector.quantize_mx(out=w4_codes[:, lo:hi].bitcast(FP8X4), scales=w4_scales[:, lo:hi],
-                                  in_=w4_bf[:, 4 * lo : 4 * hi])
+        for lo, hi in ((0, 2 * P), (2 * P, N)):
+            quantise(w4_codes[:, lo:hi], w4_scales[:, lo:hi], w4_bf[:, TILES * lo : TILES * hi])
 
         pending = None
         for j in range(S // SLICE):
             if j not in loss:
                 loss[j] = mortality(j)
             h_bf = net_growth(loss[j], j)
-            if j < 2:
-                saturate_uptake(later[j + 2], 1, j + 2)
+            if j + 2 < TILES:
+                saturate(late_a[j + 2], 1, j + 2)
             if j < TILES:
-                grow(b_later[j], 1, j)
+                multiply_growth(late_b[j], 1, j)
             if pending is not None:
                 tendencies(*pending)
             pending = (h_bf, j)

@@ -22,56 +22,41 @@ PASSES = K // (P * PACK)
 QUADS = 4
 BLOCKS = 16
 HALF = 512
+QUARTER = 256
 SLICE = 128
 TILES = H // P
 OUT_TILES = N // P
+STAGE = 4 * T
 
 REACH = 128
 WORDS = 4 * HALF
-STAGE = 4 * T
-W1_BYTES = PASSES * 2 * H
-PAIR_SCALES = PASSES * 2 * P
-SCALE_WINDOW = 0
-W1_CODES = SCALE_WINDOW + T - REACH
-W1_RAW = W1_CODES + W1_BYTES + WORDS - REACH
-W2_RAW = W1_RAW + W1_BYTES - REACH
-DRIFT = W2_RAW + 2 * STAGE
-TAB = DRIFT + 64 + STAGE
-LAST_TAB = TAB + 2 * STAGE
-W2_BF = LAST_TAB + 2 * WORDS + H + PAIR_SCALES + 8 * H
-W4_BF = W2_BF + 4 * PASSES * H
+W1_SCALES = PASSES * H
+W1_CODES = 0
+WINDOW = W1_CODES + 2 * W1_SCALES - REACH
+V_FIRST = WINDOW + REACH
+W2_FIRST = V_FIRST + 2 * WORDS
+TAB0 = W2_FIRST + STAGE - REACH
+TAB2 = TAB0 + STAGE
+TAB1 = TAB2 + STAGE + H
+W2_SECOND = TAB1 + STAGE + REACH
 OFFSET = {
-    "scale_window": SCALE_WINDOW,
     "w1_codes": W1_CODES,
-    "w1_raw": W1_RAW,
-    "v_words0_0": W1_RAW + REACH - WORDS,
-    "w1_scales_first": W1_RAW + REACH,
-    "v_words0_1": W1_RAW + REACH + PAIR_SCALES,
-    "w2_raw0": W2_RAW,
-    "warm_out": W1_RAW + REACH,
-    "w3_raw": W2_RAW,
-    "gathered_scales": DRIFT - S // 2,
-    "w2_raw1": W2_RAW + STAGE,
-    "drift_cols": DRIFT,
-    "w2_raw2": DRIFT + 64,
-    "w4_raw": W2_RAW + STAGE,
-    "tab0": TAB,
-    "v_words2_0": TAB,
-    "v_words2_1": TAB + WORDS,
-    "v_words1_0": TAB + 2 * WORDS,
-    "warm_in": LAST_TAB - 32,
-    "tab1": TAB + STAGE,
-    "tab2": LAST_TAB,
-    "v_words1_1": LAST_TAB,
-    "w2_codes0": LAST_TAB + WORDS,
-    "w3_scale_rows": LAST_TAB + 2 * WORDS,
-    "w1_scales_rest": LAST_TAB + 2 * WORDS + H,
-    "w2_bf1": LAST_TAB + 2 * WORDS + H + PAIR_SCALES,
-    "w2_bf0": W2_BF,
-    "w2_bf2": W2_BF,
-    "w3_codes": W2_BF,
-    "root1_1": W4_BF,
-    "w4_bf": W4_BF,
+    "scale_window": WINDOW,
+    "v_words0": V_FIRST,
+    "w2_raw0": W2_FIRST,
+    "w4_raw": W2_FIRST,
+    "tab0": TAB0,
+    "drift_cols": TAB0 + REACH,
+    "w1_scale_rows": TAB0 + 2 * REACH,
+    "v_words1": TAB0 + 2 * REACH + W1_SCALES,
+    "w1_raw": TAB2,
+    "tab2": TAB2,
+    "w3_raw": TAB2,
+    "tab1": TAB1,
+    "w3_scale_rows": TAB1 - H + REACH,
+    "w2_raw2": TAB1 + REACH,
+    "gathered_scales": W2_SECOND,
+    "w2_raw1": W2_SECOND,
 }
 
 
@@ -83,31 +68,34 @@ def tile_list_plankton_tendency_kernel(
         keep = ctx.enter_context(tc.tile_pool(name="keep", bufs=1))
         shared = ctx.enter_context(tc.tile_pool(name="shared", bufs=1))
         ring = ctx.enter_context(tc.tile_pool(name="ring", bufs=2))
-        psum = ctx.enter_context(tc.psum_pool(name="psum", bufs=4))
+        psum = ctx.enter_context(tc.psum_pool(name="psum", bufs=1))
 
-        def held(name, shape, dtype, align=64):
+        def held(name, shape, dtype):
             if name in OFFSET:
-                return shared.tile(shape, dtype, name=name, align_bytes=align, offset=OFFSET[name])
-            return keep.tile(shape, dtype, name=name, align_bytes=align)
+                return shared.tile(shape, dtype, name=name, align_bytes=64, offset=OFFSET[name])
+            return keep.tile(shape, dtype, name=name, align_bytes=64)
 
-        def bank(tag):
-            return psum.tile([P, HALF], F32, name=tag, tag=tag)
+        def bank(number):
+            return psum.tile([P, HALF], F32, name=f"bank{number}", tag=f"bank{number}")
 
         offsets = keep.tile([P, S // 16], U16, name="offsets")
         nc.sync.dma_start(offsets[:], offs)
 
         scale_window = held("scale_window", [P, T], U8)
         w1_scales_raw = held("w1_scales_raw", [P, PASSES, H], U8)
-        v_scales = held("v_scales", [P, PASSES, S], U8)
-        warm_in = held("warm_in", [P, 16], F32, align=32)
-        warm_out = held("warm_out", [P, 16], F32)
-        nc.vector.memset(scale_window[:].bitcast(I32), 0)
-        nc.gpsimd.memset(w1_scales_raw[:].bitcast(I32), 0)
-        nc.vector.memset(warm_in[:], 1.0)
-        nc.scalar.activation(warm_out[:], warm_in[:], ACT.Abs_reciprocal_sqrt)
-        nc.vector.memset(v_scales[:].bitcast(I32), 0)
         w3_scales_raw = held("w3_scales_raw", [P, 1, H], U8)
+        early_scales = held("early_scales", [P, 2, S], U8)
+        last_scales = held("last_scales", [P, S], U8)
+        nc.vector.memset(w1_scales_raw[:].bitcast(I32), 0)
+        nc.vector.memset(early_scales[:].bitcast(I32), 0)
+        nc.vector.memset(last_scales[:].bitcast(I32), 0)
         nc.vector.memset(w3_scales_raw[:].bitcast(I32), 0)
+
+        scale_words = tab_scales.bitcast(I32)
+        nc.sync.dma_start(scale_window[0:P:4, :].bitcast(I32), scale_words[0:2].rearrange("a q n -> q a n"))
+        nc.sync.dma_start(scale_window[2:P:4, :].bitcast(I32), scale_words[1:3].rearrange("a q n -> q a n"))
+        nc.sync.dma_start(scale_window[1:P:2, :].bitcast(I32),
+                          scale_words[0].unsqueeze(1).to_broadcast([BLOCKS, 4, T // 4]))
 
         tab = {}
 
@@ -115,133 +103,145 @@ def tile_list_plankton_tendency_kernel(
             tab[a] = held(f"tab{a}", [P, T], I32)
             nc.sync.dma_start(tab[a][:], tab_words[a].rearrange("p t i -> p (t i)").bitcast(I32))
 
-        def scale_rows(tile, d):
-            return tile[32 * d + 4 : 32 * d + 28 : 2, :].bitcast(I32)
+        w2_raw = {}
+
+        def load_w2(a):
+            w2_raw[a] = held(f"w2_raw{a}", [P, PACK, H], F32)
+            rows = w2[P * PACK * a : P * PACK * (a + 1), :]
+            nc.sync.dma_start(w2_raw[a][:], rows.rearrange("(p j) c -> p j c", j=PACK))
 
         def quadrant_rows(scales, d):
             return scales.bitcast(I32)[:, 4 * d : 4 * d + 4, :]
 
-        load_tab(0)
-        for d in range(QUADS):
-            (nc.scalar, nc.sync)[d % 2].dma_start(
-                scale_rows(scale_window, d), quadrant_rows(tab_scales, d).rearrange("a s n -> s a n")
+        def order_columns(name, raw, dtype):
+            done = held(name, [P, raw.shape[1], raw.shape[2]], dtype)
+            nc.vector.tensor_copy(
+                done[:].bitcast(I32).rearrange("p a (t q w) -> p a t q w", t=TILES, q=BLOCKS),
+                raw[:].bitcast(I32).rearrange("p a (q t w) -> p a t q w", t=TILES, q=BLOCKS),
             )
+            return done
+
         w1_raw = held("w1_raw", [P, PASSES, 2 * H], U8)
         nc.sync.dma_start(w1_raw[:].bitcast(I32), w1_words.bitcast(I32).rearrange("a p n -> p a n"))
+        load_tab(0)
         load_tab(1)
-        load_tab(2)
 
         for d in range(QUADS):
-            nc.gpsimd.dma_start(
+            (nc.scalar, nc.gpsimd)[d // 2].dma_start(
                 w1_scales_raw[32 * d : 32 * d + 4, :, :].bitcast(I32),
                 quadrant_rows(w1_scales, d).rearrange("a s n -> s a n"),
-            )
-        for d in range(QUADS):
-            nc.gpsimd.dma_start(
-                w3_scales_raw[32 * d + 4 : 32 * d + 16, 0, :].bitcast(I32), quadrant_rows(w3_scales, d)
             )
 
         gathered_scales = held("gathered_scales", [P, S], U8)
         nc.vector.tensor_copy(gathered_scales[:], scale_window[:].indirect(offsets[:]))
         for d in range(QUADS):
-            (nc.scalar, nc.sync)[d % 2].dma_start(
-                v_scales[32 * d : 32 * d + 4, :, :].bitcast(I32), scale_rows(gathered_scales, d)
+            nc.scalar.dma_start(
+                early_scales[32 * d : 32 * d + 4, :, :].bitcast(I32),
+                gathered_scales[32 * d : 32 * d + 32 : 4, :].bitcast(I32),
+            )
+        for d in range(QUADS):
+            nc.scalar.dma_start(
+                last_scales[32 * d : 32 * d + 4, :].bitcast(I32),
+                gathered_scales[32 * d + 6 : 32 * d + 32 : 8, :].bitcast(I32),
             )
 
-        w2_raw = {}
-        for a in range(PASSES):
-            w2_raw[a] = held(f"w2_raw{a}", [P, PACK, H], F32)
-            rows = w2[P * PACK * a : P * PACK * (a + 1), :]
-            nc.sync.dma_start(w2_raw[a][:], rows.rearrange("(p j) c -> p j c", j=PACK))
+        for d in range(QUADS):
+            nc.gpsimd.dma_start(
+                w3_scales_raw[32 * d + 4 : 32 * d + 16, 0, :].bitcast(I32), quadrant_rows(w3_scales, d)
+            )
+        w1_codes = order_columns("w1_codes", w1_raw, U8)
+        load_tab(2)
+        load_w2(0)
         drift_cols = held("drift_cols", [P, OUT_TILES], F32)
         with nc.allow_non_contiguous_dma(reason="one drift value for each partition and tile of out"):
-            nc.gpsimd.dma_start(drift_cols[:], drift.rearrange("(m p) -> p m", p=P))
+            nc.sync.dma_start(drift_cols[:], drift.rearrange("(m p) -> p m", p=P))
+        load_w2(1)
+        load_w2(2)
 
         v_words = {}
+        for a in range(PASSES):
+            both = held(f"v_words{a}", [P, 2, HALF], U32)
+            for half in range(2):
+                v_words[a, half] = both[:, half, :]
 
         def gather_words(a, half):
-            v_words[a, half] = held(f"v_words{a}_{half}", [P, HALF], U32)
             entries = offsets[:, half * (HALF // 16) : (half + 1) * (HALF // 16)]
-            nc.vector.tensor_copy(v_words[a, half][:], tab[a][:].bitcast(U32).indirect(entries))
-
-        def order_columns(name, raw, dtype, first=0, count=TILES):
-            done = held(name, [P, raw.shape[1], raw.shape[2] * count // TILES], dtype)
-            source = raw[:].bitcast(I32).rearrange("p a (q t w) -> p a t q w", t=TILES, q=BLOCKS)
-            nc.vector.tensor_copy(
-                done[:].bitcast(I32).rearrange("p a (t q w) -> p a t q w", t=count, q=BLOCKS),
-                source[:, :, first : first + count],
-            )
-            return done
-
-        w1_codes = order_columns("w1_codes", w1_raw, U8)
-        gather_words(0, 0)
-        w1_scales_first = order_columns("w1_scales_first", w1_scales_raw, U8, 0, 2)
-        gather_words(0, 1)
-        gather_words(1, 0)
-        gather_words(2, 0)
-        gather_words(2, 1)
-        w1_scales_rest = order_columns("w1_scales_rest", w1_scales_raw, U8, 2, 2)
-        gather_words(1, 1)
-
-        w2_codes = [held(f"w2_codes{a}", [P, H], U32) for a in range(PASSES)]
-        w2_scales = [held(f"w2_scales{a}", [P, H], U8) for a in range(PASSES)]
-        w2_bf = {}
-
-        def round_w2(a):
-            w2_bf[a] = held(f"w2_bf{a}", [P, PACK * H], BF16)
-            rounded = w2_bf[a][:].rearrange("p (t q i j) -> p t q j i", t=TILES, q=BLOCKS, j=PACK)
-            source = w2_raw[a][:].rearrange("p j (q t i) -> p t q j i", t=TILES, q=BLOCKS)
-            for pair in range(2):
-                copy = nc.scalar.copy if 2 * a + pair < PASSES else nc.vector.tensor_copy
-                copy(rounded[:, 2 * pair : 2 * pair + 2], source[:, 2 * pair : 2 * pair + 2])
+            nc.vector.tensor_copy(v_words[a, half], tab[a][:].bitcast(U32).indirect(entries))
 
         def quantise(codes, scales, values):
             nc.vector.quantize_mx(out=codes.bitcast(FP8X4), scales=scales, in_=values)
 
-        def table_pass(acc, codes, scales, a, lo, width):
+        def table_pass(acc, codes, scales, a, lo, width, start, stop):
             half, at = divmod(lo, HALF)
+            v_scales = last_scales[:] if a == PASSES - 1 else early_scales[:, a, :]
             nc.tensor.matmul_mx(
                 out=acc,
                 lhsT=codes,
                 lhsT_scale=scales,
                 rhs=v_words[a, half][:, at : at + width].bitcast(FP8X4),
-                rhs_scale=v_scales[:, a, lo : lo + width],
-                start=(a == 0),
-                stop=(a == PASSES - 1),
+                rhs_scale=v_scales[:, lo : lo + width],
+                start=start,
+                stop=stop,
             )
 
-        def uptake(half, t):
-            acc = bank("first")
-            pair_scales = (w1_scales_first, w1_scales_rest)[t // 2]
-            for a in range(PASSES):
-                table_pass(acc[:], w1_codes[:, a, 2 * P * t : 2 * P * (t + 1)].bitcast(FP4X4),
-                           pair_scales[:, a, P * (t % 2) : P * (t % 2 + 1)], a, HALF * half, HALF)
-            return acc
+        def pair_pass(acc, codes, scales, a, quarter, u):
+            for e in range(2):
+                t = 2 * u + e
+                table_pass(acc[:, QUARTER * e : QUARTER * (e + 1)], codes(a, t), scales[a][:, P * t : P * (t + 1)],
+                           a, QUARTER * quarter, QUARTER, a == 0 and e == 0, a == PASSES - 1 and e == 1)
 
-        def growth_pass(acc, a, half, t):
-            table_pass(acc[:], w2_codes[a][:, P * t : P * (t + 1)].bitcast(FP8X4),
-                       w2_scales[a][:, P * t : P * (t + 1)], a, HALF * half, HALF)
+        def w1_tile(a, t):
+            return w1_codes[:, a, 2 * P * t : 2 * P * (t + 1)].bitcast(FP4X4)
 
-        def late_growth(t):
-            acc = bank("second")
-            for a in range(PASSES):
-                growth_pass(acc, a, 1, t)
-            return acc
+        gather_words(0, 0)
+        gather_words(0, 1)
+        w1_scale_rows = order_columns("w1_scale_rows", w1_scales_raw, U8)
+        w1_planes = [w1_scale_rows[:, a, :] for a in range(PASSES)]
+        uptake = {(quarter, u): bank(2 * quarter + u) for quarter in range(4) for u in range(2)}
+        for a in range(PASSES):
+            for half in range(2):
+                if a > 0:
+                    gather_words(a, half)
+                for quarter in (2 * half, 2 * half + 1):
+                    for u in range(2):
+                        pair_pass(uptake[quarter, u], w1_tile, w1_planes, a, quarter, u)
 
-        def mortality(j):
-            acc = bank("first")
+        w2_codes = [held(f"w2_codes{a}", [P, H], U32) for a in range(PASSES)]
+        w2_scales = [held(f"w2_scales{a}", [P, H], U8) for a in range(PASSES)]
+        w2_bf = [held(f"w2_bf{a}", [P, PACK * H], BF16) for a in range(PASSES)]
+
+        def round_w2(a):
+            rounded = w2_bf[a][:].rearrange("p (t q i j) -> p t q j i", t=TILES, q=BLOCKS, j=PACK)
+            source = w2_raw[a][:].rearrange("p j (q t i) -> p t q j i", t=TILES, q=BLOCKS)
+            nc.vector.tensor_copy(rounded[:, 0:2], source[:, 0:2])
+            for t in (2, 3):
+                nc.gpsimd.tensor_scalar(rounded[:, t], source[:, t], 1.0, 0.0, ALU.mult, ALU.add)
+
+        def quantise_w2(a, lo, hi):
+            quantise(w2_codes[a][:, lo:hi], w2_scales[a][:, lo:hi], w2_bf[a][:, PACK * lo : PACK * hi])
+
+        def w2_tile(a, t):
+            return w2_codes[a][:, P * t : P * (t + 1)].bitcast(FP8X4)
+
+        def growth_pass(a, quarter, u):
+            pair_pass(growth[quarter, u], w2_tile, w2_scales, a, quarter, u)
+
+        def mortality(j, number):
+            acc = bank(number)
             for t in range(TILES):
                 for a in range(PASSES):
                     table_pass(acc[:, SLICE * t : SLICE * (t + 1)],
                                w3_codes[:, a, P * t : P * (t + 1)].bitcast(FP8X4),
-                               w3_scale_rows[4 * (a + 1) : P, 0, P * t : P * (t + 1)], a, SLICE * j, SLICE)
+                               w3_scale_rows[4 * (a + 1) : P, 0, P * t : P * (t + 1)], a, SLICE * j, SLICE,
+                               a == 0, a == PASSES - 1)
             return acc
 
         saturated = {}
 
-        def saturate(acc, half, t):
+        def saturate(half, t):
+            acc = uptake[half, t]
             magnitude = ring.tile([P, HALF], F32, name="magnitude")
-            root = held(f"root{half}_{t}", [P, HALF], F32)
+            root = ring.tile([P, HALF], F32, name="root")
             inverse = ring.tile([P, HALF], F32, name="inverse", bufs=4)
             nc.scalar.activation(magnitude[:], acc[:], ACT.Abs)
             nc.scalar.activation(root[:], magnitude[:], ACT.Abs_reciprocal_sqrt, bias=1.0)
@@ -249,13 +249,14 @@ def tile_list_plankton_tendency_kernel(
             saturated[half, t] = held(f"saturated{half}_{t}", [P, HALF], F32)
             nc.vector.tensor_tensor(saturated[half, t][:], acc[:], inverse[:], ALU.mult)
 
-        gain = [held(f"gain{half}", [P, TILES, HALF], F32) for half in range(2)]
+        gain = [held(f"gain{quarter}", [P, TILES, QUARTER], F32) for quarter in range(4)]
 
-        def multiply_growth(acc, half, t):
-            nc.vector.tensor_tensor(gain[half][:, t, :], acc[:], saturated[half, t][:], ALU.mult)
+        def multiply_growth(quarter, u):
+            nc.vector.tensor_tensor(gain[quarter][:, 2 * u : 2 * u + 2, :].rearrange("p e c -> p (e c)"),
+                                    growth[quarter, u][:], saturated[quarter, u][:], ALU.mult)
 
         def net_growth(acc, j):
-            half, at = divmod(SLICE * j, HALF)
+            half, at = divmod(SLICE * j, QUARTER)
             h_bf = ring.tile([P, TILES * SLICE], BF16, name="h_bf", align_bytes=64)
             nc.vector.tensor_tensor(
                 h_bf[:].rearrange("p (c i t) -> p c t i", t=TILES, i=4),
@@ -268,11 +269,11 @@ def tile_list_plankton_tendency_kernel(
         w4_codes = held("w4_codes", [P, N], U32)
         w4_scales = held("w4_scales", [P, N], U8)
 
-        def tendencies(h_bf, j):
+        def tendencies(h_bf, j, number):
             h_codes = ring.tile([P, SLICE], U32, name="h_codes", align_bytes=64, bufs=4)
             h_scales = ring.tile([P, SLICE], U8, name="h_scales", align_bytes=64, bufs=4)
             quantise(h_codes[:], h_scales[:], h_bf[:])
-            acc = bank("second")
+            acc = bank(number)
             result = ring.tile([P, OUT_TILES, SLICE], F32, name="result", bufs=4)
             for m in range(OUT_TILES):
                 nc.tensor.matmul_mx(
@@ -289,62 +290,81 @@ def tile_list_plankton_tendency_kernel(
                                      bias=drift_cols[:, m : m + 1])
             nc.sync.dma_start(out[:, SLICE * j : SLICE * (j + 1)].rearrange("(m p) s -> p m s", p=P), result[:])
 
-        early_a = [uptake(0, t) for t in range(TILES)]
-        early_b = [bank("second") for t in range(TILES)]
-        late_a, late_b, loss = {}, {}, {}
-        for a in range(PASSES):
-            round_w2(a)
-            if a == 0:
-                w3_raw = held("w3_raw", [P, PASSES, H], I32)
-                nc.sync.dma_start(w3_raw[:], w3_words.rearrange("a p e i -> p a (e i)").bitcast(I32))
-            if a == 1:
-                w4_raw = held("w4_raw", [P, TILES, N], F32)
-                w4_rows = w4.rearrange("(q t i) n -> t q i n", t=TILES, i=8)
-                for t in range(TILES):
-                    nc.sync.dma_start(w4_raw[:, t, :], w4_rows[t])
-            saturate(early_a[a], 0, a)
-            quantise(w2_codes[a][:], w2_scales[a][:], w2_bf[a][:])
-            if a < PASSES - 1:
-                late_a[a] = uptake(1, a)
-            for t in range(TILES):
-                growth_pass(early_b[t], a, 0, t)
+        growth = {}
+        w3_raw = held("w3_raw", [P, PASSES, H], I32)
+        nc.sync.dma_start(w3_raw[:], w3_words.rearrange("a p e i -> p a (e i)").bitcast(I32))
+        w4_raw = held("w4_raw", [P, TILES, N], F32)
+        w4_rows = w4.rearrange("(q t i) n -> t q i n", t=TILES, i=8)
+        for t in range(TILES):
+            nc.sync.dma_start(w4_raw[:, t, :], w4_rows[t])
+
         w3_scale_rows = order_columns("w3_scale_rows", w3_scales_raw, U8)
+        round_w2(0)
+        saturate(0, 0)
+        round_w2(1)
+        quantise_w2(0, 0, H)
+        saturate(0, 1)
+        round_w2(2)
+        quantise_w2(1, 0, H)
+        for u in range(2):
+            growth[0, u] = bank(u)
+            for a in range(PASSES - 1):
+                growth_pass(a, 0, u)
+        for u in range(2):
+            quantise_w2(2, 2 * P * u, 2 * P * (u + 1))
+            growth_pass(2, 0, u)
         w3_codes = order_columns("w3_codes", w3_raw, U32)
-        loss[0] = mortality(0)
-        saturate(early_a[3], 0, 3)
-        late_a[2] = uptake(1, 2)
-
-        def hand_over_growth(t):
-            multiply_growth(early_b[t], 0, t)
-            late_b[t] = late_growth(t)
-
-        hand_over_growth(0)
-        saturate(late_a[0], 1, 0)
-        loss[1] = mortality(1)
-        hand_over_growth(1)
-        hand_over_growth(2)
-        saturate(late_a[1], 1, 1)
-        late_a[3] = uptake(1, 3)
-        hand_over_growth(3)
 
         w4_bf = held("w4_bf", [P, TILES * N], BF16)
-        nc.scalar.copy(
-            w4_bf[:].rearrange("p (c i t) -> p c t i", t=TILES, i=4),
-            w4_raw[:].rearrange("p t (c i) -> p c t i", i=4),
-        )
-        for lo, hi in ((0, 2 * P), (2 * P, N)):
-            quantise(w4_codes[:, lo:hi], w4_scales[:, lo:hi], w4_bf[:, TILES * lo : TILES * hi])
+        for m in range(OUT_TILES):
+            nc.gpsimd.tensor_scalar(
+                w4_bf[:, TILES * P * m : TILES * P * (m + 1)].rearrange("p (c i t) -> p c t i", t=TILES, i=4),
+                w4_raw[:, :, P * m : P * (m + 1)].rearrange("p t (c i) -> p c t i", i=4),
+                1.0, 0.0, ALU.mult, ALU.add,
+            )
 
-        pending = None
-        for j in range(S // SLICE):
-            if j not in loss:
-                loss[j] = mortality(j)
-            h_bf = net_growth(loss[j], j)
-            if j + 2 < TILES:
-                saturate(late_a[j + 2], 1, j + 2)
-            if j < TILES:
-                multiply_growth(late_b[j], 1, j)
-            if pending is not None:
-                tendencies(*pending)
-            pending = (h_bf, j)
-        tendencies(*pending)
+        growth_pair, loss_pair, out_pair = (0, 1, 2, 1), (0, 1, 0, 2), (0, 1, 0, 3)
+        loss, h_bf = {}, {}
+
+        def grow(quarter):
+            for u in range(2):
+                growth[quarter, u] = bank(2 * growth_pair[quarter] + u)
+                for a in range(PASSES):
+                    growth_pass(a, quarter, u)
+
+        def lose(quarter):
+            for u in range(2):
+                loss[2 * quarter + u] = mortality(2 * quarter + u, 2 * loss_pair[quarter] + u)
+
+        def multiply(quarter):
+            for u in range(2):
+                multiply_growth(quarter, u)
+
+        def finish(quarter):
+            for u in range(2):
+                h_bf[u] = net_growth(loss[2 * quarter + u], 2 * quarter + u)
+            for u in range(2):
+                tendencies(h_bf[u], 2 * quarter + u, 2 * out_pair[quarter] + u)
+
+        saturate(1, 0)
+        saturate(1, 1)
+        grow(1)
+        multiply(0)
+        lose(0)
+        quantise(w4_codes[:], w4_scales[:], w4_bf[:])
+        multiply(1)
+        lose(1)
+        finish(0)
+        saturate(2, 0)
+        saturate(2, 1)
+        grow(2)
+        lose(2)
+        finish(1)
+        grow(3)
+        multiply(2)
+        lose(3)
+        saturate(3, 0)
+        saturate(3, 1)
+        finish(2)
+        multiply(3)
+        finish(3)

@@ -36,27 +36,29 @@ WINDOW = W1_CODES + 2 * W1_SCALES - REACH
 V_FIRST = WINDOW + REACH
 W2_FIRST = V_FIRST + 2 * WORDS
 TAB0 = W2_FIRST + STAGE - REACH
-TAB2 = TAB0 + STAGE
-TAB1 = TAB2 + STAGE + H
-W2_SECOND = TAB1 + STAGE + REACH
+W2_SECOND = TAB0 + STAGE - REACH
+TAB2 = W2_SECOND + STAGE + W1_SCALES // 2
+W2_LAST = TAB2 + STAGE + S + H
+TAB1 = W2_LAST + STAGE - REACH
 OFFSET = {
     "w1_codes": W1_CODES,
     "scale_window": WINDOW,
     "v_words0": V_FIRST,
     "w2_raw0": W2_FIRST,
-    "w4_raw": W2_FIRST,
     "tab0": TAB0,
     "drift_cols": TAB0 + REACH,
-    "w1_scale_rows": TAB0 + 2 * REACH,
-    "v_words1": TAB0 + 2 * REACH + W1_SCALES,
-    "w1_raw": TAB2,
-    "tab2": TAB2,
-    "w3_raw": TAB2,
-    "tab1": TAB1,
-    "w3_scale_rows": TAB1 - H + REACH,
-    "w2_raw2": TAB1 + REACH,
-    "gathered_scales": W2_SECOND,
+    "v_words1": TAB0 + 2 * REACH,
+    "w1_scales_first": TAB0 + 2 * REACH + 2 * WORDS,
     "w2_raw1": W2_SECOND,
+    "w1_scales_rest": TAB2 - W1_SCALES // 2 + REACH,
+    "tab2": TAB2,
+    "w1_raw": W2_LAST - 2 * W1_SCALES,
+    "last_scales": TAB2 + STAGE,
+    "w2_raw2": W2_LAST,
+    "tab1": TAB1,
+    "w4_raw": TAB1 + REACH,
+    "w3_scale_rows": W2_FIRST,
+    "w3_raw": TAB1 + STAGE - REACH,
 }
 
 
@@ -86,16 +88,19 @@ def tile_list_plankton_tendency_kernel(
         w3_scales_raw = held("w3_scales_raw", [P, 1, H], U8)
         early_scales = held("early_scales", [P, 2, S], U8)
         last_scales = held("last_scales", [P, S], U8)
-        nc.vector.memset(w1_scales_raw[:].bitcast(I32), 0)
+        nc.gpsimd.memset(w1_scales_raw[:].bitcast(I32), 0)
         nc.vector.memset(early_scales[:].bitcast(I32), 0)
-        nc.vector.memset(last_scales[:].bitcast(I32), 0)
         nc.vector.memset(w3_scales_raw[:].bitcast(I32), 0)
+        warm_in = held("warm_in", [P, 16], F32)
+        warm_out = held("warm_out", [P, 16], F32)
+        nc.vector.memset(warm_in[:], 1.0)
+        nc.scalar.activation(warm_out[:], warm_in[:], ACT.Abs_reciprocal_sqrt)
 
         scale_words = tab_scales.bitcast(I32)
         nc.sync.dma_start(scale_window[0:P:4, :].bitcast(I32), scale_words[0:2].rearrange("a q n -> q a n"))
         nc.sync.dma_start(scale_window[2:P:4, :].bitcast(I32), scale_words[1:3].rearrange("a q n -> q a n"))
-        nc.sync.dma_start(scale_window[1:P:2, :].bitcast(I32),
-                          scale_words[0].unsqueeze(1).to_broadcast([BLOCKS, 4, T // 4]))
+        nc.sync.dma_start(scale_window[1:P:4, :].bitcast(I32), scale_words[0:2].rearrange("a q n -> q a n"))
+        nc.sync.dma_start(scale_window[3:P:4, :].bitcast(I32), scale_words[1:3].rearrange("a q n -> q a n"))
 
         tab = {}
 
@@ -113,11 +118,12 @@ def tile_list_plankton_tendency_kernel(
         def quadrant_rows(scales, d):
             return scales.bitcast(I32)[:, 4 * d : 4 * d + 4, :]
 
-        def order_columns(name, raw, dtype):
-            done = held(name, [P, raw.shape[1], raw.shape[2]], dtype)
+        def order_columns(name, raw, dtype, first=0, count=TILES):
+            done = held(name, [P, raw.shape[1], raw.shape[2] * count // TILES], dtype)
+            source = raw[:].bitcast(I32).rearrange("p a (q t w) -> p a t q w", t=TILES, q=BLOCKS)
             nc.vector.tensor_copy(
-                done[:].bitcast(I32).rearrange("p a (t q w) -> p a t q w", t=TILES, q=BLOCKS),
-                raw[:].bitcast(I32).rearrange("p a (q t w) -> p a t q w", t=TILES, q=BLOCKS),
+                done[:].bitcast(I32).rearrange("p a (t q w) -> p a t q w", t=count, q=BLOCKS),
+                source[:, :, first : first + count],
             )
             return done
 
@@ -127,7 +133,7 @@ def tile_list_plankton_tendency_kernel(
         load_tab(1)
 
         for d in range(QUADS):
-            (nc.scalar, nc.gpsimd)[d // 2].dma_start(
+            nc.gpsimd.dma_start(
                 w1_scales_raw[32 * d : 32 * d + 4, :, :].bitcast(I32),
                 quadrant_rows(w1_scales, d).rearrange("a s n -> s a n"),
             )
@@ -139,24 +145,22 @@ def tile_list_plankton_tendency_kernel(
                 early_scales[32 * d : 32 * d + 4, :, :].bitcast(I32),
                 gathered_scales[32 * d : 32 * d + 32 : 4, :].bitcast(I32),
             )
+
+        w1_codes = order_columns("w1_codes", w1_raw, U8)
+        load_tab(2)
+        nc.vector.memset(last_scales[:].bitcast(I32), 0)
         for d in range(QUADS):
             nc.scalar.dma_start(
                 last_scales[32 * d : 32 * d + 4, :].bitcast(I32),
                 gathered_scales[32 * d + 6 : 32 * d + 32 : 8, :].bitcast(I32),
             )
-
         for d in range(QUADS):
             nc.gpsimd.dma_start(
                 w3_scales_raw[32 * d + 4 : 32 * d + 16, 0, :].bitcast(I32), quadrant_rows(w3_scales, d)
             )
-        w1_codes = order_columns("w1_codes", w1_raw, U8)
-        load_tab(2)
-        load_w2(0)
         drift_cols = held("drift_cols", [P, OUT_TILES], F32)
         with nc.allow_non_contiguous_dma(reason="one drift value for each partition and tile of out"):
             nc.sync.dma_start(drift_cols[:], drift.rearrange("(m p) -> p m", p=P))
-        load_w2(1)
-        load_w2(2)
 
         v_words = {}
         for a in range(PASSES):
@@ -187,7 +191,7 @@ def tile_list_plankton_tendency_kernel(
         def pair_pass(acc, codes, scales, a, quarter, u):
             for e in range(2):
                 t = 2 * u + e
-                table_pass(acc[:, QUARTER * e : QUARTER * (e + 1)], codes(a, t), scales[a][:, P * t : P * (t + 1)],
+                table_pass(acc[:, QUARTER * e : QUARTER * (e + 1)], codes(a, t), scales(a, t),
                            a, QUARTER * quarter, QUARTER, a == 0 and e == 0, a == PASSES - 1 and e == 1)
 
         def w1_tile(a, t):
@@ -195,17 +199,26 @@ def tile_list_plankton_tendency_kernel(
 
         gather_words(0, 0)
         gather_words(0, 1)
-        w1_scale_rows = order_columns("w1_scale_rows", w1_scales_raw, U8)
-        w1_planes = [w1_scale_rows[:, a, :] for a in range(PASSES)]
+        w1_pair = {0: order_columns("w1_scales_first", w1_scales_raw, U8, 0, 2)}
+        load_w2(0)
+        load_w2(1)
         uptake = {(quarter, u): bank(2 * quarter + u) for quarter in range(4) for u in range(2)}
+
+        def w1_scale_tile(a, t):
+            return w1_pair[t // 2][:, a, P * (t % 2) : P * (t % 2 + 1)]
+
         for a in range(PASSES):
             for half in range(2):
                 if a > 0:
                     gather_words(a, half)
                 for quarter in (2 * half, 2 * half + 1):
-                    for u in range(2):
-                        pair_pass(uptake[quarter, u], w1_tile, w1_planes, a, quarter, u)
+                    pair_pass(uptake[quarter, 0], w1_tile, w1_scale_tile, a, quarter, 0)
+        w1_pair[1] = order_columns("w1_scales_rest", w1_scales_raw, U8, 2, 2)
+        for quarter in range(4):
+            for a in range(PASSES):
+                pair_pass(uptake[quarter, 1], w1_tile, w1_scale_tile, a, quarter, 1)
 
+        load_w2(2)
         w2_codes = [held(f"w2_codes{a}", [P, H], U32) for a in range(PASSES)]
         w2_scales = [held(f"w2_scales{a}", [P, H], U8) for a in range(PASSES)]
         w2_bf = [held(f"w2_bf{a}", [P, PACK * H], BF16) for a in range(PASSES)]
@@ -213,9 +226,8 @@ def tile_list_plankton_tendency_kernel(
         def round_w2(a):
             rounded = w2_bf[a][:].rearrange("p (t q i j) -> p t q j i", t=TILES, q=BLOCKS, j=PACK)
             source = w2_raw[a][:].rearrange("p j (q t i) -> p t q j i", t=TILES, q=BLOCKS)
-            nc.vector.tensor_copy(rounded[:, 0:2], source[:, 0:2])
-            for t in (2, 3):
-                nc.gpsimd.tensor_scalar(rounded[:, t], source[:, t], 1.0, 0.0, ALU.mult, ALU.add)
+            for u in range(2):
+                nc.vector.tensor_copy(rounded[:, 2 * u : 2 * u + 2], source[:, 2 * u : 2 * u + 2])
 
         def quantise_w2(a, lo, hi):
             quantise(w2_codes[a][:, lo:hi], w2_scales[a][:, lo:hi], w2_bf[a][:, PACK * lo : PACK * hi])
@@ -223,8 +235,11 @@ def tile_list_plankton_tendency_kernel(
         def w2_tile(a, t):
             return w2_codes[a][:, P * t : P * (t + 1)].bitcast(FP8X4)
 
+        def w2_scale_tile(a, t):
+            return w2_scales[a][:, P * t : P * (t + 1)]
+
         def growth_pass(a, quarter, u):
-            pair_pass(growth[quarter, u], w2_tile, w2_scales, a, quarter, u)
+            pair_pass(growth[quarter, u], w2_tile, w2_scale_tile, a, quarter, u)
 
         def mortality(j, number):
             acc = bank(number)
@@ -298,8 +313,8 @@ def tile_list_plankton_tendency_kernel(
         for t in range(TILES):
             nc.sync.dma_start(w4_raw[:, t, :], w4_rows[t])
 
-        w3_scale_rows = order_columns("w3_scale_rows", w3_scales_raw, U8)
         round_w2(0)
+        w3_scale_rows = order_columns("w3_scale_rows", w3_scales_raw, U8)
         saturate(0, 0)
         round_w2(1)
         quantise_w2(0, 0, H)

@@ -20,7 +20,8 @@ P = 128
 PACK = 4
 PASSES = K // (P * PACK)
 QUADS = 4
-BLOCKS = 16
+RUN = 4
+RUNS = P // RUN
 HALF = 512
 QUARTER = 256
 SLICE = 128
@@ -120,9 +121,9 @@ def tile_list_plankton_tendency_kernel(
 
         def order_columns(name, raw, dtype, first=0, count=TILES):
             done = held(name, [P, raw.shape[1], raw.shape[2] * count // TILES], dtype)
-            source = raw[:].bitcast(I32).rearrange("p a (q t w) -> p a t q w", t=TILES, q=BLOCKS)
+            source = raw[:].bitcast(I32).rearrange("p a (q t w) -> p a t q w", t=TILES, q=RUNS)
             nc.vector.tensor_copy(
-                done[:].bitcast(I32).rearrange("p a (t q w) -> p a t q w", t=count, q=BLOCKS),
+                done[:].bitcast(I32).rearrange("p a (t q w) -> p a t q w", t=count, q=RUNS),
                 source[:, :, first : first + count],
             )
             return done
@@ -224,8 +225,8 @@ def tile_list_plankton_tendency_kernel(
         w2_bf = [held(f"w2_bf{a}", [P, PACK * H], BF16) for a in range(PASSES)]
 
         def round_w2(a):
-            rounded = w2_bf[a][:].rearrange("p (t q i j) -> p t q j i", t=TILES, q=BLOCKS, j=PACK)
-            source = w2_raw[a][:].rearrange("p j (q t i) -> p t q j i", t=TILES, q=BLOCKS)
+            rounded = w2_bf[a][:].rearrange("p (t q i j) -> p t q j i", t=TILES, q=RUNS, j=PACK)
+            source = w2_raw[a][:].rearrange("p j (q t i) -> p t q j i", t=TILES, q=RUNS)
             for u in range(2):
                 nc.vector.tensor_copy(rounded[:, 2 * u : 2 * u + 2], source[:, 2 * u : 2 * u + 2])
 
@@ -253,30 +254,36 @@ def tile_list_plankton_tendency_kernel(
 
         saturated = {}
 
+        def weave(acc, tiles):
+            return acc[:].rearrange("p (e c) -> p c e", e=tiles)
+
+        def woven(values):
+            return values.rearrange("p (c e) -> p c e", e=2)
+
         def saturate(half, t):
             acc = uptake[half, t]
             magnitude = ring.tile([P, HALF], F32, name="magnitude")
             root = ring.tile([P, HALF], F32, name="root")
             inverse = ring.tile([P, HALF], F32, name="inverse", bufs=4)
-            nc.scalar.activation(magnitude[:], acc[:], ACT.Abs)
+            nc.scalar.activation(woven(magnitude[:]), weave(acc, 2), ACT.Abs)
             nc.scalar.activation(root[:], magnitude[:], ACT.Abs_reciprocal_sqrt, bias=1.0)
             nc.scalar.activation(inverse[:], root[:], ACT.Square)
             saturated[half, t] = held(f"saturated{half}_{t}", [P, HALF], F32)
-            nc.vector.tensor_tensor(saturated[half, t][:], acc[:], inverse[:], ALU.mult)
+            nc.vector.tensor_tensor(woven(saturated[half, t][:]), weave(acc, 2), woven(inverse[:]), ALU.mult)
 
-        gain = [held(f"gain{quarter}", [P, TILES, QUARTER], F32) for quarter in range(4)]
+        gain = [held(f"gain{quarter}", [P, 2, 2 * QUARTER], F32) for quarter in range(4)]
 
         def multiply_growth(quarter, u):
-            nc.vector.tensor_tensor(gain[quarter][:, 2 * u : 2 * u + 2, :].rearrange("p e c -> p (e c)"),
-                                    growth[quarter, u][:], saturated[quarter, u][:], ALU.mult)
+            nc.vector.tensor_tensor(woven(gain[quarter][:, u, :]), weave(growth[quarter, u], 2),
+                                    woven(saturated[quarter, u][:]), ALU.mult)
 
         def net_growth(acc, j):
             half, at = divmod(SLICE * j, QUARTER)
             h_bf = ring.tile([P, TILES * SLICE], BF16, name="h_bf", align_bytes=64)
             nc.vector.tensor_tensor(
-                h_bf[:].rearrange("p (c i t) -> p c t i", t=TILES, i=4),
-                gain[half][:, :, at : at + SLICE].rearrange("p t (c i) -> p c t i", i=4),
-                acc[:].rearrange("p (t c i) -> p c t i", t=TILES, i=4),
+                h_bf[:].rearrange("p (c u e) -> p c u e", u=2, e=2),
+                gain[half][:, :, 2 * at : 2 * (at + SLICE)].rearrange("p u (c e) -> p c u e", e=2),
+                acc[:].rearrange("p (u e c) -> p c u e", u=2, e=2),
                 ALU.subtract,
             )
             return h_bf
@@ -309,7 +316,7 @@ def tile_list_plankton_tendency_kernel(
         w3_raw = held("w3_raw", [P, PASSES, H], I32)
         nc.sync.dma_start(w3_raw[:], w3_words.rearrange("a p e i -> p a (e i)").bitcast(I32))
         w4_raw = held("w4_raw", [P, TILES, N], F32)
-        w4_rows = w4.rearrange("(q t i) n -> t q i n", t=TILES, i=8)
+        w4_rows = w4.rearrange("(q t i) n -> t q i n", t=TILES, i=RUN)
         for t in range(TILES):
             nc.sync.dma_start(w4_raw[:, t, :], w4_rows[t])
 

@@ -20,7 +20,7 @@ P = 128
 PACK = 4
 PASSES = K // (P * PACK)
 QUADS = 4
-RUN = 4
+RUN = 8
 RUNS = P // RUN
 HALF = 512
 QUARTER = 256
@@ -29,6 +29,7 @@ TILES = H // P
 OUT_TILES = N // P
 STAGE = 4 * T
 
+W2_ORDER = (0, 1, 2)
 REACH = 128
 WORDS = 4 * HALF
 W1_SCALES = PASSES * H
@@ -39,26 +40,37 @@ W2_FIRST = V_FIRST + 2 * WORDS
 TAB0 = W2_FIRST + STAGE - REACH
 W2_SECOND = TAB0 + STAGE - REACH
 TAB2 = W2_SECOND + STAGE + W1_SCALES // 2
-W2_LAST = TAB2 + STAGE + S + H
+W2_LAST = TAB2 + STAGE + S + H + 2 * REACH
 TAB1 = W2_LAST + STAGE - REACH
+W2_BF = TAB1 + 2 * STAGE
 OFFSET = {
-    "w1_codes": W1_CODES,
     "scale_window": WINDOW,
     "v_words0": V_FIRST,
     "w2_raw0": W2_FIRST,
     "tab0": TAB0,
     "drift_cols": TAB0 + REACH,
     "v_words1": TAB0 + 2 * REACH,
-    "w1_scales_first": TAB0 + 2 * REACH + 2 * WORDS,
+    "w3_scales_raw": TAB0 + 2 * REACH + 2 * WORDS + W1_SCALES // 2,
     "w2_raw1": W2_SECOND,
     "w1_scales_rest": TAB2 - W1_SCALES // 2 + REACH,
     "tab2": TAB2,
-    "w1_raw": W2_LAST - 2 * W1_SCALES,
+    "w1_raw": W2_LAST - 2 * REACH - 2 * W1_SCALES,
     "last_scales": TAB2 + STAGE,
+    "w1_scales_first": TAB2 + STAGE + S + H - W1_SCALES // 2 + 2 * REACH,
     "w2_raw2": W2_LAST,
     "tab1": TAB1,
     "w4_raw": TAB1 + REACH,
-    "w3_scale_rows": W2_FIRST,
+    "w2_bf0": W2_BF,
+    "saturated0_0": W2_BF,
+    "saturated1_1": W2_BF,
+    "saturated2_1": W2_BF,
+    "saturated3_1": W2_BF,
+    "w2_bf1": W2_BF + 8 * H,
+    "saturated0_1": W2_BF + 8 * H,
+    "w2_bf2": W2_BF + 16 * H,
+    "saturated1_0": W2_BF + 16 * H,
+    "saturated2_0": W2_BF + 16 * H,
+    "saturated3_0": W2_BF + 16 * H,
     "w3_raw": TAB1 + STAGE - REACH,
 }
 
@@ -86,12 +98,11 @@ def tile_list_plankton_tendency_kernel(
 
         scale_window = held("scale_window", [P, T], U8)
         w1_scales_raw = held("w1_scales_raw", [P, PASSES, H], U8)
-        w3_scales_raw = held("w3_scales_raw", [P, 1, H], U8)
+        w3_scales_raw = held("w3_scales_raw", [P, PASSES, H], U8)
         early_scales = held("early_scales", [P, 2, S], U8)
         last_scales = held("last_scales", [P, S], U8)
         nc.gpsimd.memset(w1_scales_raw[:].bitcast(I32), 0)
         nc.vector.memset(early_scales[:].bitcast(I32), 0)
-        nc.vector.memset(w3_scales_raw[:].bitcast(I32), 0)
         warm_in = held("warm_in", [P, 16], F32)
         warm_out = held("warm_out", [P, 16], F32)
         nc.vector.memset(warm_in[:], 1.0)
@@ -101,7 +112,7 @@ def tile_list_plankton_tendency_kernel(
         nc.sync.dma_start(scale_window[0:P:4, :].bitcast(I32), scale_words[0:2].rearrange("a q n -> q a n"))
         nc.sync.dma_start(scale_window[2:P:4, :].bitcast(I32), scale_words[1:3].rearrange("a q n -> q a n"))
         nc.sync.dma_start(scale_window[1:P:4, :].bitcast(I32), scale_words[0:2].rearrange("a q n -> q a n"))
-        nc.sync.dma_start(scale_window[3:P:4, :].bitcast(I32), scale_words[1:3].rearrange("a q n -> q a n"))
+        nc.scalar.dma_start(scale_window[3:P:4, :].bitcast(I32), scale_words[1:3].rearrange("a q n -> q a n"))
 
         tab = {}
 
@@ -119,10 +130,10 @@ def tile_list_plankton_tendency_kernel(
         def quadrant_rows(scales, d):
             return scales.bitcast(I32)[:, 4 * d : 4 * d + 4, :]
 
-        def order_columns(name, raw, dtype, first=0, count=TILES):
+        def order_columns(name, raw, dtype, first=0, count=TILES, engine=nc.gpsimd):
             done = held(name, [P, raw.shape[1], raw.shape[2] * count // TILES], dtype)
             source = raw[:].bitcast(I32).rearrange("p a (q t w) -> p a t q w", t=TILES, q=RUNS)
-            nc.vector.tensor_copy(
+            engine.tensor_copy(
                 done[:].bitcast(I32).rearrange("p a (t q w) -> p a t q w", t=count, q=RUNS),
                 source[:, :, first : first + count],
             )
@@ -134,7 +145,7 @@ def tile_list_plankton_tendency_kernel(
         load_tab(1)
 
         for d in range(QUADS):
-            nc.gpsimd.dma_start(
+            (nc.gpsimd if d else nc.scalar).dma_start(
                 w1_scales_raw[32 * d : 32 * d + 4, :, :].bitcast(I32),
                 quadrant_rows(w1_scales, d).rearrange("a s n -> s a n"),
             )
@@ -149,60 +160,56 @@ def tile_list_plankton_tendency_kernel(
 
         w1_codes = order_columns("w1_codes", w1_raw, U8)
         load_tab(2)
-        nc.vector.memset(last_scales[:].bitcast(I32), 0)
+        nc.gpsimd.memset(last_scales[:].bitcast(I32), 0)
         for d in range(QUADS):
             nc.scalar.dma_start(
                 last_scales[32 * d : 32 * d + 4, :].bitcast(I32),
                 gathered_scales[32 * d + 6 : 32 * d + 32 : 8, :].bitcast(I32),
             )
-        for d in range(QUADS):
-            nc.gpsimd.dma_start(
-                w3_scales_raw[32 * d + 4 : 32 * d + 16, 0, :].bitcast(I32), quadrant_rows(w3_scales, d)
-            )
         drift_cols = held("drift_cols", [P, OUT_TILES], F32)
         with nc.allow_non_contiguous_dma(reason="one drift value for each partition and tile of out"):
             nc.sync.dma_start(drift_cols[:], drift.rearrange("(m p) -> p m", p=P))
 
-        v_words = {}
-        for a in range(PASSES):
-            both = held(f"v_words{a}", [P, 2, HALF], U32)
-            for half in range(2):
-                v_words[a, half] = both[:, half, :]
+        v_words = [held(f"v_words{a}", [P, S], U32) for a in range(PASSES)]
 
-        def gather_words(a, half):
-            entries = offsets[:, half * (HALF // 16) : (half + 1) * (HALF // 16)]
-            nc.vector.tensor_copy(v_words[a, half], tab[a][:].bitcast(U32).indirect(entries))
+        def gather_words(a, lo, hi):
+            entries = offsets[:, lo // 16 : hi // 16]
+            nc.vector.tensor_copy(v_words[a][:, lo:hi], tab[a][:].bitcast(U32).indirect(entries))
 
         def quantise(codes, scales, values):
             nc.vector.quantize_mx(out=codes.bitcast(FP8X4), scales=scales, in_=values)
 
         def table_pass(acc, codes, scales, a, lo, width, start, stop):
-            half, at = divmod(lo, HALF)
             v_scales = last_scales[:] if a == PASSES - 1 else early_scales[:, a, :]
             nc.tensor.matmul_mx(
                 out=acc,
                 lhsT=codes,
                 lhsT_scale=scales,
-                rhs=v_words[a, half][:, at : at + width].bitcast(FP8X4),
+                rhs=v_words[a][:, lo : lo + width].bitcast(FP8X4),
                 rhs_scale=v_scales[:, lo : lo + width],
                 start=start,
                 stop=stop,
             )
 
-        def pair_pass(acc, codes, scales, a, quarter, u):
+        def pair_pass(acc, codes, scales, a, quarter, u, order=(0, 1, 2)):
             for e in range(2):
                 t = 2 * u + e
                 table_pass(acc[:, QUARTER * e : QUARTER * (e + 1)], codes(a, t), scales(a, t),
-                           a, QUARTER * quarter, QUARTER, a == 0 and e == 0, a == PASSES - 1 and e == 1)
+                           a, QUARTER * quarter, QUARTER, a == order[0] and e == 0, a == order[-1] and e == 1)
 
         def w1_tile(a, t):
             return w1_codes[:, a, 2 * P * t : 2 * P * (t + 1)].bitcast(FP4X4)
 
-        gather_words(0, 0)
-        gather_words(0, 1)
+        gather_words(0, 0, S)
         w1_pair = {0: order_columns("w1_scales_first", w1_scales_raw, U8, 0, 2)}
         load_w2(0)
         load_w2(1)
+        nc.gpsimd.memset(w3_scales_raw[:].bitcast(I32), 0)
+        for d in range(QUADS):
+            nc.sync.dma_start(
+                w3_scales_raw[32 * d : 32 * d + 4, :, :].bitcast(I32),
+                quadrant_rows(w3_scales, d).rearrange("a s n -> s a n"),
+            )
         uptake = {(quarter, u): bank(2 * quarter + u) for quarter in range(4) for u in range(2)}
 
         def w1_scale_tile(a, t):
@@ -210,8 +217,10 @@ def tile_list_plankton_tendency_kernel(
 
         for a in range(PASSES):
             for half in range(2):
-                if a > 0:
-                    gather_words(a, half)
+                if a == 2:
+                    gather_words(a, HALF * half, HALF * (half + 1))
+                elif a == 1 and half == 0:
+                    gather_words(a, 0, S)
                 for quarter in (2 * half, 2 * half + 1):
                     pair_pass(uptake[quarter, 0], w1_tile, w1_scale_tile, a, quarter, 0)
         w1_pair[1] = order_columns("w1_scales_rest", w1_scales_raw, U8, 2, 2)
@@ -240,7 +249,7 @@ def tile_list_plankton_tendency_kernel(
             return w2_scales[a][:, P * t : P * (t + 1)]
 
         def growth_pass(a, quarter, u):
-            pair_pass(growth[quarter, u], w2_tile, w2_scale_tile, a, quarter, u)
+            pair_pass(growth[quarter, u], w2_tile, w2_scale_tile, a, quarter, u, W2_ORDER)
 
         def mortality(j, number):
             acc = bank(number)
@@ -248,7 +257,7 @@ def tile_list_plankton_tendency_kernel(
                 for a in range(PASSES):
                     table_pass(acc[:, SLICE * t : SLICE * (t + 1)],
                                w3_codes[:, a, P * t : P * (t + 1)].bitcast(FP8X4),
-                               w3_scale_rows[4 * (a + 1) : P, 0, P * t : P * (t + 1)], a, SLICE * j, SLICE,
+                               w3_scale_rows[:, a, P * t : P * (t + 1)], a, SLICE * j, SLICE,
                                a == 0, a == PASSES - 1)
             return acc
 
@@ -264,7 +273,7 @@ def tile_list_plankton_tendency_kernel(
             acc = uptake[half, t]
             magnitude = ring.tile([P, HALF], F32, name="magnitude")
             root = ring.tile([P, HALF], F32, name="root")
-            inverse = ring.tile([P, HALF], F32, name="inverse", bufs=4)
+            inverse = ring.tile([P, HALF], F32, name="inverse")
             nc.scalar.activation(woven(magnitude[:]), weave(acc, 2), ACT.Abs)
             nc.scalar.activation(root[:], magnitude[:], ACT.Abs_reciprocal_sqrt, bias=1.0)
             nc.scalar.activation(inverse[:], root[:], ACT.Square)
@@ -277,29 +286,29 @@ def tile_list_plankton_tendency_kernel(
             nc.vector.tensor_tensor(woven(gain[quarter][:, u, :]), weave(growth[quarter, u], 2),
                                     woven(saturated[quarter, u][:]), ALU.mult)
 
-        def net_growth(acc, j):
-            half, at = divmod(SLICE * j, QUARTER)
-            h_bf = ring.tile([P, TILES * SLICE], BF16, name="h_bf", align_bytes=64)
+        def net_growth(h_bf, acc, quarter, u):
             nc.vector.tensor_tensor(
-                h_bf[:].rearrange("p (c u e) -> p c u e", u=2, e=2),
-                gain[half][:, :, 2 * at : 2 * (at + SLICE)].rearrange("p u (c e) -> p c u e", e=2),
+                h_bf.rearrange("p (c u e) -> p c u e", u=2, e=2),
+                gain[quarter][:, :, 2 * SLICE * u : 2 * SLICE * (u + 1)].rearrange("p u (c e) -> p c u e", e=2),
                 acc[:].rearrange("p (u e c) -> p c u e", u=2, e=2),
                 ALU.subtract,
             )
-            return h_bf
 
         w4_codes = held("w4_codes", [P, N], U32)
         w4_scales = held("w4_scales", [P, N], U8)
 
-        def tendencies(h_bf, j, number):
-            h_codes = ring.tile([P, SLICE], U32, name="h_codes", align_bytes=64, bufs=4)
-            h_scales = ring.tile([P, SLICE], U8, name="h_scales", align_bytes=64, bufs=4)
-            quantise(h_codes[:], h_scales[:], h_bf[:])
-            acc = bank(number)
-            result = ring.tile([P, OUT_TILES, SLICE], F32, name="result", bufs=4)
+        def tendencies(h_bf, lo, width, banks):
+            h_codes = ring.tile([P, width], U32, name="h_codes", align_bytes=64)
+            h_scales = ring.tile([P, width], U8, name="h_scales", align_bytes=64)
+            quantise(h_codes[:], h_scales[:], h_bf)
+            accs = [bank(number) for number in banks]
+            result = ring.tile([P, OUT_TILES, width], F32, name="result", bufs=3)
+            sums = []
             for m in range(OUT_TILES):
+                which, at = divmod(width * m, HALF)
+                sums.append(accs[which][:, at : at + width])
                 nc.tensor.matmul_mx(
-                    out=acc[:, SLICE * m : SLICE * (m + 1)],
+                    out=sums[m],
                     lhsT=w4_codes[:, P * m : P * (m + 1)].bitcast(FP8X4),
                     lhsT_scale=w4_scales[:, P * m : P * (m + 1)],
                     rhs=h_codes[:].bitcast(FP8X4),
@@ -308,9 +317,8 @@ def tile_list_plankton_tendency_kernel(
                     stop=True,
                 )
             for m in range(OUT_TILES):
-                nc.scalar.activation(result[:, m, :], acc[:, SLICE * m : SLICE * (m + 1)], ACT.Identity,
-                                     bias=drift_cols[:, m : m + 1])
-            nc.sync.dma_start(out[:, SLICE * j : SLICE * (j + 1)].rearrange("(m p) s -> p m s", p=P), result[:])
+                nc.scalar.activation(result[:, m, :], sums[m], ACT.Identity, bias=drift_cols[:, m : m + 1])
+            nc.sync.dma_start(out[:, lo : lo + width].rearrange("(m p) s -> p m s", p=P), result[:])
 
         growth = {}
         w3_raw = held("w3_raw", [P, PASSES, H], I32)
@@ -320,22 +328,27 @@ def tile_list_plankton_tendency_kernel(
         for t in range(TILES):
             nc.sync.dma_start(w4_raw[:, t, :], w4_rows[t])
 
-        round_w2(0)
-        w3_scale_rows = order_columns("w3_scale_rows", w3_scales_raw, U8)
-        saturate(0, 0)
-        round_w2(1)
-        quantise_w2(0, 0, H)
-        saturate(0, 1)
-        round_w2(2)
-        quantise_w2(1, 0, H)
-        for u in range(2):
-            growth[0, u] = bank(u)
-            for a in range(PASSES - 1):
+        def grow_early(u, passes):
+            for a in passes:
                 growth_pass(a, 0, u)
+
+        round_w2(0)
+        quantise_w2(0, 0, H)
+        saturate(0, 0)
+        growth[0, 0] = bank(0)
+        grow_early(0, (0,))
+        round_w2(1)
+        quantise_w2(1, 0, H)
+        grow_early(0, (1,))
+        saturate(0, 1)
+        growth[0, 1] = bank(1)
+        grow_early(1, (0, 1))
+        round_w2(2)
         for u in range(2):
             quantise_w2(2, 2 * P * u, 2 * P * (u + 1))
-            growth_pass(2, 0, u)
-        w3_codes = order_columns("w3_codes", w3_raw, U32)
+            grow_early(u, (2,))
+        w3_scale_rows = order_columns("w3_scale_rows", w3_scales_raw, U8)
+        w3_codes = order_columns("w3_codes", w3_raw, U32, engine=nc.vector)
 
         w4_bf = held("w4_bf", [P, TILES * N], BF16)
         for m in range(OUT_TILES):
@@ -348,45 +361,62 @@ def tile_list_plankton_tendency_kernel(
         growth_pair, loss_pair, out_pair = (0, 1, 2, 1), (0, 1, 0, 2), (0, 1, 0, 3)
         loss, h_bf = {}, {}
 
-        def grow(quarter):
-            for u in range(2):
-                growth[quarter, u] = bank(2 * growth_pair[quarter] + u)
-                for a in range(PASSES):
-                    growth_pass(a, quarter, u)
+        def grow(quarter, u):
+            growth[quarter, u] = bank(2 * growth_pair[quarter] + u)
+            for a in range(PASSES):
+                growth_pass(a, quarter, u)
 
-        def lose(quarter):
-            for u in range(2):
-                loss[2 * quarter + u] = mortality(2 * quarter + u, 2 * loss_pair[quarter] + u)
+        def lose(quarter, u):
+            loss[2 * quarter + u] = mortality(2 * quarter + u, 2 * loss_pair[quarter] + u)
 
-        def multiply(quarter):
+        def subtract(quarter):
+            h_bf[quarter] = ring.tile([P, TILES * QUARTER], BF16, name="h_bf", align_bytes=64)
             for u in range(2):
-                multiply_growth(quarter, u)
+                net_growth(h_bf[quarter][:, HALF * u : HALF * (u + 1)], loss[2 * quarter + u], quarter, u)
 
         def finish(quarter):
-            for u in range(2):
-                h_bf[u] = net_growth(loss[2 * quarter + u], 2 * quarter + u)
-            for u in range(2):
-                tendencies(h_bf[u], 2 * quarter + u, 2 * out_pair[quarter] + u)
+            pair = out_pair[quarter]
+            tendencies(h_bf[quarter][:], QUARTER * quarter, QUARTER, (2 * pair, 2 * pair + 1))
+
+        def finish_slice(quarter, u):
+            tendencies(h_bf[quarter][:, HALF * u : HALF * (u + 1)], QUARTER * quarter + SLICE * u, SLICE,
+                       (2 * out_pair[quarter] + u,))
 
         saturate(1, 0)
+        grow(1, 0)
+        multiply_growth(0, 0)
+        lose(0, 0)
         saturate(1, 1)
-        grow(1)
-        multiply(0)
-        lose(0)
+        grow(1, 1)
+        multiply_growth(0, 1)
+        lose(0, 1)
         quantise(w4_codes[:], w4_scales[:], w4_bf[:])
-        multiply(1)
-        lose(1)
-        finish(0)
+        multiply_growth(1, 0)
+        lose(1, 0)
+        subtract(0)
+        multiply_growth(1, 1)
+        lose(1, 1)
         saturate(2, 0)
+        grow(2, 0)
+        finish(0)
         saturate(2, 1)
-        grow(2)
-        lose(2)
+        grow(2, 1)
+        subtract(1)
+        for u in range(2):
+            lose(2, u)
+        multiply_growth(2, 0)
         finish(1)
-        grow(3)
-        multiply(2)
-        lose(3)
         saturate(3, 0)
+        lose(3, 0)
+        multiply_growth(2, 1)
+        for u in range(2):
+            grow(3, u)
         saturate(3, 1)
+        lose(3, 1)
+        subtract(2)
+        multiply_growth(3, 0)
         finish(2)
-        multiply(3)
-        finish(3)
+        multiply_growth(3, 1)
+        subtract(3)
+        for u in range(2):
+            finish_slice(3, u)

@@ -44,6 +44,7 @@ W2_LAST = TAB2 + STAGE + S + H + 2 * REACH
 TAB1 = W2_LAST + STAGE - REACH
 W2_BF = TAB1 + 2 * STAGE
 OFFSET = {
+    "w1_codes": W1_CODES,
     "scale_window": WINDOW,
     "v_words0": V_FIRST,
     "w2_raw0": W2_FIRST,
@@ -56,7 +57,8 @@ OFFSET = {
     "tab2": TAB2,
     "w1_raw": W2_LAST - 2 * REACH - 2 * W1_SCALES,
     "last_scales": TAB2 + STAGE,
-    "w1_scales_first": TAB2 + STAGE + S + H - W1_SCALES // 2 + 2 * REACH,
+    "w1_scales_first": TAB0 + 2 * REACH + 2 * WORDS,
+    "w3_scale_rows": W2_LAST,
     "w2_raw2": W2_LAST,
     "tab1": TAB1,
     "w4_raw": TAB1 + REACH,
@@ -98,7 +100,7 @@ def tile_list_plankton_tendency_kernel(
 
         scale_window = held("scale_window", [P, T], U8)
         w1_scales_raw = held("w1_scales_raw", [P, PASSES, H], U8)
-        w3_scales_raw = held("w3_scales_raw", [P, PASSES, H], U8)
+        w3_scales_raw = held("w3_scales_raw", [P, 1, H], U8)
         early_scales = held("early_scales", [P, 2, S], U8)
         last_scales = held("last_scales", [P, S], U8)
         nc.gpsimd.memset(w1_scales_raw[:].bitcast(I32), 0)
@@ -130,10 +132,10 @@ def tile_list_plankton_tendency_kernel(
         def quadrant_rows(scales, d):
             return scales.bitcast(I32)[:, 4 * d : 4 * d + 4, :]
 
-        def order_columns(name, raw, dtype, first=0, count=TILES, engine=nc.gpsimd):
+        def order_columns(name, raw, dtype, first=0, count=TILES):
             done = held(name, [P, raw.shape[1], raw.shape[2] * count // TILES], dtype)
             source = raw[:].bitcast(I32).rearrange("p a (q t w) -> p a t q w", t=TILES, q=RUNS)
-            engine.tensor_copy(
+            nc.vector.tensor_copy(
                 done[:].bitcast(I32).rearrange("p a (t q w) -> p a t q w", t=count, q=RUNS),
                 source[:, :, first : first + count],
             )
@@ -160,7 +162,7 @@ def tile_list_plankton_tendency_kernel(
 
         w1_codes = order_columns("w1_codes", w1_raw, U8)
         load_tab(2)
-        nc.gpsimd.memset(last_scales[:].bitcast(I32), 0)
+        nc.vector.memset(last_scales[:].bitcast(I32), 0)
         for d in range(QUADS):
             nc.scalar.dma_start(
                 last_scales[32 * d : 32 * d + 4, :].bitcast(I32),
@@ -204,11 +206,10 @@ def tile_list_plankton_tendency_kernel(
         w1_pair = {0: order_columns("w1_scales_first", w1_scales_raw, U8, 0, 2)}
         load_w2(0)
         load_w2(1)
-        nc.gpsimd.memset(w3_scales_raw[:].bitcast(I32), 0)
+        nc.vector.memset(w3_scales_raw[:].bitcast(I32), 0)
         for d in range(QUADS):
-            nc.sync.dma_start(
-                w3_scales_raw[32 * d : 32 * d + 4, :, :].bitcast(I32),
-                quadrant_rows(w3_scales, d).rearrange("a s n -> s a n"),
+            nc.scalar.dma_start(
+                w3_scales_raw[32 * d + 4 : 32 * d + 16, 0, :].bitcast(I32), quadrant_rows(w3_scales, d)
             )
         uptake = {(quarter, u): bank(2 * quarter + u) for quarter in range(4) for u in range(2)}
 
@@ -257,7 +258,7 @@ def tile_list_plankton_tendency_kernel(
                 for a in range(PASSES):
                     table_pass(acc[:, SLICE * t : SLICE * (t + 1)],
                                w3_codes[:, a, P * t : P * (t + 1)].bitcast(FP8X4),
-                               w3_scale_rows[:, a, P * t : P * (t + 1)], a, SLICE * j, SLICE,
+                               w3_scale_rows[4 * (a + 1) : P, 0, P * t : P * (t + 1)], a, SLICE * j, SLICE,
                                a == 0, a == PASSES - 1)
             return acc
 
@@ -348,15 +349,13 @@ def tile_list_plankton_tendency_kernel(
             quantise_w2(2, 2 * P * u, 2 * P * (u + 1))
             grow_early(u, (2,))
         w3_scale_rows = order_columns("w3_scale_rows", w3_scales_raw, U8)
-        w3_codes = order_columns("w3_codes", w3_raw, U32, engine=nc.vector)
+        w3_codes = order_columns("w3_codes", w3_raw, U32)
 
         w4_bf = held("w4_bf", [P, TILES * N], BF16)
-        for m in range(OUT_TILES):
-            nc.gpsimd.tensor_scalar(
-                w4_bf[:, TILES * P * m : TILES * P * (m + 1)].rearrange("p (c i t) -> p c t i", t=TILES, i=4),
-                w4_raw[:, :, P * m : P * (m + 1)].rearrange("p t (c i) -> p c t i", i=4),
-                1.0, 0.0, ALU.mult, ALU.add,
-            )
+        nc.scalar.copy(
+            w4_bf[:].rearrange("p (c i t) -> p c t i", t=TILES, i=4),
+            w4_raw[:].rearrange("p t (c i) -> p c t i", i=4),
+        )
 
         growth_pair, loss_pair, out_pair = (0, 1, 2, 1), (0, 1, 0, 2), (0, 1, 0, 3)
         loss, h_bf = {}, {}

@@ -42,7 +42,6 @@ W2_SECOND = TAB0 + STAGE - REACH
 TAB2 = W2_SECOND + STAGE + W1_SCALES // 2
 W2_LAST = TAB2 + STAGE + S + H + 2 * REACH
 TAB1 = W2_LAST + STAGE - REACH
-W2_BF = TAB1 + 2 * STAGE
 OFFSET = {
     "w1_codes": W1_CODES,
     "scale_window": WINDOW,
@@ -51,28 +50,16 @@ OFFSET = {
     "tab0": TAB0,
     "drift_cols": TAB0 + REACH,
     "v_words1": TAB0 + 2 * REACH,
-    "w3_scales_raw": TAB0 + 2 * REACH + 2 * WORDS + W1_SCALES // 2,
     "w2_raw1": W2_SECOND,
     "w1_scales_rest": TAB2 - W1_SCALES // 2 + REACH,
     "tab2": TAB2,
     "w1_raw": W2_LAST - 2 * REACH - 2 * W1_SCALES,
     "last_scales": TAB2 + STAGE,
     "w1_scales_first": TAB0 + 2 * REACH + 2 * WORDS,
-    "w3_scale_rows": W2_LAST,
+    "w3_scale_rows": W2_FIRST,
     "w2_raw2": W2_LAST,
     "tab1": TAB1,
     "w4_raw": TAB1 + REACH,
-    "w2_bf0": W2_BF,
-    "saturated0_0": W2_BF,
-    "saturated1_1": W2_BF,
-    "saturated2_1": W2_BF,
-    "saturated3_1": W2_BF,
-    "w2_bf1": W2_BF + 8 * H,
-    "saturated0_1": W2_BF + 8 * H,
-    "w2_bf2": W2_BF + 16 * H,
-    "saturated1_0": W2_BF + 16 * H,
-    "saturated2_0": W2_BF + 16 * H,
-    "saturated3_0": W2_BF + 16 * H,
     "w3_raw": TAB1 + STAGE - REACH,
 }
 
@@ -105,6 +92,7 @@ def tile_list_plankton_tendency_kernel(
         last_scales = held("last_scales", [P, S], U8)
         nc.gpsimd.memset(w1_scales_raw[:].bitcast(I32), 0)
         nc.vector.memset(early_scales[:].bitcast(I32), 0)
+        nc.vector.memset(w3_scales_raw[:].bitcast(I32), 0)
         warm_in = held("warm_in", [P, 16], F32)
         warm_out = held("warm_out", [P, 16], F32)
         nc.vector.memset(warm_in[:], 1.0)
@@ -114,7 +102,7 @@ def tile_list_plankton_tendency_kernel(
         nc.sync.dma_start(scale_window[0:P:4, :].bitcast(I32), scale_words[0:2].rearrange("a q n -> q a n"))
         nc.sync.dma_start(scale_window[2:P:4, :].bitcast(I32), scale_words[1:3].rearrange("a q n -> q a n"))
         nc.sync.dma_start(scale_window[1:P:4, :].bitcast(I32), scale_words[0:2].rearrange("a q n -> q a n"))
-        nc.scalar.dma_start(scale_window[3:P:4, :].bitcast(I32), scale_words[1:3].rearrange("a q n -> q a n"))
+        nc.sync.dma_start(scale_window[3:P:4, :].bitcast(I32), scale_words[1:3].rearrange("a q n -> q a n"))
 
         tab = {}
 
@@ -147,7 +135,7 @@ def tile_list_plankton_tendency_kernel(
         load_tab(1)
 
         for d in range(QUADS):
-            (nc.gpsimd if d else nc.scalar).dma_start(
+            nc.gpsimd.dma_start(
                 w1_scales_raw[32 * d : 32 * d + 4, :, :].bitcast(I32),
                 quadrant_rows(w1_scales, d).rearrange("a s n -> s a n"),
             )
@@ -167,6 +155,10 @@ def tile_list_plankton_tendency_kernel(
             nc.scalar.dma_start(
                 last_scales[32 * d : 32 * d + 4, :].bitcast(I32),
                 gathered_scales[32 * d + 6 : 32 * d + 32 : 8, :].bitcast(I32),
+            )
+        for d in range(QUADS):
+            nc.gpsimd.dma_start(
+                w3_scales_raw[32 * d + 4 : 32 * d + 16, 0, :].bitcast(I32), quadrant_rows(w3_scales, d)
             )
         drift_cols = held("drift_cols", [P, OUT_TILES], F32)
         with nc.allow_non_contiguous_dma(reason="one drift value for each partition and tile of out"):
@@ -206,11 +198,6 @@ def tile_list_plankton_tendency_kernel(
         w1_pair = {0: order_columns("w1_scales_first", w1_scales_raw, U8, 0, 2)}
         load_w2(0)
         load_w2(1)
-        nc.vector.memset(w3_scales_raw[:].bitcast(I32), 0)
-        for d in range(QUADS):
-            nc.scalar.dma_start(
-                w3_scales_raw[32 * d + 4 : 32 * d + 16, 0, :].bitcast(I32), quadrant_rows(w3_scales, d)
-            )
         uptake = {(quarter, u): bank(2 * quarter + u) for quarter in range(4) for u in range(2)}
 
         def w1_scale_tile(a, t):
@@ -274,7 +261,7 @@ def tile_list_plankton_tendency_kernel(
             acc = uptake[half, t]
             magnitude = ring.tile([P, HALF], F32, name="magnitude")
             root = ring.tile([P, HALF], F32, name="root")
-            inverse = ring.tile([P, HALF], F32, name="inverse")
+            inverse = ring.tile([P, HALF], F32, name="inverse", bufs=4)
             nc.scalar.activation(woven(magnitude[:]), weave(acc, 2), ACT.Abs)
             nc.scalar.activation(root[:], magnitude[:], ACT.Abs_reciprocal_sqrt, bias=1.0)
             nc.scalar.activation(inverse[:], root[:], ACT.Square)
@@ -298,12 +285,12 @@ def tile_list_plankton_tendency_kernel(
         w4_codes = held("w4_codes", [P, N], U32)
         w4_scales = held("w4_scales", [P, N], U8)
 
-        def tendencies(h_bf, lo, width, banks):
+        def tendencies(h_bf, lo, width, banks, on_vector=False):
             h_codes = ring.tile([P, width], U32, name="h_codes", align_bytes=64)
             h_scales = ring.tile([P, width], U8, name="h_scales", align_bytes=64)
             quantise(h_codes[:], h_scales[:], h_bf)
             accs = [bank(number) for number in banks]
-            result = ring.tile([P, OUT_TILES, width], F32, name="result", bufs=3)
+            result = ring.tile([P, OUT_TILES, width], F32, name="result", bufs=4)
             sums = []
             for m in range(OUT_TILES):
                 which, at = divmod(width * m, HALF)
@@ -317,8 +304,16 @@ def tile_list_plankton_tendency_kernel(
                     start=True,
                     stop=True,
                 )
-            for m in range(OUT_TILES):
-                nc.scalar.activation(result[:, m, :], sums[m], ACT.Identity, bias=drift_cols[:, m : m + 1])
+            if on_vector:
+                nc.vector.tensor_tensor(
+                    result[:],
+                    accs[0][:, 0 : OUT_TILES * width].rearrange("p (m c) -> p m c", m=OUT_TILES),
+                    drift_cols[:].unsqueeze(2).to_broadcast([P, OUT_TILES, width]),
+                    ALU.add,
+                )
+            else:
+                for m in range(OUT_TILES):
+                    nc.scalar.activation(result[:, m, :], sums[m], ACT.Identity, bias=drift_cols[:, m : m + 1])
             nc.sync.dma_start(out[:, lo : lo + width].rearrange("(m p) s -> p m s", p=P), result[:])
 
         growth = {}
@@ -334,6 +329,7 @@ def tile_list_plankton_tendency_kernel(
                 growth_pass(a, 0, u)
 
         round_w2(0)
+        w3_scale_rows = order_columns("w3_scale_rows", w3_scales_raw, U8)
         quantise_w2(0, 0, H)
         saturate(0, 0)
         growth[0, 0] = bank(0)
@@ -348,16 +344,17 @@ def tile_list_plankton_tendency_kernel(
         for u in range(2):
             quantise_w2(2, 2 * P * u, 2 * P * (u + 1))
             grow_early(u, (2,))
-        w3_scale_rows = order_columns("w3_scale_rows", w3_scales_raw, U8)
         w3_codes = order_columns("w3_codes", w3_raw, U32)
 
         w4_bf = held("w4_bf", [P, TILES * N], BF16)
-        nc.scalar.copy(
-            w4_bf[:].rearrange("p (c i t) -> p c t i", t=TILES, i=4),
-            w4_raw[:].rearrange("p t (c i) -> p c t i", i=4),
-        )
+        for m in range(OUT_TILES):
+            nc.gpsimd.tensor_scalar(
+                w4_bf[:, TILES * P * m : TILES * P * (m + 1)].rearrange("p (c i t) -> p c t i", t=TILES, i=4),
+                w4_raw[:, :, P * m : P * (m + 1)].rearrange("p t (c i) -> p c t i", i=4),
+                1.0, 0.0, ALU.mult, ALU.add,
+            )
 
-        growth_pair, loss_pair, out_pair = (0, 1, 2, 1), (0, 1, 0, 2), (0, 1, 0, 3)
+        growth_pair, loss_pair, out_pair = (0, 1, 2, 3), (0, 1, 2, 0), (0, 1, 2, 1)
         loss, h_bf = {}, {}
 
         def grow(quarter, u):
@@ -379,43 +376,37 @@ def tile_list_plankton_tendency_kernel(
 
         def finish_slice(quarter, u):
             tendencies(h_bf[quarter][:, HALF * u : HALF * (u + 1)], QUARTER * quarter + SLICE * u, SLICE,
-                       (2 * out_pair[quarter] + u,))
+                       (2 * out_pair[quarter] + u,), True)
 
-        saturate(1, 0)
-        grow(1, 0)
-        multiply_growth(0, 0)
-        lose(0, 0)
-        saturate(1, 1)
-        grow(1, 1)
-        multiply_growth(0, 1)
-        lose(0, 1)
-        quantise(w4_codes[:], w4_scales[:], w4_bf[:])
+        for u in range(2):
+            saturate(1, u)
+            grow(1, u)
+        for u in range(2):
+            multiply_growth(0, u)
+            lose(0, u)
+            saturate(2, u)
+            grow(2, u)
         multiply_growth(1, 0)
         lose(1, 0)
         subtract(0)
+        quantise(w4_codes[:], w4_scales[:], w4_bf[:])
         multiply_growth(1, 1)
         lose(1, 1)
-        saturate(2, 0)
-        grow(2, 0)
         finish(0)
-        saturate(2, 1)
-        grow(2, 1)
-        subtract(1)
         for u in range(2):
-            lose(2, u)
-        multiply_growth(2, 0)
-        finish(1)
-        saturate(3, 0)
-        lose(3, 0)
-        multiply_growth(2, 1)
-        for u in range(2):
+            saturate(3, u)
             grow(3, u)
-        saturate(3, 1)
-        lose(3, 1)
+        subtract(1)
+        multiply_growth(2, 0)
+        lose(2, 0)
+        finish(1)
+        multiply_growth(2, 1)
+        lose(2, 1)
+        for u in range(2):
+            lose(3, u)
+            multiply_growth(3, u)
         subtract(2)
-        multiply_growth(3, 0)
         finish(2)
-        multiply_growth(3, 1)
         subtract(3)
         for u in range(2):
             finish_slice(3, u)

@@ -36,26 +36,26 @@ W1_SCALES = PASSES * H
 W1_CODES = 0
 WINDOW = W1_CODES + 2 * W1_SCALES - REACH
 V_FIRST = WINDOW + REACH
-W2_FIRST = V_FIRST + 2 * WORDS
-TAB0 = W2_FIRST + STAGE - REACH
+TAB0 = V_FIRST + 2 * WORDS
 W2_SECOND = TAB0 + STAGE - REACH
 TAB2 = W2_SECOND + STAGE + W1_SCALES // 2
-W2_LAST = TAB2 + STAGE + S + H + 2 * REACH
+W2_FIRST = TAB2 + STAGE + S
+W2_LAST = W2_FIRST + STAGE
 TAB1 = W2_LAST + STAGE - REACH
 OFFSET = {
     "w1_codes": W1_CODES,
     "scale_window": WINDOW,
     "v_words0": V_FIRST,
-    "w2_raw0": W2_FIRST,
     "tab0": TAB0,
-    "drift_cols": TAB0 + REACH,
-    "v_words1": TAB0 + 2 * REACH,
+    "drift_cols": TAB0,
+    "v_words1": TAB0 + REACH,
+    "w1_scales_first": TAB0 + REACH + 2 * WORDS,
     "w2_raw1": W2_SECOND,
     "w1_scales_rest": TAB2 - W1_SCALES // 2 + REACH,
     "tab2": TAB2,
-    "w1_raw": W2_LAST - 2 * REACH - 2 * W1_SCALES,
+    "w1_raw": W2_FIRST - 2 * S,
     "last_scales": TAB2 + STAGE,
-    "w1_scales_first": TAB0 + 2 * REACH + 2 * WORDS,
+    "w2_raw0": W2_FIRST,
     "w3_scale_rows": W2_FIRST,
     "w2_raw2": W2_LAST,
     "tab1": TAB1,
@@ -150,6 +150,7 @@ def tile_list_plankton_tendency_kernel(
 
         w1_codes = order_columns("w1_codes", w1_raw, U8)
         load_tab(2)
+        load_w2(0)
         nc.vector.memset(last_scales[:].bitcast(I32), 0)
         for d in range(QUADS):
             nc.scalar.dma_start(
@@ -160,9 +161,6 @@ def tile_list_plankton_tendency_kernel(
             nc.gpsimd.dma_start(
                 w3_scales_raw[32 * d + 4 : 32 * d + 16, 0, :].bitcast(I32), quadrant_rows(w3_scales, d)
             )
-        drift_cols = held("drift_cols", [P, OUT_TILES], F32)
-        with nc.allow_non_contiguous_dma(reason="one drift value for each partition and tile of out"):
-            nc.sync.dma_start(drift_cols[:], drift.rearrange("(m p) -> p m", p=P))
 
         v_words = [held(f"v_words{a}", [P, S], U32) for a in range(PASSES)]
 
@@ -196,8 +194,10 @@ def tile_list_plankton_tendency_kernel(
 
         gather_words(0, 0, S)
         w1_pair = {0: order_columns("w1_scales_first", w1_scales_raw, U8, 0, 2)}
-        load_w2(0)
         load_w2(1)
+        drift_cols = held("drift_cols", [P, OUT_TILES], F32)
+        with nc.allow_non_contiguous_dma(reason="one drift value for each partition and tile of out"):
+            nc.sync.dma_start(drift_cols[:], drift.rearrange("(m p) -> p m", p=P))
         uptake = {(quarter, u): bank(2 * quarter + u) for quarter in range(4) for u in range(2)}
 
         def w1_scale_tile(a, t):
@@ -219,16 +219,20 @@ def tile_list_plankton_tendency_kernel(
         load_w2(2)
         w2_codes = [held(f"w2_codes{a}", [P, H], U32) for a in range(PASSES)]
         w2_scales = [held(f"w2_scales{a}", [P, H], U8) for a in range(PASSES)]
-        w2_bf = [held(f"w2_bf{a}", [P, PACK * H], BF16) for a in range(PASSES)]
+        w2_bf = {(a, u): held(f"w2_bf{a}_{u}", [P, PACK * 2 * P], BF16) for a in range(PASSES) for u in range(2)}
 
-        def round_w2(a):
-            rounded = w2_bf[a][:].rearrange("p (t q i j) -> p t q j i", t=TILES, q=RUNS, j=PACK)
-            source = w2_raw[a][:].rearrange("p j (q t i) -> p t q j i", t=TILES, q=RUNS)
-            for u in range(2):
-                nc.vector.tensor_copy(rounded[:, 2 * u : 2 * u + 2], source[:, 2 * u : 2 * u + 2])
+        def round_w2(a, u):
+            rounded = w2_bf[a, u][:].rearrange("p (t q i j) -> p t q j i", t=2, q=RUNS, j=PACK)
+            source = w2_raw[a][:].rearrange("p j (q t i) -> p t q j i", t=TILES, q=RUNS)[:, 2 * u : 2 * u + 2]
+            if u == 0 or a == PASSES - 1:
+                nc.vector.tensor_copy(rounded, source)
+            else:
+                for e in range(2):
+                    nc.gpsimd.tensor_scalar(rounded[:, e], source[:, e], 1.0, 0.0, ALU.mult, ALU.add)
 
-        def quantise_w2(a, lo, hi):
-            quantise(w2_codes[a][:, lo:hi], w2_scales[a][:, lo:hi], w2_bf[a][:, PACK * lo : PACK * hi])
+        def quantise_w2(a, u):
+            columns = slice(2 * P * u, 2 * P * (u + 1))
+            quantise(w2_codes[a][:, columns], w2_scales[a][:, columns], w2_bf[a, u][:])
 
         def w2_tile(a, t):
             return w2_codes[a][:, P * t : P * (t + 1)].bitcast(FP8X4)
@@ -328,22 +332,28 @@ def tile_list_plankton_tendency_kernel(
             for a in passes:
                 growth_pass(a, 0, u)
 
-        round_w2(0)
+        for a in range(PASSES - 1):
+            round_w2(a, 1)
+        round_w2(0, 0)
         w3_scale_rows = order_columns("w3_scale_rows", w3_scales_raw, U8)
-        quantise_w2(0, 0, H)
+        quantise_w2(0, 0)
         saturate(0, 0)
         growth[0, 0] = bank(0)
         grow_early(0, (0,))
-        round_w2(1)
-        quantise_w2(1, 0, H)
+        round_w2(1, 0)
+        quantise_w2(0, 1)
+        quantise_w2(1, 0)
         grow_early(0, (1,))
         saturate(0, 1)
         growth[0, 1] = bank(1)
-        grow_early(1, (0, 1))
-        round_w2(2)
-        for u in range(2):
-            quantise_w2(2, 2 * P * u, 2 * P * (u + 1))
-            grow_early(u, (2,))
+        grow_early(1, (0,))
+        round_w2(2, 0)
+        round_w2(2, 1)
+        quantise_w2(2, 0)
+        grow_early(0, (2,))
+        quantise_w2(1, 1)
+        quantise_w2(2, 1)
+        grow_early(1, (1, 2))
         w3_codes = order_columns("w3_codes", w3_raw, U32)
 
         w4_bf = held("w4_bf", [P, TILES * N], BF16)
@@ -376,7 +386,7 @@ def tile_list_plankton_tendency_kernel(
 
         def finish_slice(quarter, u):
             tendencies(h_bf[quarter][:, HALF * u : HALF * (u + 1)], QUARTER * quarter + SLICE * u, SLICE,
-                       (2 * out_pair[quarter] + u,), True)
+                       (2 * out_pair[quarter] + u,), u == 1)
 
         for u in range(2):
             saturate(1, u)

@@ -30,6 +30,7 @@ OUT_TILES = N // P
 STAGE = 4 * T
 
 W2_ORDER = (0, 1, 2)
+LATE = 3
 REACH = 128
 WORDS = 4 * HALF
 W1_SCALES = PASSES * H
@@ -267,10 +268,16 @@ def tile_list_plankton_tendency_kernel(
             root = ring.tile([P, HALF], F32, name="root")
             inverse = ring.tile([P, HALF], F32, name="inverse", bufs=4)
             nc.scalar.activation(woven(magnitude[:]), weave(acc, 2), ACT.Abs)
+            if half >= LATE:
+                drive = ring.tile([P, HALF], F32, name="drive", bufs=4)
+                nc.scalar.copy(woven(drive[:]), weave(acc, 2))
             nc.scalar.activation(root[:], magnitude[:], ACT.Abs_reciprocal_sqrt, bias=1.0)
             nc.scalar.activation(inverse[:], root[:], ACT.Square)
             saturated[half, t] = held(f"saturated{half}_{t}", [P, HALF], F32)
-            nc.vector.tensor_tensor(woven(saturated[half, t][:]), weave(acc, 2), woven(inverse[:]), ALU.mult)
+            if half >= LATE:
+                nc.gpsimd.tensor_tensor(saturated[half, t][:], drive[:], inverse[:], ALU.mult)
+            else:
+                nc.vector.tensor_tensor(woven(saturated[half, t][:]), weave(acc, 2), woven(inverse[:]), ALU.mult)
 
         gain = [held(f"gain{quarter}", [P, 2, 2 * QUARTER], F32) for quarter in range(4)]
 
@@ -396,25 +403,25 @@ def tile_list_plankton_tendency_kernel(
             lose(0, u)
             saturate(2, u)
             grow(2, u)
-        multiply_growth(1, 0)
-        lose(1, 0)
+        for u in range(2):
+            multiply_growth(1, u)
+            lose(1, u)
         subtract(0)
         quantise(w4_codes[:], w4_scales[:], w4_bf[:])
-        multiply_growth(1, 1)
-        lose(1, 1)
+        multiply_growth(2, 0)
         finish(0)
+        lose(2, 0)
+        multiply_growth(2, 1)
+        lose(2, 1)
         for u in range(2):
             saturate(3, u)
             grow(3, u)
         subtract(1)
-        multiply_growth(2, 0)
-        lose(2, 0)
+        multiply_growth(3, 0)
         finish(1)
-        multiply_growth(2, 1)
-        lose(2, 1)
         for u in range(2):
             lose(3, u)
-            multiply_growth(3, u)
+        multiply_growth(3, 1)
         subtract(2)
         finish(2)
         subtract(3)

@@ -30,7 +30,7 @@ OUT_TILES = N // P
 STAGE = 4 * T
 
 W2_ORDER = (0, 1, 2)
-LATE = 3
+COPIED = ((1, 1), (2, 0), (2, 1))
 REACH = 128
 WORDS = 4 * HALF
 W1_SCALES = PASSES * H
@@ -61,6 +61,8 @@ OFFSET = {
     "w2_raw2": W2_LAST,
     "tab1": TAB1,
     "w4_raw": TAB1 + REACH,
+    "saturated2_0": TAB1 + REACH,
+    "saturated2_1": TAB1 + REACH + WORDS,
     "w3_raw": TAB1 + STAGE - REACH,
 }
 
@@ -206,11 +208,11 @@ def tile_list_plankton_tendency_kernel(
 
         for a in range(PASSES):
             for half in range(2):
-                if a == 2:
+                if a > 0 and (a, half) != (2, 0):
                     gather_words(a, HALF * half, HALF * (half + 1))
-                elif a == 1 and half == 0:
-                    gather_words(a, 0, S)
                 for quarter in (2 * half, 2 * half + 1):
+                    if (a, half) == (2, 0):
+                        gather_words(a, QUARTER * quarter, QUARTER * (quarter + 1))
                     pair_pass(uptake[quarter, 0], w1_tile, w1_scale_tile, a, quarter, 0)
         w1_pair[1] = order_columns("w1_scales_rest", w1_scales_raw, U8, 2, 2)
         for quarter in range(4):
@@ -268,13 +270,13 @@ def tile_list_plankton_tendency_kernel(
             root = ring.tile([P, HALF], F32, name="root")
             inverse = ring.tile([P, HALF], F32, name="inverse", bufs=4)
             nc.scalar.activation(woven(magnitude[:]), weave(acc, 2), ACT.Abs)
-            if half >= LATE:
+            if (half, t) in COPIED:
                 drive = ring.tile([P, HALF], F32, name="drive", bufs=4)
                 nc.scalar.copy(woven(drive[:]), weave(acc, 2))
             nc.scalar.activation(root[:], magnitude[:], ACT.Abs_reciprocal_sqrt, bias=1.0)
             nc.scalar.activation(inverse[:], root[:], ACT.Square)
             saturated[half, t] = held(f"saturated{half}_{t}", [P, HALF], F32)
-            if half >= LATE:
+            if (half, t) in COPIED:
                 nc.gpsimd.tensor_tensor(saturated[half, t][:], drive[:], inverse[:], ALU.mult)
             else:
                 nc.vector.tensor_tensor(woven(saturated[half, t][:]), weave(acc, 2), woven(inverse[:]), ALU.mult)
@@ -335,9 +337,9 @@ def tile_list_plankton_tendency_kernel(
         for t in range(TILES):
             nc.sync.dma_start(w4_raw[:, t, :], w4_rows[t])
 
-        def grow_early(u, passes):
+        def grow_early(quarter, u, passes):
             for a in passes:
-                growth_pass(a, 0, u)
+                growth_pass(a, quarter, u)
 
         for a in range(PASSES - 1):
             round_w2(a, 1)
@@ -346,21 +348,19 @@ def tile_list_plankton_tendency_kernel(
         quantise_w2(0, 0)
         saturate(0, 0)
         growth[0, 0] = bank(0)
-        grow_early(0, (0,))
+        grow_early(0, 0, (0,))
         round_w2(1, 0)
         quantise_w2(0, 1)
         quantise_w2(1, 0)
-        grow_early(0, (1,))
-        saturate(0, 1)
-        growth[0, 1] = bank(1)
-        grow_early(1, (0,))
+        grow_early(0, 0, (1,))
+        saturate(1, 0)
+        growth[1, 0] = bank(2)
+        grow_early(1, 0, (0, 1))
         round_w2(2, 0)
         round_w2(2, 1)
         quantise_w2(2, 0)
-        grow_early(0, (2,))
-        quantise_w2(1, 1)
-        quantise_w2(2, 1)
-        grow_early(1, (1, 2))
+        grow_early(0, 0, (2,))
+        grow_early(1, 0, (2,))
         w3_codes = order_columns("w3_codes", w3_raw, U32)
 
         w4_bf = held("w4_bf", [P, TILES * N], BF16)
@@ -395,27 +395,31 @@ def tile_list_plankton_tendency_kernel(
             tendencies(h_bf[quarter][:, HALF * u : HALF * (u + 1)], QUARTER * quarter + SLICE * u, SLICE,
                        (2 * out_pair[quarter] + u,), u == 1)
 
-        for u in range(2):
-            saturate(1, u)
-            grow(1, u)
-        for u in range(2):
-            multiply_growth(0, u)
-            lose(0, u)
-            saturate(2, u)
-            grow(2, u)
-        for u in range(2):
-            multiply_growth(1, u)
-            lose(1, u)
+        for quarter in range(2):
+            multiply_growth(quarter, 0)
+            lose(quarter, 0)
+        saturate(0, 1)
+        quantise_w2(1, 1)
+        quantise_w2(2, 1)
+        grow(0, 1)
+        saturate(1, 1)
+        grow(1, 1)
+        for quarter in range(2):
+            multiply_growth(quarter, 1)
+            lose(quarter, 1)
+            saturate(2, quarter)
+            grow(2, quarter)
         subtract(0)
         quantise(w4_codes[:], w4_scales[:], w4_bf[:])
-        multiply_growth(2, 0)
+        saturate(3, 0)
+        grow(3, 0)
         finish(0)
+        multiply_growth(2, 0)
         lose(2, 0)
+        saturate(3, 1)
+        grow(3, 1)
         multiply_growth(2, 1)
         lose(2, 1)
-        for u in range(2):
-            saturate(3, u)
-            grow(3, u)
         subtract(1)
         multiply_growth(3, 0)
         finish(1)

@@ -43,6 +43,7 @@ TAB2 = W2_SECOND + STAGE + W1_SCALES // 2
 W2_FIRST = TAB2 + STAGE + S
 W2_LAST = W2_FIRST + STAGE
 TAB1 = W2_LAST + STAGE - REACH
+W2_BF = TAB1 + 2 * STAGE
 OFFSET = {
     "w1_codes": W1_CODES,
     "scale_window": WINDOW,
@@ -64,6 +65,9 @@ OFFSET = {
     "saturated2_0": TAB1 + REACH,
     "saturated2_1": TAB1 + REACH + WORDS,
     "w3_raw": TAB1 + STAGE - REACH,
+    "saturated1_1": W2_BF,
+    "w2_bf2_1": W2_BF + WORDS - REACH,
+    "w4_bf": W2_BF + WORDS,
 }
 
 

@@ -27,47 +27,46 @@ QUARTER = 256
 SLICE = 128
 TILES = H // P
 OUT_TILES = N // P
+UNITS = 8
 STAGE = 4 * T
 
-W2_ORDER = (0, 1, 2)
-COPIED = ((1, 1), (2, 0), (2, 1))
+COPIED = (3, 4, 5, 6, 7)
 REACH = 128
-WORDS = 4 * HALF
-W1_SCALES = PASSES * H
-W1_CODES = 0
-WINDOW = W1_CODES + 2 * W1_SCALES - REACH
-V_FIRST = WINDOW + REACH
-TAB0 = V_FIRST + 2 * WORDS
+W1_BYTES = PASSES * 2 * H
+WINDOW = W1_BYTES - REACH
+TAB0 = W1_BYTES + 4 * S
 W2_SECOND = TAB0 + STAGE - REACH
-TAB2 = W2_SECOND + STAGE + W1_SCALES // 2
-W2_FIRST = TAB2 + STAGE + S
-W2_LAST = W2_FIRST + STAGE
-TAB1 = W2_LAST + STAGE - REACH
-W2_BF = TAB1 + 2 * STAGE
+TAB2 = W2_SECOND + STAGE
+W1_RAW = TAB2 + STAGE - REACH
+W2_FIRST = W1_RAW + W1_BYTES - REACH
+TAB1 = W2_FIRST + STAGE
+W2_LAST = TAB1 + STAGE - REACH
 OFFSET = {
-    "w1_codes": W1_CODES,
+    "w1_codes": 0,
     "scale_window": WINDOW,
-    "v_words0": V_FIRST,
+    "v_words0": W1_BYTES,
     "tab0": TAB0,
     "drift_cols": TAB0,
     "v_words1": TAB0 + REACH,
-    "w1_scales_first": TAB0 + REACH + 2 * WORDS,
     "w2_raw1": W2_SECOND,
-    "w1_scales_rest": TAB2 - W1_SCALES // 2 + REACH,
     "tab2": TAB2,
-    "w1_raw": W2_FIRST - 2 * S,
-    "last_scales": TAB2 + STAGE,
+    "w4_raw": TAB2 + REACH,
+    "saturated4": TAB2 + REACH,
+    "saturated5": TAB2 + REACH + 4 * HALF,
+    "w2_codes0_1": W2_LAST + REACH,
+    "w2_codes1_1": W2_LAST + REACH + 8 * P,
+    "saturated2": TAB1,
+    "saturated3": W2_LAST + STAGE,
+    "w4_codes": W2_LAST + STAGE,
+    "w1_raw": W1_RAW,
+    "last_scales": W1_RAW + REACH,
+    "w1_scale_rows": W1_RAW + REACH + S,
+    "w2_bf0_0": W2_LAST + 2 * STAGE,
+    "w3_scale_rows": W2_LAST + 2 * STAGE,
     "w2_raw0": W2_FIRST,
-    "w3_scale_rows": W2_FIRST,
-    "w2_raw2": W2_LAST,
     "tab1": TAB1,
-    "w4_raw": TAB1 + REACH,
-    "saturated2_0": TAB1 + REACH,
-    "saturated2_1": TAB1 + REACH + WORDS,
-    "w3_raw": TAB1 + STAGE - REACH,
-    "saturated1_1": W2_BF,
-    "w2_bf2_1": W2_BF + WORDS - REACH,
-    "w4_bf": W2_BF + WORDS,
+    "w3_raw": TAB1,
+    "w2_raw2": W2_LAST,
 }
 
 
@@ -92,24 +91,25 @@ def tile_list_plankton_tendency_kernel(
         offsets = keep.tile([P, S // 16], U16, name="offsets")
         nc.sync.dma_start(offsets[:], offs)
 
-        scale_window = held("scale_window", [P, T], U8)
-        w1_scales_raw = held("w1_scales_raw", [P, PASSES, H], U8)
-        w3_scales_raw = held("w3_scales_raw", [P, 1, H], U8)
-        early_scales = held("early_scales", [P, 2, S], U8)
-        last_scales = held("last_scales", [P, S], U8)
-        nc.gpsimd.memset(w1_scales_raw[:].bitcast(I32), 0)
-        nc.vector.memset(early_scales[:].bitcast(I32), 0)
-        nc.vector.memset(w3_scales_raw[:].bitcast(I32), 0)
         warm_in = held("warm_in", [P, 16], F32)
         warm_out = held("warm_out", [P, 16], F32)
         nc.vector.memset(warm_in[:], 1.0)
         nc.scalar.activation(warm_out[:], warm_in[:], ACT.Abs_reciprocal_sqrt)
 
+        scale_window = held("scale_window", [P, T], U8)
+        w1_scales_raw = held("w1_scales_raw", [P, PASSES, H], U8)
+        w3_scales_raw = held("w3_scales_raw", [P, 1, H], U8)
+        early_scales = held("early_scales", [P, 2, S], U8)
+        nc.vector.memset(w1_scales_raw[:].bitcast(I32), 0)
+        nc.vector.memset(early_scales[:].bitcast(I32), 0)
+        nc.vector.memset(w3_scales_raw[:].bitcast(I32), 0)
+
         scale_words = tab_scales.bitcast(I32)
-        nc.sync.dma_start(scale_window[0:P:4, :].bitcast(I32), scale_words[0:2].rearrange("a q n -> q a n"))
-        nc.sync.dma_start(scale_window[2:P:4, :].bitcast(I32), scale_words[1:3].rearrange("a q n -> q a n"))
-        nc.sync.dma_start(scale_window[1:P:4, :].bitcast(I32), scale_words[0:2].rearrange("a q n -> q a n"))
-        nc.sync.dma_start(scale_window[3:P:4, :].bitcast(I32), scale_words[1:3].rearrange("a q n -> q a n"))
+        for x in range(4):
+            first = x // 2
+            nc.sync.dma_start(
+                scale_window[x:P:4, :].bitcast(I32), scale_words[first : first + 2].rearrange("a q n -> q a n")
+            )
 
         tab = {}
 
@@ -127,13 +127,15 @@ def tile_list_plankton_tendency_kernel(
         def quadrant_rows(scales, d):
             return scales.bitcast(I32)[:, 4 * d : 4 * d + 4, :]
 
-        def order_columns(name, raw, dtype, first=0, count=TILES):
-            done = held(name, [P, raw.shape[1], raw.shape[2] * count // TILES], dtype)
-            source = raw[:].bitcast(I32).rearrange("p a (q t w) -> p a t q w", t=TILES, q=RUNS)
-            nc.vector.tensor_copy(
-                done[:].bitcast(I32).rearrange("p a (t q w) -> p a t q w", t=count, q=RUNS),
-                source[:, :, first : first + count],
-            )
+        def order_columns(name, raw, dtype, on_scalar=False):
+            done = held(name, list(raw.shape), dtype)
+            word = U32 if on_scalar else I32
+            source = raw[:].bitcast(word).rearrange("p a (q t w) -> p t a q w", t=TILES, q=RUNS)
+            target = done[:].bitcast(word).rearrange("p a (t q w) -> p t a q w", t=TILES, q=RUNS)
+            if on_scalar:
+                nc.scalar.copy(target, source)
+            else:
+                nc.vector.tensor_copy(target, source)
             return done
 
         w1_raw = held("w1_raw", [P, PASSES, 2 * H], U8)
@@ -142,9 +144,14 @@ def tile_list_plankton_tendency_kernel(
         load_tab(1)
 
         for d in range(QUADS):
-            nc.gpsimd.dma_start(
+            queue = nc.gpsimd if d < 2 else nc.scalar
+            queue.dma_start(
                 w1_scales_raw[32 * d : 32 * d + 4, :, :].bitcast(I32),
                 quadrant_rows(w1_scales, d).rearrange("a s n -> s a n"),
+            )
+        for d in range(QUADS):
+            nc.gpsimd.dma_start(
+                w3_scales_raw[32 * d + 4 : 32 * d + 16, 0, :].bitcast(I32), quadrant_rows(w3_scales, d)
             )
 
         gathered_scales = held("gathered_scales", [P, S], U8)
@@ -158,22 +165,36 @@ def tile_list_plankton_tendency_kernel(
         w1_codes = order_columns("w1_codes", w1_raw, U8)
         load_tab(2)
         load_w2(0)
-        nc.vector.memset(last_scales[:].bitcast(I32), 0)
+        last_scales = held("last_scales", [P, S], U8)
         for d in range(QUADS):
             nc.scalar.dma_start(
                 last_scales[32 * d : 32 * d + 4, :].bitcast(I32),
                 gathered_scales[32 * d + 6 : 32 * d + 32 : 8, :].bitcast(I32),
             )
-        for d in range(QUADS):
-            nc.gpsimd.dma_start(
-                w3_scales_raw[32 * d + 4 : 32 * d + 16, 0, :].bitcast(I32), quadrant_rows(w3_scales, d)
-            )
+        w1_scale_rows = order_columns("w1_scale_rows", w1_scales_raw, U8, True)
 
         v_words = [held(f"v_words{a}", [P, S], U32) for a in range(PASSES)]
 
         def gather_words(a, lo, hi):
             entries = offsets[:, lo // 16 : hi // 16]
             nc.vector.tensor_copy(v_words[a][:, lo:hi], tab[a][:].bitcast(U32).indirect(entries))
+
+        gather_words(0, 0, S)
+        load_w2(1)
+        drift_cols = held("drift_cols", [P, OUT_TILES], F32)
+        with nc.allow_non_contiguous_dma(reason="one drift value for each partition and tile of out"):
+            nc.sync.dma_start(drift_cols[:], drift.rearrange("(m p) -> p m", p=P))
+        gather_words(1, 0, HALF)
+        gather_words(1, HALF, S)
+        w3_raw = held("w3_raw", [P, PASSES, H], I32)
+        nc.sync.dma_start(w3_raw[:], w3_words.rearrange("a p e i -> p a (e i)").bitcast(I32))
+        load_w2(2)
+        for quarter in range(4):
+            gather_words(2, QUARTER * quarter, QUARTER * (quarter + 1))
+        w4_raw = held("w4_raw", [P, TILES, N], F32)
+        w4_rows = w4.rearrange("(q t i) n -> t q i n", t=TILES, i=RUN)
+        for t in range(TILES):
+            nc.sync.dma_start(w4_raw[:, t, :], w4_rows[t])
 
         def quantise(codes, scales, values):
             nc.vector.quantize_mx(out=codes.bitcast(FP8X4), scales=scales, in_=values)
@@ -190,7 +211,8 @@ def tile_list_plankton_tendency_kernel(
                 stop=stop,
             )
 
-        def pair_pass(acc, codes, scales, a, quarter, u, order=(0, 1, 2)):
+        def unit_pass(acc, codes, scales, a, unit, order=(0, 1, 2)):
+            quarter, u = divmod(unit, 2)
             for e in range(2):
                 t = 2 * u + e
                 table_pass(acc[:, QUARTER * e : QUARTER * (e + 1)], codes(a, t), scales(a, t),
@@ -199,113 +221,101 @@ def tile_list_plankton_tendency_kernel(
         def w1_tile(a, t):
             return w1_codes[:, a, 2 * P * t : 2 * P * (t + 1)].bitcast(FP4X4)
 
-        gather_words(0, 0, S)
-        w1_pair = {0: order_columns("w1_scales_first", w1_scales_raw, U8, 0, 2)}
-        load_w2(1)
-        drift_cols = held("drift_cols", [P, OUT_TILES], F32)
-        with nc.allow_non_contiguous_dma(reason="one drift value for each partition and tile of out"):
-            nc.sync.dma_start(drift_cols[:], drift.rearrange("(m p) -> p m", p=P))
-        uptake = {(quarter, u): bank(2 * quarter + u) for quarter in range(4) for u in range(2)}
-
         def w1_scale_tile(a, t):
-            return w1_pair[t // 2][:, a, P * (t % 2) : P * (t % 2 + 1)]
+            return w1_scale_rows[:, a, P * t : P * (t + 1)]
 
-        for a in range(PASSES):
-            for half in range(2):
-                if a > 0 and (a, half) != (2, 0):
-                    gather_words(a, HALF * half, HALF * (half + 1))
-                for quarter in (2 * half, 2 * half + 1):
-                    if (a, half) == (2, 0):
-                        gather_words(a, QUARTER * quarter, QUARTER * (quarter + 1))
-                    pair_pass(uptake[quarter, 0], w1_tile, w1_scale_tile, a, quarter, 0)
-        w1_pair[1] = order_columns("w1_scales_rest", w1_scales_raw, U8, 2, 2)
-        for quarter in range(4):
-            for a in range(PASSES):
-                pair_pass(uptake[quarter, 1], w1_tile, w1_scale_tile, a, quarter, 1)
+        uptake = [bank(unit) for unit in range(UNITS)]
+        for unit in range(UNITS):
+            order = (0, 1, 2) if unit < 2 else (2, 0, 1)
+            for a in order:
+                unit_pass(uptake[unit], w1_tile, w1_scale_tile, a, unit, order)
 
-        load_w2(2)
-        w2_codes = [held(f"w2_codes{a}", [P, H], U32) for a in range(PASSES)]
-        w2_scales = [held(f"w2_scales{a}", [P, H], U8) for a in range(PASSES)]
-        w2_bf = {(a, u): held(f"w2_bf{a}_{u}", [P, PACK * 2 * P], BF16) for a in range(PASSES) for u in range(2)}
+        pairs = [(a, u) for a in range(PASSES) for u in range(2)]
+        w2_codes = {(a, u): held(f"w2_codes{a}_{u}", [P, 2 * P], U32) for a, u in pairs}
+        w2_scales = {(a, u): held(f"w2_scales{a}_{u}", [P, 2 * P], U8) for a, u in pairs}
+        w2_bf = {(a, u): held(f"w2_bf{a}_{u}", [P, PACK * 2 * P], BF16) for a, u in pairs}
 
-        def round_w2(a, u):
+        def round_w2(a, u, on_gpsimd=False):
             rounded = w2_bf[a, u][:].rearrange("p (t q i j) -> p t q j i", t=2, q=RUNS, j=PACK)
             source = w2_raw[a][:].rearrange("p j (q t i) -> p t q j i", t=TILES, q=RUNS)[:, 2 * u : 2 * u + 2]
-            if u == 0 or a == PASSES - 1:
-                nc.vector.tensor_copy(rounded, source)
-            else:
+            if on_gpsimd:
                 for e in range(2):
                     nc.gpsimd.tensor_scalar(rounded[:, e], source[:, e], 1.0, 0.0, ALU.mult, ALU.add)
+            else:
+                nc.vector.tensor_copy(rounded, source)
 
         def quantise_w2(a, u):
-            columns = slice(2 * P * u, 2 * P * (u + 1))
-            quantise(w2_codes[a][:, columns], w2_scales[a][:, columns], w2_bf[a, u][:])
+            quantise(w2_codes[a, u][:], w2_scales[a, u][:], w2_bf[a, u][:])
 
         def w2_tile(a, t):
-            return w2_codes[a][:, P * t : P * (t + 1)].bitcast(FP8X4)
+            return w2_codes[a, t // 2][:, P * (t % 2) : P * (t % 2 + 1)].bitcast(FP8X4)
 
         def w2_scale_tile(a, t):
-            return w2_scales[a][:, P * t : P * (t + 1)]
+            return w2_scales[a, t // 2][:, P * (t % 2) : P * (t % 2 + 1)]
 
-        def growth_pass(a, quarter, u):
-            pair_pass(growth[quarter, u], w2_tile, w2_scale_tile, a, quarter, u, W2_ORDER)
+        growth, loss, saturated, h_bf = {}, {}, {}, {}
 
-        def mortality(j, number):
-            acc = bank(number)
+        def grow(unit, number, passes=(0, 1, 2)):
+            if unit not in growth:
+                growth[unit] = bank(number)
+            for a in passes:
+                unit_pass(growth[unit], w2_tile, w2_scale_tile, a, unit, passes if len(passes) == PASSES else (0, 1, 2))
+
+        def lose(j, number):
+            loss[j] = bank(number)
             for t in range(TILES):
                 for a in range(PASSES):
-                    table_pass(acc[:, SLICE * t : SLICE * (t + 1)],
+                    table_pass(loss[j][:, SLICE * t : SLICE * (t + 1)],
                                w3_codes[:, a, P * t : P * (t + 1)].bitcast(FP8X4),
                                w3_scale_rows[4 * (a + 1) : P, 0, P * t : P * (t + 1)], a, SLICE * j, SLICE,
                                a == 0, a == PASSES - 1)
-            return acc
 
-        saturated = {}
-
-        def weave(acc, tiles):
-            return acc[:].rearrange("p (e c) -> p c e", e=tiles)
+        def weave(acc):
+            return acc[:].rearrange("p (e c) -> p c e", e=2)
 
         def woven(values):
             return values.rearrange("p (c e) -> p c e", e=2)
 
-        def saturate(half, t):
-            acc = uptake[half, t]
+        def saturate(unit):
+            acc = uptake[unit]
             magnitude = ring.tile([P, HALF], F32, name="magnitude")
             root = ring.tile([P, HALF], F32, name="root")
             inverse = ring.tile([P, HALF], F32, name="inverse", bufs=4)
-            nc.scalar.activation(woven(magnitude[:]), weave(acc, 2), ACT.Abs)
-            if (half, t) in COPIED:
+            nc.scalar.activation(woven(magnitude[:]), weave(acc), ACT.Abs)
+            if unit in COPIED:
                 drive = ring.tile([P, HALF], F32, name="drive", bufs=4)
-                nc.scalar.copy(woven(drive[:]), weave(acc, 2))
+                nc.scalar.copy(woven(drive[:]), weave(acc))
             nc.scalar.activation(root[:], magnitude[:], ACT.Abs_reciprocal_sqrt, bias=1.0)
             nc.scalar.activation(inverse[:], root[:], ACT.Square)
-            saturated[half, t] = held(f"saturated{half}_{t}", [P, HALF], F32)
-            if (half, t) in COPIED:
-                nc.gpsimd.tensor_tensor(saturated[half, t][:], drive[:], inverse[:], ALU.mult)
+            saturated[unit] = held(f"saturated{unit}", [P, HALF], F32)
+            if unit in COPIED:
+                nc.gpsimd.tensor_tensor(saturated[unit][:], drive[:], inverse[:], ALU.mult)
             else:
-                nc.vector.tensor_tensor(woven(saturated[half, t][:]), weave(acc, 2), woven(inverse[:]), ALU.mult)
+                nc.vector.tensor_tensor(woven(saturated[unit][:]), weave(acc), woven(inverse[:]), ALU.mult)
 
-        gain = [held(f"gain{quarter}", [P, 2, 2 * QUARTER], F32) for quarter in range(4)]
+        gain = [held(f"gain{quarter}", [P, 2, HALF], F32) for quarter in range(4)]
 
-        def multiply_growth(quarter, u):
-            nc.vector.tensor_tensor(woven(gain[quarter][:, u, :]), weave(growth[quarter, u], 2),
-                                    woven(saturated[quarter, u][:]), ALU.mult)
+        def multiply(unit):
+            quarter, u = divmod(unit, 2)
+            nc.vector.tensor_tensor(woven(gain[quarter][:, u, :]), weave(growth[unit]),
+                                    woven(saturated[unit][:]), ALU.mult)
 
-        def net_growth(h_bf, acc, quarter, u):
+        def subtract(j):
+            quarter, side = divmod(j, 2)
+            if side == 0:
+                h_bf[quarter] = ring.tile([P, TILES * QUARTER], BF16, name="h_bf", align_bytes=64)
             nc.vector.tensor_tensor(
-                h_bf.rearrange("p (c u e) -> p c u e", u=2, e=2),
-                gain[quarter][:, :, 2 * SLICE * u : 2 * SLICE * (u + 1)].rearrange("p u (c e) -> p c u e", e=2),
-                acc[:].rearrange("p (u e c) -> p c u e", u=2, e=2),
+                h_bf[quarter][:, HALF * side : HALF * (side + 1)].rearrange("p (c u e) -> p c u e", u=2, e=2),
+                gain[quarter][:, :, 2 * SLICE * side : 2 * SLICE * (side + 1)].rearrange("p u (c e) -> p c u e", e=2),
+                loss[j][:].rearrange("p (u e c) -> p c u e", u=2, e=2),
                 ALU.subtract,
             )
 
-        w4_codes = held("w4_codes", [P, N], U32)
-        w4_scales = held("w4_scales", [P, N], U8)
 
-        def tendencies(h_bf, lo, width, banks, on_vector=False):
+        def tendencies(values, lo, width, banks, on_vector=False):
             h_codes = ring.tile([P, width], U32, name="h_codes", align_bytes=64)
             h_scales = ring.tile([P, width], U8, name="h_scales", align_bytes=64)
-            quantise(h_codes[:], h_scales[:], h_bf)
+            quantise(h_codes[:], h_scales[:], values)
             accs = [bank(number) for number in banks]
             result = ring.tile([P, OUT_TILES, width], F32, name="result", bufs=4)
             sums = []
@@ -333,39 +343,35 @@ def tile_list_plankton_tendency_kernel(
                     nc.scalar.activation(result[:, m, :], sums[m], ACT.Identity, bias=drift_cols[:, m : m + 1])
             nc.sync.dma_start(out[:, lo : lo + width].rearrange("(m p) s -> p m s", p=P), result[:])
 
-        growth = {}
-        w3_raw = held("w3_raw", [P, PASSES, H], I32)
-        nc.sync.dma_start(w3_raw[:], w3_words.rearrange("a p e i -> p a (e i)").bitcast(I32))
-        w4_raw = held("w4_raw", [P, TILES, N], F32)
-        w4_rows = w4.rearrange("(q t i) n -> t q i n", t=TILES, i=RUN)
-        for t in range(TILES):
-            nc.sync.dma_start(w4_raw[:, t, :], w4_rows[t])
+        def finish(quarter, banks):
+            tendencies(h_bf[quarter][:], QUARTER * quarter, QUARTER, banks)
 
-        def grow_early(quarter, u, passes):
-            for a in passes:
-                growth_pass(a, quarter, u)
+        def finish_slice(j, number, on_vector):
+            quarter, side = divmod(j, 2)
+            tendencies(h_bf[quarter][:, HALF * side : HALF * (side + 1)], SLICE * j, SLICE, (number,), on_vector)
 
-        for a in range(PASSES - 1):
-            round_w2(a, 1)
+        round_w2(0, 1, True)
+        round_w2(1, 1, True)
         round_w2(0, 0)
-        w3_scale_rows = order_columns("w3_scale_rows", w3_scales_raw, U8)
+        saturate(0)
         quantise_w2(0, 0)
-        saturate(0, 0)
-        growth[0, 0] = bank(0)
-        grow_early(0, 0, (0,))
         round_w2(1, 0)
-        quantise_w2(0, 1)
+        saturate(1)
         quantise_w2(1, 0)
-        grow_early(0, 0, (1,))
-        saturate(1, 0)
-        growth[1, 0] = bank(2)
-        grow_early(1, 0, (0, 1))
+        w3_scale_rows = order_columns("w3_scale_rows", w3_scales_raw, U8)
+        w3_codes = order_columns("w3_codes", w3_raw, U32)
+        saturate(2)
+        lose(0, 0)
+        lose(1, 1)
+        grow(0, 2, (0, 1))
         round_w2(2, 0)
         round_w2(2, 1)
         quantise_w2(2, 0)
-        grow_early(0, 0, (2,))
-        grow_early(1, 0, (2,))
-        w3_codes = order_columns("w3_codes", w3_raw, U32)
+        grow(0, 2, (2,))
+        quantise_w2(0, 1)
+        quantise_w2(1, 1)
+        quantise_w2(2, 1)
+        saturate(3)
 
         w4_bf = held("w4_bf", [P, TILES * N], BF16)
         for m in range(OUT_TILES):
@@ -375,63 +381,44 @@ def tile_list_plankton_tendency_kernel(
                 1.0, 0.0, ALU.mult, ALU.add,
             )
 
-        growth_pair, loss_pair, out_pair = (0, 1, 2, 3), (0, 1, 2, 0), (0, 1, 2, 1)
-        loss, h_bf = {}, {}
-
-        def grow(quarter, u):
-            growth[quarter, u] = bank(2 * growth_pair[quarter] + u)
-            for a in range(PASSES):
-                growth_pass(a, quarter, u)
-
-        def lose(quarter, u):
-            loss[2 * quarter + u] = mortality(2 * quarter + u, 2 * loss_pair[quarter] + u)
-
-        def subtract(quarter):
-            h_bf[quarter] = ring.tile([P, TILES * QUARTER], BF16, name="h_bf", align_bytes=64)
-            for u in range(2):
-                net_growth(h_bf[quarter][:, HALF * u : HALF * (u + 1)], loss[2 * quarter + u], quarter, u)
-
-        def finish(quarter):
-            pair = out_pair[quarter]
-            tendencies(h_bf[quarter][:], QUARTER * quarter, QUARTER, (2 * pair, 2 * pair + 1))
-
-        def finish_slice(quarter, u):
-            tendencies(h_bf[quarter][:, HALF * u : HALF * (u + 1)], QUARTER * quarter + SLICE * u, SLICE,
-                       (2 * out_pair[quarter] + u,), u == 1)
-
-        for quarter in range(2):
-            multiply_growth(quarter, 0)
-            lose(quarter, 0)
-        saturate(0, 1)
-        quantise_w2(1, 1)
-        quantise_w2(2, 1)
-        grow(0, 1)
-        saturate(1, 1)
-        grow(1, 1)
-        for quarter in range(2):
-            multiply_growth(quarter, 1)
-            lose(quarter, 1)
-            saturate(2, quarter)
-            grow(2, quarter)
+        saturate(4)
+        grow(2, 4, (2, 0, 1))
+        grow(1, 3)
+        multiply(0)
+        grow(3, 2)
+        saturate(5)
+        multiply(1)
+        lose(2, 5)
         subtract(0)
-        quantise(w4_codes[:], w4_scales[:], w4_bf[:])
-        saturate(3, 0)
-        grow(3, 0)
-        finish(0)
-        multiply_growth(2, 0)
-        lose(2, 0)
-        saturate(3, 1)
-        grow(3, 1)
-        multiply_growth(2, 1)
-        lose(2, 1)
+        lose(3, 3)
         subtract(1)
-        multiply_growth(3, 0)
-        finish(1)
-        for u in range(2):
-            lose(3, u)
-        multiply_growth(3, 1)
+        grow(4, 0)
+        multiply(2)
+        saturate(6)
+        multiply(3)
+        grow(5, 1)
+        w4_codes = held("w4_codes", [P, N], U32)
+        w4_scales = held("w4_scales", [P, N], U8)
+        quantise(w4_codes[:], w4_scales[:], w4_bf[:])
+        saturate(7)
+        finish(0, (4, 6))
+        lose(4, 2)
         subtract(2)
-        finish(2)
+        lose(5, 5)
         subtract(3)
-        for u in range(2):
-            finish_slice(3, u)
+        grow(6, 3)
+        multiply(4)
+        grow(7, 0)
+        multiply(5)
+        finish(1, (1, 7))
+        lose(6, 4)
+        lose(7, 6)
+        subtract(4)
+        subtract(5)
+        multiply(6)
+        finish(2, (2, 5))
+        multiply(7)
+        subtract(6)
+        finish_slice(6, 3, False)
+        subtract(7)
+        finish_slice(7, 0, True)

@@ -30,7 +30,8 @@ OUT_TILES = N // P
 UNITS = 8
 STAGE = 4 * T
 
-COPIED = (3, 4, 5, 6, 7)
+COPIED = (4, 5, 6, 7)
+ROOT_TWICE = (4, 5)
 REACH = 128
 W1_BYTES = PASSES * 2 * H
 WINDOW = W1_BYTES - REACH
@@ -51,12 +52,9 @@ OFFSET = {
     "w2_raw1": W2_SECOND,
     "tab2": TAB2,
     "w4_raw": TAB2 + REACH,
-    "saturated4": TAB2 + REACH,
-    "saturated5": TAB2 + REACH + 4 * HALF,
-    "w2_codes0_1": W2_LAST + REACH,
-    "w2_codes1_1": W2_LAST + REACH + 8 * P,
     "saturated2": TAB1,
-    "saturated3": W2_LAST + STAGE,
+    "w2_bf1_1": TAB1 + 4 * HALF,
+    "saturated3": W2_LAST + STAGE - REACH,
     "w4_codes": W2_LAST + STAGE,
     "w1_raw": W1_RAW,
     "last_scales": W1_RAW + REACH,
@@ -279,19 +277,24 @@ def tile_list_plankton_tendency_kernel(
         def saturate(unit):
             acc = uptake[unit]
             magnitude = ring.tile([P, HALF], F32, name="magnitude")
-            root = ring.tile([P, HALF], F32, name="root")
-            inverse = ring.tile([P, HALF], F32, name="inverse", bufs=4)
+            root = ring.tile([P, HALF], F32, name="root", bufs=4)
             nc.scalar.activation(woven(magnitude[:]), weave(acc), ACT.Abs)
             if unit in COPIED:
                 drive = ring.tile([P, HALF], F32, name="drive", bufs=4)
                 nc.scalar.copy(woven(drive[:]), weave(acc))
             nc.scalar.activation(root[:], magnitude[:], ACT.Abs_reciprocal_sqrt, bias=1.0)
-            nc.scalar.activation(inverse[:], root[:], ACT.Square)
             saturated[unit] = held(f"saturated{unit}", [P, HALF], F32)
-            if unit in COPIED:
-                nc.gpsimd.tensor_tensor(saturated[unit][:], drive[:], inverse[:], ALU.mult)
+            if unit in ROOT_TWICE:
+                part = ring.tile([P, HALF], F32, name="part")
+                nc.gpsimd.tensor_tensor(part[:], drive[:], root[:], ALU.mult)
+                nc.gpsimd.tensor_tensor(saturated[unit][:], part[:], root[:], ALU.mult)
             else:
-                nc.vector.tensor_tensor(woven(saturated[unit][:]), weave(acc), woven(inverse[:]), ALU.mult)
+                inverse = ring.tile([P, HALF], F32, name="inverse", bufs=4)
+                nc.scalar.activation(inverse[:], root[:], ACT.Square)
+                if unit in COPIED:
+                    nc.gpsimd.tensor_tensor(saturated[unit][:], drive[:], inverse[:], ALU.mult)
+                else:
+                    nc.vector.tensor_tensor(woven(saturated[unit][:]), weave(acc), woven(inverse[:]), ALU.mult)
 
         gain = [held(f"gain{quarter}", [P, 2, HALF], F32) for quarter in range(4)]
 
@@ -303,7 +306,7 @@ def tile_list_plankton_tendency_kernel(
         def subtract(j):
             quarter, side = divmod(j, 2)
             if side == 0:
-                h_bf[quarter] = ring.tile([P, TILES * QUARTER], BF16, name="h_bf", align_bytes=64)
+                h_bf[quarter] = ring.tile([P, TILES * QUARTER], BF16, name="h_bf", align_bytes=64, bufs=4)
             nc.vector.tensor_tensor(
                 h_bf[quarter][:, HALF * side : HALF * (side + 1)].rearrange("p (c u e) -> p c u e", u=2, e=2),
                 gain[quarter][:, :, 2 * SLICE * side : 2 * SLICE * (side + 1)].rearrange("p u (c e) -> p c u e", e=2),
@@ -313,8 +316,8 @@ def tile_list_plankton_tendency_kernel(
 
 
         def tendencies(values, lo, width, banks, on_vector=False):
-            h_codes = ring.tile([P, width], U32, name="h_codes", align_bytes=64)
-            h_scales = ring.tile([P, width], U8, name="h_scales", align_bytes=64)
+            h_codes = ring.tile([P, width], U32, name="h_codes", align_bytes=64, bufs=4)
+            h_scales = ring.tile([P, width], U8, name="h_scales", align_bytes=64, bufs=4)
             quantise(h_codes[:], h_scales[:], values)
             accs = [bank(number) for number in banks]
             result = ring.tile([P, OUT_TILES, width], F32, name="result", bufs=4)
@@ -350,42 +353,39 @@ def tile_list_plankton_tendency_kernel(
             quarter, side = divmod(j, 2)
             tendencies(h_bf[quarter][:, HALF * side : HALF * (side + 1)], SLICE * j, SLICE, (number,), on_vector)
 
-        round_w2(0, 1, True)
-        round_w2(1, 1, True)
         round_w2(0, 0)
-        saturate(0)
+        round_w2(0, 1)
         quantise_w2(0, 0)
+        quantise_w2(0, 1)
+        saturate(0)
         round_w2(1, 0)
         saturate(1)
         quantise_w2(1, 0)
         w3_scale_rows = order_columns("w3_scale_rows", w3_scales_raw, U8)
         w3_codes = order_columns("w3_codes", w3_raw, U32)
+        round_w2(1, 1)
         saturate(2)
         lose(0, 0)
         lose(1, 1)
         grow(0, 2, (0, 1))
         round_w2(2, 0)
-        round_w2(2, 1)
+        quantise_w2(1, 1)
         quantise_w2(2, 0)
         grow(0, 2, (2,))
-        quantise_w2(0, 1)
-        quantise_w2(1, 1)
-        quantise_w2(2, 1)
+        round_w2(2, 1)
         saturate(3)
-
-        w4_bf = held("w4_bf", [P, TILES * N], BF16)
-        for m in range(OUT_TILES):
-            nc.gpsimd.tensor_scalar(
-                w4_bf[:, TILES * P * m : TILES * P * (m + 1)].rearrange("p (c i t) -> p c t i", t=TILES, i=4),
-                w4_raw[:, :, P * m : P * (m + 1)].rearrange("p t (c i) -> p c t i", i=4),
-                1.0, 0.0, ALU.mult, ALU.add,
-            )
+        quantise_w2(2, 1)
 
         saturate(4)
         grow(2, 4, (2, 0, 1))
         grow(1, 3)
         multiply(0)
         grow(3, 2)
+        w4_bf = held("w4_bf", [P, TILES * N], BF16)
+        nc.scalar.copy(
+            w4_bf[:].rearrange("p (c i t) -> p c t i", t=TILES, i=4),
+            w4_raw[:].rearrange("p t (c i) -> p c t i", i=4),
+        )
         saturate(5)
         multiply(1)
         lose(2, 5)
@@ -401,24 +401,24 @@ def tile_list_plankton_tendency_kernel(
         w4_scales = held("w4_scales", [P, N], U8)
         quantise(w4_codes[:], w4_scales[:], w4_bf[:])
         saturate(7)
-        finish(0, (4, 6))
-        lose(4, 2)
+        lose(4, 4)
         subtract(2)
-        lose(5, 5)
+        lose(5, 2)
         subtract(3)
-        grow(6, 3)
+        finish(0, (6, 7))
+        grow(6, 5)
         multiply(4)
-        grow(7, 0)
+        grow(7, 3)
         multiply(5)
-        finish(1, (1, 7))
-        lose(6, 4)
-        lose(7, 6)
         subtract(4)
         subtract(5)
+        finish(1, (4, 2))
+        lose(6, 0)
+        lose(7, 1)
         multiply(6)
-        finish(2, (2, 5))
         multiply(7)
+        finish(2, (6, 7))
         subtract(6)
-        finish_slice(6, 3, False)
+        finish_slice(6, 5, False)
         subtract(7)
-        finish_slice(7, 0, True)
+        finish_slice(7, 3, True)

@@ -251,7 +251,7 @@ def tile_list_plankton_tendency_kernel(
         def w2_scale_tile(a, t):
             return w2_scales[a, t // 2][:, P * (t % 2) : P * (t % 2 + 1)]
 
-        growth, loss, saturated, h_bf = {}, {}, {}, {}
+        growth, loss, saturated, pending, h_bf = {}, {}, {}, {}, {}
 
         def grow(unit, number, passes=(0, 1, 2)):
             if unit not in growth:
@@ -274,27 +274,35 @@ def tile_list_plankton_tendency_kernel(
         def woven(values):
             return values.rearrange("p (c e) -> p c e", e=2)
 
-        def saturate(unit):
-            acc = uptake[unit]
-            magnitude = ring.tile([P, HALF], F32, name="magnitude")
-            root = ring.tile([P, HALF], F32, name="root", bufs=4)
-            nc.scalar.activation(woven(magnitude[:]), weave(acc), ACT.Abs)
-            if unit in COPIED:
-                drive = ring.tile([P, HALF], F32, name="drive", bufs=4)
-                nc.scalar.copy(woven(drive[:]), weave(acc))
-            nc.scalar.activation(root[:], magnitude[:], ACT.Abs_reciprocal_sqrt, bias=1.0)
-            saturated[unit] = held(f"saturated{unit}", [P, HALF], F32)
-            if unit in ROOT_TWICE:
-                part = ring.tile([P, HALF], F32, name="part")
-                nc.gpsimd.tensor_tensor(part[:], drive[:], root[:], ALU.mult)
-                nc.gpsimd.tensor_tensor(saturated[unit][:], part[:], root[:], ALU.mult)
-            else:
-                inverse = ring.tile([P, HALF], F32, name="inverse", bufs=4)
-                nc.scalar.activation(inverse[:], root[:], ACT.Square)
+        def saturate(quarter):
+            units = (2 * quarter, 2 * quarter + 1)
+            magnitude, drive, root, inverse = {}, {}, {}, {}
+            for unit in units:
+                magnitude[unit] = ring.tile([P, HALF], F32, name="magnitude")
+                nc.scalar.activation(woven(magnitude[unit][:]), weave(uptake[unit]), ACT.Abs)
                 if unit in COPIED:
-                    nc.gpsimd.tensor_tensor(saturated[unit][:], drive[:], inverse[:], ALU.mult)
+                    drive[unit] = ring.tile([P, HALF], F32, name="drive", bufs=4)
+                    nc.scalar.copy(woven(drive[unit][:]), weave(uptake[unit]))
+            for unit in units:
+                root[unit] = ring.tile([P, HALF], F32, name="root", bufs=4)
+                nc.scalar.activation(root[unit][:], magnitude[unit][:], ACT.Abs_reciprocal_sqrt, bias=1.0)
+            for unit in units:
+                if unit not in ROOT_TWICE:
+                    inverse[unit] = ring.tile([P, HALF], F32, name="inverse", bufs=4)
+                    nc.scalar.activation(inverse[unit][:], root[unit][:], ACT.Square)
+            for unit in units:
+                saturated[unit] = held(f"saturated{unit}", [P, HALF], F32)
+                if unit in ROOT_TWICE:
+                    part = ring.tile([P, HALF], F32, name="part")
+                    nc.gpsimd.tensor_tensor(part[:], drive[unit][:], root[unit][:], ALU.mult)
+                    nc.gpsimd.tensor_tensor(saturated[unit][:], part[:], root[unit][:], ALU.mult)
+                elif unit in COPIED:
+                    nc.gpsimd.tensor_tensor(saturated[unit][:], drive[unit][:], inverse[unit][:], ALU.mult)
                 else:
-                    nc.vector.tensor_tensor(woven(saturated[unit][:]), weave(acc), woven(inverse[:]), ALU.mult)
+                    pending[unit] = inverse[unit]
+
+        def release(unit):
+            nc.vector.tensor_tensor(woven(saturated[unit][:]), weave(uptake[unit]), woven(pending[unit][:]), ALU.mult)
 
         gain = [held(f"gain{quarter}", [P, 2, HALF], F32) for quarter in range(4)]
 
@@ -353,30 +361,31 @@ def tile_list_plankton_tendency_kernel(
             quarter, side = divmod(j, 2)
             tendencies(h_bf[quarter][:, HALF * side : HALF * (side + 1)], SLICE * j, SLICE, (number,), on_vector)
 
+        saturate(0)
+        saturate(1)
         round_w2(0, 0)
         round_w2(0, 1)
         quantise_w2(0, 0)
         quantise_w2(0, 1)
-        saturate(0)
         round_w2(1, 0)
-        saturate(1)
+        release(0)
         quantise_w2(1, 0)
+        release(1)
         w3_scale_rows = order_columns("w3_scale_rows", w3_scales_raw, U8)
         w3_codes = order_columns("w3_codes", w3_raw, U32)
         round_w2(1, 1)
-        saturate(2)
         lose(0, 0)
         lose(1, 1)
+        release(2)
         grow(0, 2, (0, 1))
         round_w2(2, 0)
         quantise_w2(1, 1)
         quantise_w2(2, 0)
         grow(0, 2, (2,))
         round_w2(2, 1)
-        saturate(3)
+        release(3)
         quantise_w2(2, 1)
-
-        saturate(4)
+        saturate(2)
         grow(2, 4, (2, 0, 1))
         grow(1, 3)
         multiply(0)
@@ -386,22 +395,20 @@ def tile_list_plankton_tendency_kernel(
             w4_bf[:].rearrange("p (c i t) -> p c t i", t=TILES, i=4),
             w4_raw[:].rearrange("p t (c i) -> p c t i", i=4),
         )
-        saturate(5)
+        saturate(3)
         multiply(1)
         lose(2, 5)
-        subtract(0)
-        lose(3, 3)
-        subtract(1)
-        grow(4, 0)
         multiply(2)
-        saturate(6)
+        lose(3, 3)
+        subtract(0)
+        grow(4, 4)
+        subtract(1)
+        grow(5, 0)
         multiply(3)
-        grow(5, 1)
         w4_codes = held("w4_codes", [P, N], U32)
         w4_scales = held("w4_scales", [P, N], U8)
         quantise(w4_codes[:], w4_scales[:], w4_bf[:])
-        saturate(7)
-        lose(4, 4)
+        lose(4, 1)
         subtract(2)
         lose(5, 2)
         subtract(3)
@@ -410,14 +417,14 @@ def tile_list_plankton_tendency_kernel(
         multiply(4)
         grow(7, 3)
         multiply(5)
+        lose(6, 4)
+        finish(1, (0, 6))
         subtract(4)
-        subtract(5)
-        finish(1, (4, 2))
-        lose(6, 0)
         lose(7, 1)
+        subtract(5)
         multiply(6)
         multiply(7)
-        finish(2, (6, 7))
+        finish(2, (2, 7))
         subtract(6)
         finish_slice(6, 5, False)
         subtract(7)

@@ -31,7 +31,6 @@ UNITS = 8
 STAGE = 4 * T
 
 COPIED = (4, 5, 6, 7)
-ROOT_TWICE = (4, 5)
 REACH = 128
 W1_BYTES = PASSES * 2 * H
 WINDOW = W1_BYTES - REACH
@@ -53,13 +52,21 @@ OFFSET = {
     "tab2": TAB2,
     "w4_raw": TAB2 + REACH,
     "saturated2": TAB1,
-    "w2_bf1_1": TAB1 + 4 * HALF,
+    "w2_bf2_1": W2_LAST + 4 * STAGE,
+    "w4_bf": W2_LAST + 4 * STAGE,
+    "saturated4": TAB2 + REACH,
+    "saturated5": TAB2 + REACH + 4 * HALF,
+    "w2_bf0_1": W2_LAST + 3 * STAGE,
+    "w2_bf1_1": W2_LAST + 3 * STAGE,
+    "w2_codes1_1": TAB1 + 4 * HALF,
+    "w2_codes1_0": TAB1 + 6 * HALF,
+    "w2_bf0_0": W2_LAST + 2 * STAGE,
+    "saturated0": W2_LAST + 2 * STAGE + H,
     "saturated3": W2_LAST + STAGE - REACH,
     "w4_codes": W2_LAST + STAGE,
     "w1_raw": W1_RAW,
     "last_scales": W1_RAW + REACH,
     "w1_scale_rows": W1_RAW + REACH + S,
-    "w2_bf0_0": W2_LAST + 2 * STAGE,
     "w3_scale_rows": W2_LAST + 2 * STAGE,
     "w2_raw0": W2_FIRST,
     "tab1": TAB1,
@@ -287,16 +294,11 @@ def tile_list_plankton_tendency_kernel(
                 root[unit] = ring.tile([P, HALF], F32, name="root", bufs=4)
                 nc.scalar.activation(root[unit][:], magnitude[unit][:], ACT.Abs_reciprocal_sqrt, bias=1.0)
             for unit in units:
-                if unit not in ROOT_TWICE:
-                    inverse[unit] = ring.tile([P, HALF], F32, name="inverse", bufs=4)
-                    nc.scalar.activation(inverse[unit][:], root[unit][:], ACT.Square)
+                inverse[unit] = ring.tile([P, HALF], F32, name="inverse", bufs=4)
+                nc.scalar.activation(inverse[unit][:], root[unit][:], ACT.Square)
             for unit in units:
                 saturated[unit] = held(f"saturated{unit}", [P, HALF], F32)
-                if unit in ROOT_TWICE:
-                    part = ring.tile([P, HALF], F32, name="part")
-                    nc.gpsimd.tensor_tensor(part[:], drive[unit][:], root[unit][:], ALU.mult)
-                    nc.gpsimd.tensor_tensor(saturated[unit][:], part[:], root[unit][:], ALU.mult)
-                elif unit in COPIED:
+                if unit in COPIED:
                     nc.gpsimd.tensor_tensor(saturated[unit][:], drive[unit][:], inverse[unit][:], ALU.mult)
                 else:
                     pending[unit] = inverse[unit]
@@ -366,40 +368,42 @@ def tile_list_plankton_tendency_kernel(
         round_w2(0, 0)
         round_w2(0, 1)
         quantise_w2(0, 0)
-        quantise_w2(0, 1)
         round_w2(1, 0)
+        quantise_w2(0, 1)
+        round_w2(1, 1, True)
         release(0)
-        quantise_w2(1, 0)
         release(1)
         w3_scale_rows = order_columns("w3_scale_rows", w3_scales_raw, U8)
         w3_codes = order_columns("w3_codes", w3_raw, U32)
-        round_w2(1, 1)
         lose(0, 0)
         lose(1, 1)
+        quantise_w2(1, 0)
+        quantise_w2(1, 1)
         release(2)
         grow(0, 2, (0, 1))
         round_w2(2, 0)
-        quantise_w2(1, 1)
+        round_w2(2, 1)
         quantise_w2(2, 0)
         grow(0, 2, (2,))
-        round_w2(2, 1)
-        release(3)
         quantise_w2(2, 1)
+        release(3)
+        w4_bf = held("w4_bf", [P, TILES * N], BF16)
+        for m in range(OUT_TILES):
+            nc.gpsimd.tensor_scalar(
+                w4_bf[:, TILES * P * m : TILES * P * (m + 1)].rearrange("p (c i t) -> p c t i", t=TILES, i=4),
+                w4_raw[:, :, P * m : P * (m + 1)].rearrange("p t (c i) -> p c t i", i=4),
+                1.0, 0.0, ALU.mult, ALU.add,
+            )
         saturate(2)
-        grow(2, 4, (2, 0, 1))
         grow(1, 3)
+        grow(2, 4, (2, 0, 1))
         multiply(0)
         grow(3, 2)
-        w4_bf = held("w4_bf", [P, TILES * N], BF16)
-        nc.scalar.copy(
-            w4_bf[:].rearrange("p (c i t) -> p c t i", t=TILES, i=4),
-            w4_raw[:].rearrange("p t (c i) -> p c t i", i=4),
-        )
         saturate(3)
         multiply(1)
-        lose(2, 5)
+        lose(2, 3)
         multiply(2)
-        lose(3, 3)
+        lose(3, 5)
         subtract(0)
         grow(4, 4)
         subtract(1)
@@ -413,9 +417,9 @@ def tile_list_plankton_tendency_kernel(
         lose(5, 2)
         subtract(3)
         finish(0, (6, 7))
-        grow(6, 5)
+        grow(6, 3)
         multiply(4)
-        grow(7, 3)
+        grow(7, 5)
         multiply(5)
         lose(6, 4)
         finish(1, (0, 6))
@@ -426,6 +430,6 @@ def tile_list_plankton_tendency_kernel(
         multiply(7)
         finish(2, (2, 7))
         subtract(6)
-        finish_slice(6, 5, False)
+        finish_slice(6, 3, False)
         subtract(7)
-        finish_slice(7, 3, True)
+        finish_slice(7, 5, True)

@@ -41,37 +41,38 @@ W1_RAW = TAB2 + STAGE - REACH
 W2_FIRST = W1_RAW + W1_BYTES - REACH
 TAB1 = W2_FIRST + STAGE
 W2_LAST = TAB1 + STAGE - REACH
+SPARE = W2_LAST + STAGE
 OFFSET = {
     "w1_codes": 0,
     "scale_window": WINDOW,
     "v_words0": W1_BYTES,
     "tab0": TAB0,
-    "drift_cols": TAB0,
     "v_words1": TAB0 + REACH,
     "w2_raw1": W2_SECOND,
     "tab2": TAB2,
+    "drift_cols": TAB0,
     "w4_raw": TAB2 + REACH,
-    "saturated2": TAB1,
-    "w2_bf2_1": W2_LAST + 4 * STAGE,
-    "w4_bf": W2_LAST + 4 * STAGE,
     "saturated4": TAB2 + REACH,
     "saturated5": TAB2 + REACH + 4 * HALF,
-    "w2_bf0_1": W2_LAST + 3 * STAGE,
-    "w2_bf1_1": W2_LAST + 3 * STAGE,
-    "w2_codes1_1": TAB1 + 4 * HALF,
-    "w2_codes1_0": TAB1 + 6 * HALF,
-    "w2_bf0_0": W2_LAST + 2 * STAGE,
-    "saturated0": W2_LAST + 2 * STAGE + H,
-    "saturated3": W2_LAST + STAGE - REACH,
-    "w4_codes": W2_LAST + STAGE,
     "w1_raw": W1_RAW,
     "last_scales": W1_RAW + REACH,
     "w1_scale_rows": W1_RAW + REACH + S,
-    "w3_scale_rows": W2_LAST + 2 * STAGE,
     "w2_raw0": W2_FIRST,
     "tab1": TAB1,
     "w3_raw": TAB1,
+    "saturated3": TAB1,
+    "w4_codes": TAB1,
+    "w4_bf": SPARE + 16 * HALF - REACH,
     "w2_raw2": W2_LAST,
+    "w2_codes1_1": W2_LAST + REACH,
+    "w2_bf0_0": SPARE,
+    "saturated0": SPARE,
+    "w2_bf0_1": SPARE + 4 * HALF,
+    "w2_bf1_1": SPARE + 4 * HALF,
+    "w2_bf2_0": SPARE + 8 * HALF,
+    "w3_scale_rows": SPARE + 8 * HALF,
+    "w2_bf2_1": SPARE + 12 * HALF,
+    "saturated2": TAB1 + 4 * HALF,
 }
 
 
@@ -191,9 +192,9 @@ def tile_list_plankton_tendency_kernel(
             nc.sync.dma_start(drift_cols[:], drift.rearrange("(m p) -> p m", p=P))
         gather_words(1, 0, HALF)
         gather_words(1, HALF, S)
+        load_w2(2)
         w3_raw = held("w3_raw", [P, PASSES, H], I32)
         nc.sync.dma_start(w3_raw[:], w3_words.rearrange("a p e i -> p a (e i)").bitcast(I32))
-        load_w2(2)
         for quarter in range(4):
             gather_words(2, QUARTER * quarter, QUARTER * (quarter + 1))
         w4_raw = held("w4_raw", [P, TILES, N], F32)
@@ -325,7 +326,7 @@ def tile_list_plankton_tendency_kernel(
             )
 
 
-        def tendencies(values, lo, width, banks, on_vector=False):
+        def tendencies(values, lo, width, banks, on_vector=False, by_tile=False):
             h_codes = ring.tile([P, width], U32, name="h_codes", align_bytes=64, bufs=4)
             h_scales = ring.tile([P, width], U8, name="h_scales", align_bytes=64, bufs=4)
             quantise(h_codes[:], h_scales[:], values)
@@ -354,10 +355,13 @@ def tile_list_plankton_tendency_kernel(
             else:
                 for m in range(OUT_TILES):
                     nc.scalar.activation(result[:, m, :], sums[m], ACT.Identity, bias=drift_cols[:, m : m + 1])
-            nc.sync.dma_start(out[:, lo : lo + width].rearrange("(m p) s -> p m s", p=P), result[:])
+                    if by_tile:
+                        nc.sync.dma_start(out[P * m : P * (m + 1), lo : lo + width], result[:, m, :])
+            if not by_tile:
+                nc.sync.dma_start(out[:, lo : lo + width].rearrange("(m p) s -> p m s", p=P), result[:])
 
         def finish(quarter, banks):
-            tendencies(h_bf[quarter][:], QUARTER * quarter, QUARTER, banks)
+            tendencies(h_bf[quarter][:], QUARTER * quarter, QUARTER, banks, False, quarter == 2)
 
         def finish_slice(j, number, on_vector):
             quarter, side = divmod(j, 2)
@@ -373,20 +377,19 @@ def tile_list_plankton_tendency_kernel(
         round_w2(1, 1, True)
         release(0)
         release(1)
-        w3_scale_rows = order_columns("w3_scale_rows", w3_scales_raw, U8)
-        w3_codes = order_columns("w3_codes", w3_raw, U32)
-        lose(0, 0)
-        lose(1, 1)
         quantise_w2(1, 0)
-        quantise_w2(1, 1)
-        release(2)
-        grow(0, 2, (0, 1))
+        grow(0, 0, (0, 1))
         round_w2(2, 0)
         round_w2(2, 1)
         quantise_w2(2, 0)
-        grow(0, 2, (2,))
+        grow(0, 0, (2,))
+        quantise_w2(1, 1)
         quantise_w2(2, 1)
-        release(3)
+        grow(1, 1)
+        multiply(0)
+        grow(2, 0)
+        w3_scale_rows = order_columns("w3_scale_rows", w3_scales_raw, U8)
+        w3_codes = order_columns("w3_codes", w3_raw, U32)
         w4_bf = held("w4_bf", [P, TILES * N], BF16)
         for m in range(OUT_TILES):
             nc.gpsimd.tensor_scalar(
@@ -395,34 +398,35 @@ def tile_list_plankton_tendency_kernel(
                 1.0, 0.0, ALU.mult, ALU.add,
             )
         saturate(2)
-        grow(1, 3)
-        grow(2, 4, (2, 0, 1))
-        multiply(0)
-        grow(3, 2)
-        saturate(3)
+        lose(0, 4)
         multiply(1)
-        lose(2, 3)
+        lose(1, 1)
+        release(2)
+        grow(3, 2)
+        release(3)
+        saturate(3)
+        lose(2, 5)
+        lose(3, 3)
         multiply(2)
-        lose(3, 5)
+        grow(4, 0)
         subtract(0)
-        grow(4, 4)
+        grow(5, 4)
         subtract(1)
-        grow(5, 0)
+        lose(4, 1)
         multiply(3)
+        lose(5, 2)
         w4_codes = held("w4_codes", [P, N], U32)
         w4_scales = held("w4_scales", [P, N], U8)
         quantise(w4_codes[:], w4_scales[:], w4_bf[:])
-        lose(4, 1)
         subtract(2)
-        lose(5, 2)
         subtract(3)
         finish(0, (6, 7))
-        grow(6, 3)
+        grow(6, 5)
         multiply(4)
-        grow(7, 5)
+        grow(7, 3)
         multiply(5)
-        lose(6, 4)
-        finish(1, (0, 6))
+        lose(6, 0)
+        finish(1, (4, 6))
         subtract(4)
         lose(7, 1)
         subtract(5)
@@ -430,6 +434,6 @@ def tile_list_plankton_tendency_kernel(
         multiply(7)
         finish(2, (2, 7))
         subtract(6)
-        finish_slice(6, 3, False)
+        finish_slice(6, 5, False)
         subtract(7)
-        finish_slice(7, 5, True)
+        finish_slice(7, 3, True)

@@ -30,7 +30,7 @@ OUT_TILES = N // P
 UNITS = 8
 STAGE = 4 * T
 
-COPIED = (4, 5, 6, 7)
+COPIED = (4, 5, 6)
 REACH = 128
 W1_BYTES = PASSES * 2 * H
 WINDOW = W1_BYTES - REACH
@@ -53,6 +53,7 @@ OFFSET = {
     "drift_cols": TAB0,
     "w4_raw": TAB2 + REACH,
     "saturated4": TAB2 + REACH,
+    "saturated7": TAB2 + REACH,
     "saturated5": TAB2 + REACH + 4 * HALF,
     "w1_raw": W1_RAW,
     "last_scales": W1_RAW + REACH,
@@ -420,20 +421,21 @@ def tile_list_plankton_tendency_kernel(
         quantise(w4_codes[:], w4_scales[:], w4_bf[:])
         subtract(2)
         subtract(3)
-        finish(0, (6, 7))
-        grow(6, 5)
+        finish(0, (6, 5))
+        grow(6, 3)
         multiply(4)
-        grow(7, 3)
+        release(7)
+        grow(7, 0)
         multiply(5)
-        lose(6, 0)
-        finish(1, (4, 6))
+        lose(6, 4)
+        finish(1, (7, 6))
         subtract(4)
         lose(7, 1)
         subtract(5)
         multiply(6)
         multiply(7)
-        finish(2, (2, 7))
+        finish(2, (2, 5))
         subtract(6)
-        finish_slice(6, 5, False)
+        finish_slice(6, 3, False)
         subtract(7)
-        finish_slice(7, 3, True)
+        finish_slice(7, 0, True)

@@ -30,7 +30,7 @@ OUT_TILES = N // P
 UNITS = 8
 STAGE = 4 * T
 
-COPIED = (4, 5, 6)
+COPIED = (4, 5, 6, 7)
 REACH = 128
 W1_BYTES = PASSES * 2 * H
 WINDOW = W1_BYTES - REACH
@@ -53,7 +53,6 @@ OFFSET = {
     "drift_cols": TAB0,
     "w4_raw": TAB2 + REACH,
     "saturated4": TAB2 + REACH,
-    "saturated7": TAB2 + REACH,
     "saturated5": TAB2 + REACH + 4 * HALF,
     "w1_raw": W1_RAW,
     "last_scales": W1_RAW + REACH,
@@ -277,6 +276,17 @@ def tile_list_plankton_tendency_kernel(
                                w3_scale_rows[4 * (a + 1) : P, 0, P * t : P * (t + 1)], a, SLICE * j, SLICE,
                                a == 0, a == PASSES - 1)
 
+        def w3_tile(a, t):
+            return w3_codes[:, a, P * t : P * (t + 1)].bitcast(FP8X4)
+
+        def w3_scale_tile(a, t):
+            return w3_scale_rows[4 * (a + 1) : P, 0, P * t : P * (t + 1)]
+
+        def lose_unit(unit, number):
+            loss[unit] = bank(number)
+            for a in range(PASSES):
+                unit_pass(loss[unit], w3_tile, w3_scale_tile, a, unit)
+
         def weave(acc):
             return acc[:].rearrange("p (e c) -> p c e", e=2)
 
@@ -301,7 +311,10 @@ def tile_list_plankton_tendency_kernel(
             for unit in units:
                 saturated[unit] = held(f"saturated{unit}", [P, HALF], F32)
                 if unit in COPIED:
-                    nc.gpsimd.tensor_tensor(saturated[unit][:], drive[unit][:], inverse[unit][:], ALU.mult)
+                    for lo in (0, QUARTER):
+                        part = slice(lo, lo + QUARTER)
+                        nc.gpsimd.tensor_tensor(saturated[unit][:, part], drive[unit][:, part],
+                                                inverse[unit][:, part], ALU.mult)
                 else:
                     pending[unit] = inverse[unit]
 
@@ -326,6 +339,25 @@ def tile_list_plankton_tendency_kernel(
                 ALU.subtract,
             )
 
+
+        h_pairs = {}
+
+        def subtract_unit(unit):
+            quarter, u = divmod(unit, 2)
+            if u == 0:
+                h_pairs[quarter] = ring.tile([P, 2, HALF], BF16, name="h_pairs", bufs=3)
+            nc.vector.tensor_tensor(woven(h_pairs[quarter][:, u, :]), woven(gain[quarter][:, u, :]),
+                                    weave(loss[unit]), ALU.subtract)
+
+        def join_pairs(quarter, on_scalar=False):
+            h_bf[quarter] = ring.tile([P, TILES * QUARTER], BF16, name="h_bf", align_bytes=64, bufs=4)
+            word = U32 if on_scalar else I32
+            joined = h_bf[quarter][:].bitcast(word).rearrange("p (c u) -> p c u", u=2)
+            pairs_of_tiles = h_pairs[quarter][:].bitcast(word).rearrange("p u c -> p c u")
+            if on_scalar:
+                nc.scalar.copy(joined, pairs_of_tiles)
+            else:
+                nc.vector.tensor_copy(joined, pairs_of_tiles)
 
         def tendencies(values, lo, width, banks, on_vector=False, by_tile=False):
             h_codes = ring.tile([P, width], U32, name="h_codes", align_bytes=64, bufs=4)
@@ -399,39 +431,41 @@ def tile_list_plankton_tendency_kernel(
                 1.0, 0.0, ALU.mult, ALU.add,
             )
         saturate(2)
-        lose(0, 4)
+        lose_unit(0, 4)
         multiply(1)
-        lose(1, 1)
+        lose_unit(1, 1)
         release(2)
         grow(3, 2)
         release(3)
         saturate(3)
-        lose(2, 5)
-        lose(3, 3)
+        lose_unit(2, 5)
+        lose_unit(3, 3)
         multiply(2)
         grow(4, 0)
-        subtract(0)
+        subtract_unit(0)
         grow(5, 4)
-        subtract(1)
-        lose(4, 1)
+        subtract_unit(1)
+        lose_unit(4, 1)
         multiply(3)
-        lose(5, 2)
+        lose_unit(5, 2)
+        join_pairs(0)
+        subtract_unit(2)
         w4_codes = held("w4_codes", [P, N], U32)
         w4_scales = held("w4_scales", [P, N], U8)
         quantise(w4_codes[:], w4_scales[:], w4_bf[:])
-        subtract(2)
-        subtract(3)
+        subtract_unit(3)
         finish(0, (6, 5))
         grow(6, 3)
         multiply(4)
-        release(7)
+        join_pairs(1)
         grow(7, 0)
         multiply(5)
         lose(6, 4)
         finish(1, (7, 6))
-        subtract(4)
+        subtract_unit(4)
         lose(7, 1)
-        subtract(5)
+        subtract_unit(5)
+        join_pairs(2, True)
         multiply(6)
         multiply(7)
         finish(2, (2, 5))

@@ -34,12 +34,12 @@ COPIED = (4, 5, 6, 7)
 REACH = 128
 W1_BYTES = PASSES * 2 * H
 WINDOW = W1_BYTES - REACH
-TAB0 = W1_BYTES + 4 * S
+W2_FIRST = W1_BYTES + 4 * S
+TAB0 = W2_FIRST + STAGE - REACH
 W2_SECOND = TAB0 + STAGE - REACH
 TAB2 = W2_SECOND + STAGE
 W1_RAW = TAB2 + STAGE - REACH
-W2_FIRST = W1_RAW + W1_BYTES - REACH
-TAB1 = W2_FIRST + STAGE
+TAB1 = W1_RAW + W1_BYTES
 W2_LAST = TAB1 + STAGE - REACH
 SPARE = W2_LAST + STAGE
 OFFSET = {
@@ -50,7 +50,7 @@ OFFSET = {
     "v_words1": TAB0 + REACH,
     "w2_raw1": W2_SECOND,
     "tab2": TAB2,
-    "drift_cols": TAB0,
+    "drift_cols": TAB2 + REACH + 4 * TILES * N,
     "w4_raw": TAB2 + REACH,
     "saturated4": TAB2 + REACH,
     "saturated5": TAB2 + REACH + 4 * HALF,
@@ -170,10 +170,9 @@ def tile_list_plankton_tendency_kernel(
 
         w1_codes = order_columns("w1_codes", w1_raw, U8)
         load_tab(2)
-        load_w2(0)
         last_scales = held("last_scales", [P, S], U8)
         for d in range(QUADS):
-            nc.scalar.dma_start(
+            nc.sync.dma_start(
                 last_scales[32 * d : 32 * d + 4, :].bitcast(I32),
                 gathered_scales[32 * d + 6 : 32 * d + 32 : 8, :].bitcast(I32),
             )
@@ -185,11 +184,10 @@ def tile_list_plankton_tendency_kernel(
             entries = offsets[:, lo // 16 : hi // 16]
             nc.vector.tensor_copy(v_words[a][:, lo:hi], tab[a][:].bitcast(U32).indirect(entries))
 
-        gather_words(0, 0, S)
+        gather_words(0, 0, HALF)
+        gather_words(0, HALF, S)
+        load_w2(0)
         load_w2(1)
-        drift_cols = held("drift_cols", [P, OUT_TILES], F32)
-        with nc.allow_non_contiguous_dma(reason="one drift value for each partition and tile of out"):
-            nc.sync.dma_start(drift_cols[:], drift.rearrange("(m p) -> p m", p=P))
         gather_words(1, 0, HALF)
         gather_words(1, HALF, S)
         load_w2(2)
@@ -201,6 +199,9 @@ def tile_list_plankton_tendency_kernel(
         w4_rows = w4.rearrange("(q t i) n -> t q i n", t=TILES, i=RUN)
         for t in range(TILES):
             nc.sync.dma_start(w4_raw[:, t, :], w4_rows[t])
+        drift_cols = held("drift_cols", [P, OUT_TILES], F32)
+        with nc.allow_non_contiguous_dma(reason="one drift value for each partition and tile of out"):
+            nc.sync.dma_start(drift_cols[:], drift.rearrange("(m p) -> p m", p=P))
 
         def quantise(codes, scales, values):
             nc.vector.quantize_mx(out=codes.bitcast(FP8X4), scales=scales, in_=values)

@@ -31,6 +31,7 @@ UNITS = 8
 STAGE = 4 * T
 
 COPIED = (4, 5, 6, 7)
+SLICED = (6, 7)
 REACH = 128
 W1_BYTES = PASSES * 2 * H
 WINDOW = W1_BYTES - REACH
@@ -220,6 +221,11 @@ def tile_list_plankton_tendency_kernel(
 
         def unit_pass(acc, codes, scales, a, unit, order=(0, 1, 2)):
             quarter, u = divmod(unit, 2)
+            if unit in SLICED:
+                for t in range(TILES):
+                    table_pass(acc[:, SLICE * t : SLICE * (t + 1)], codes(a, t), scales(a, t), a, SLICE * unit, SLICE,
+                               a == order[0] and t == 0, a == order[-1] and t == TILES - 1)
+                return
             for e in range(2):
                 t = 2 * u + e
                 table_pass(acc[:, QUARTER * e : QUARTER * (e + 1)], codes(a, t), scales(a, t),
@@ -288,21 +294,21 @@ def tile_list_plankton_tendency_kernel(
             for a in range(PASSES):
                 unit_pass(loss[unit], w3_tile, w3_scale_tile, a, unit)
 
-        def weave(acc):
-            return acc[:].rearrange("p (e c) -> p c e", e=2)
+        def weave(acc, unit):
+            return acc[:].rearrange("p (e c) -> p c e", e=TILES if unit in SLICED else 2)
 
-        def woven(values):
-            return values.rearrange("p (c e) -> p c e", e=2)
+        def woven(values, unit):
+            return values.rearrange("p (c e) -> p c e", e=TILES if unit in SLICED else 2)
 
         def saturate(quarter):
             units = (2 * quarter, 2 * quarter + 1)
             magnitude, drive, root, inverse = {}, {}, {}, {}
             for unit in units:
                 magnitude[unit] = ring.tile([P, HALF], F32, name="magnitude")
-                nc.scalar.activation(woven(magnitude[unit][:]), weave(uptake[unit]), ACT.Abs)
+                nc.scalar.activation(woven(magnitude[unit][:], unit), weave(uptake[unit], unit), ACT.Abs)
                 if unit in COPIED:
                     drive[unit] = ring.tile([P, HALF], F32, name="drive", bufs=4)
-                    nc.scalar.copy(woven(drive[unit][:]), weave(uptake[unit]))
+                    nc.scalar.copy(woven(drive[unit][:], unit), weave(uptake[unit], unit))
             for unit in units:
                 root[unit] = ring.tile([P, HALF], F32, name="root", bufs=4)
                 nc.scalar.activation(root[unit][:], magnitude[unit][:], ACT.Abs_reciprocal_sqrt, bias=1.0)
@@ -320,25 +326,22 @@ def tile_list_plankton_tendency_kernel(
                     pending[unit] = inverse[unit]
 
         def release(unit):
-            nc.vector.tensor_tensor(woven(saturated[unit][:]), weave(uptake[unit]), woven(pending[unit][:]), ALU.mult)
+            nc.vector.tensor_tensor(woven(saturated[unit][:], unit), weave(uptake[unit], unit),
+                                    woven(pending[unit][:], unit), ALU.mult)
 
         gain = [held(f"gain{quarter}", [P, 2, HALF], F32) for quarter in range(4)]
 
         def multiply(unit):
             quarter, u = divmod(unit, 2)
-            nc.vector.tensor_tensor(woven(gain[quarter][:, u, :]), weave(growth[unit]),
-                                    woven(saturated[unit][:]), ALU.mult)
+            nc.vector.tensor_tensor(woven(gain[quarter][:, u, :], unit), weave(growth[unit], unit),
+                                    woven(saturated[unit][:], unit), ALU.mult)
 
         def subtract(j):
             quarter, side = divmod(j, 2)
             if side == 0:
                 h_bf[quarter] = ring.tile([P, TILES * QUARTER], BF16, name="h_bf", align_bytes=64, bufs=4)
-            nc.vector.tensor_tensor(
-                h_bf[quarter][:, HALF * side : HALF * (side + 1)].rearrange("p (c u e) -> p c u e", u=2, e=2),
-                gain[quarter][:, :, 2 * SLICE * side : 2 * SLICE * (side + 1)].rearrange("p u (c e) -> p c u e", e=2),
-                loss[j][:].rearrange("p (u e c) -> p c u e", u=2, e=2),
-                ALU.subtract,
-            )
+            nc.vector.tensor_tensor(woven(h_bf[quarter][:, HALF * side : HALF * (side + 1)], j),
+                                    woven(gain[quarter][:, side, :], j), weave(loss[j], j), ALU.subtract)
 
 
         h_pairs = {}
@@ -347,8 +350,8 @@ def tile_list_plankton_tendency_kernel(
             quarter, u = divmod(unit, 2)
             if u == 0:
                 h_pairs[quarter] = ring.tile([P, 2, HALF], BF16, name="h_pairs", bufs=3)
-            nc.vector.tensor_tensor(woven(h_pairs[quarter][:, u, :]), woven(gain[quarter][:, u, :]),
-                                    weave(loss[unit]), ALU.subtract)
+            nc.vector.tensor_tensor(woven(h_pairs[quarter][:, u, :], unit), woven(gain[quarter][:, u, :], unit),
+                                    weave(loss[unit], unit), ALU.subtract)
 
         def join_pairs(quarter, on_scalar=False):
             h_bf[quarter] = ring.tile([P, TILES * QUARTER], BF16, name="h_bf", align_bytes=64, bufs=4)
@@ -458,7 +461,7 @@ def tile_list_plankton_tendency_kernel(
         finish(0, (6, 5))
         grow(6, 3)
         multiply(4)
-        join_pairs(1)
+        join_pairs(1, True)
         grow(7, 0)
         multiply(5)
         lose(6, 4)
@@ -468,9 +471,9 @@ def tile_list_plankton_tendency_kernel(
         subtract_unit(5)
         join_pairs(2, True)
         multiply(6)
-        multiply(7)
         finish(2, (2, 5))
         subtract(6)
+        multiply(7)
         finish_slice(6, 3, False)
         subtract(7)
         finish_slice(7, 0, True)

@@ -253,7 +253,8 @@ def tile_list_plankton_tendency_kernel(
             source = w2_raw[a][:].rearrange("p j (q t i) -> p t q j i", t=TILES, q=RUNS)[:, 2 * u : 2 * u + 2]
             if on_gpsimd:
                 for e in range(2):
-                    nc.gpsimd.tensor_scalar(rounded[:, e], source[:, e], 1.0, 0.0, ALU.mult, ALU.add)
+                    nc.gpsimd.tensor_scalar(rounded[:, e].rearrange("p q j i -> p q i j"),
+                                            source[:, e].rearrange("p q j i -> p q i j"), 1.0, 0.0, ALU.mult, ALU.add)
             else:
                 nc.vector.tensor_copy(rounded, source)
 
@@ -430,8 +431,8 @@ def tile_list_plankton_tendency_kernel(
         w4_bf = held("w4_bf", [P, TILES * N], BF16)
         for m in range(OUT_TILES):
             nc.gpsimd.tensor_scalar(
-                w4_bf[:, TILES * P * m : TILES * P * (m + 1)].rearrange("p (c i t) -> p c t i", t=TILES, i=4),
-                w4_raw[:, :, P * m : P * (m + 1)].rearrange("p t (c i) -> p c t i", i=4),
+                w4_bf[:, TILES * P * m : TILES * P * (m + 1)].rearrange("p (c t) -> p c t", t=TILES),
+                w4_raw[:, :, P * m : P * (m + 1)].rearrange("p t c -> p c t"),
                 1.0, 0.0, ALU.mult, ALU.add,
             )
         saturate(2)

@@ -61,19 +61,19 @@ OFFSET = {
     "w2_raw0": W2_FIRST,
     "tab1": TAB1,
     "w3_raw": TAB1,
-    "saturated3": TAB1,
-    "w4_codes": TAB1,
     "w4_bf": SPARE + 16 * HALF - REACH,
     "w2_raw2": W2_LAST,
     "w2_codes1_1": W2_LAST + REACH,
     "w2_bf0_0": SPARE,
     "saturated0": SPARE,
+    "saturated3": SPARE + 32 * HALF,
+    "w4_codes": SPARE + 32 * HALF,
     "w2_bf0_1": SPARE + 4 * HALF,
     "w2_bf1_1": SPARE + 4 * HALF,
     "w2_bf2_0": SPARE + 8 * HALF,
-    "w3_scale_rows": SPARE + 8 * HALF,
+    "w2_bf1_0": SPARE + 20 * HALF + 2 * N * TILES,
+    "w3_scale_rows": SPARE + 20 * HALF + 2 * N * TILES,
     "w2_bf2_1": SPARE + 12 * HALF,
-    "saturated2": TAB1 + 4 * HALF,
 }
 
 
@@ -269,7 +269,7 @@ def tile_list_plankton_tendency_kernel(
 
         growth, loss, saturated, pending, h_bf = {}, {}, {}, {}, {}
 
-        def grow(unit, number, passes=(0, 1, 2)):
+        def grow(unit, number=None, passes=(0, 1, 2)):
             if unit not in growth:
                 growth[unit] = bank(number)
             for a in passes:
@@ -280,12 +280,11 @@ def tile_list_plankton_tendency_kernel(
             for t in range(TILES):
                 for a in range(PASSES):
                     table_pass(loss[j][:, SLICE * t : SLICE * (t + 1)],
-                               w3_codes[:, a, P * t : P * (t + 1)].bitcast(FP8X4),
-                               w3_scale_rows[4 * (a + 1) : P, 0, P * t : P * (t + 1)], a, SLICE * j, SLICE,
+                               w3_tile(a, t), w3_scale_tile(a, t), a, SLICE * j, SLICE,
                                a == 0, a == PASSES - 1)
 
         def w3_tile(a, t):
-            return w3_codes[:, a, P * t : P * (t + 1)].bitcast(FP8X4)
+            return w3_pairs[t // 2][:, t % 2, a, :].bitcast(FP8X4)
 
         def w3_scale_tile(a, t):
             return w3_scale_rows[4 * (a + 1) : P, 0, P * t : P * (t + 1)]
@@ -301,15 +300,18 @@ def tile_list_plankton_tendency_kernel(
         def woven(values, unit):
             return values.rearrange("p (c e) -> p c e", e=TILES if unit in SLICED else 2)
 
-        def saturate(quarter):
-            units = (2 * quarter, 2 * quarter + 1)
-            magnitude, drive, root, inverse = {}, {}, {}, {}
-            for unit in units:
-                magnitude[unit] = ring.tile([P, HALF], F32, name="magnitude")
+        magnitude, drive, root, inverse = {}, {}, {}, {}
+
+        def read_out(quarter):
+            for unit in (2 * quarter, 2 * quarter + 1):
+                magnitude[unit] = ring.tile([P, HALF], F32, name="magnitude", bufs=4)
                 nc.scalar.activation(woven(magnitude[unit][:], unit), weave(uptake[unit], unit), ACT.Abs)
                 if unit in COPIED:
                     drive[unit] = ring.tile([P, HALF], F32, name="drive", bufs=4)
                     nc.scalar.copy(woven(drive[unit][:], unit), weave(uptake[unit], unit))
+
+        def saturate(quarter):
+            units = (2 * quarter, 2 * quarter + 1)
             for unit in units:
                 root[unit] = ring.tile([P, HALF], F32, name="root", bufs=4)
                 nc.scalar.activation(root[unit][:], magnitude[unit][:], ACT.Abs_reciprocal_sqrt, bias=1.0)
@@ -341,8 +343,17 @@ def tile_list_plankton_tendency_kernel(
             quarter, side = divmod(j, 2)
             if side == 0:
                 h_bf[quarter] = ring.tile([P, TILES * QUARTER], BF16, name="h_bf", align_bytes=64, bufs=4)
-            nc.vector.tensor_tensor(woven(h_bf[quarter][:, HALF * side : HALF * (side + 1)], j),
-                                    woven(gain[quarter][:, side, :], j), weave(loss[j], j), ALU.subtract)
+            values = h_bf[quarter][:, HALF * side : HALF * (side + 1)]
+            if j in SLICED:
+                nc.vector.tensor_tensor(woven(values, j), woven(gain[quarter][:, side, :], j), weave(loss[j], j),
+                                        ALU.subtract)
+            else:
+                nc.vector.tensor_tensor(
+                    values.rearrange("p (c u e) -> p c u e", u=2, e=2),
+                    gain[quarter][:, :, QUARTER * side : QUARTER * (side + 1)].rearrange("p u (c e) -> p c u e", e=2),
+                    loss[j][:].rearrange("p (u e c) -> p c u e", u=2, e=2),
+                    ALU.subtract,
+                )
 
 
         h_pairs = {}
@@ -405,7 +416,29 @@ def tile_list_plankton_tendency_kernel(
             quarter, side = divmod(j, 2)
             tendencies(h_bf[quarter][:, HALF * side : HALF * (side + 1)], SLICE * j, SLICE, (number,), on_vector)
 
+        w3_pairs = {}
+
+        def order_w3(u):
+            w3_pairs[u] = held(f"w3_pair{u}", [P, 2, PASSES, P], U32)
+            nc.vector.tensor_copy(
+                w3_pairs[u][:].bitcast(I32).rearrange("p e a (q w) -> p e a q w", q=RUNS),
+                w3_raw[:].rearrange("p a (q t w) -> p t a q w", t=TILES, q=RUNS)[:, 2 * u : 2 * u + 2],
+            )
+
+        w4_bf = held("w4_bf", [P, TILES * N], BF16)
+
+        def round_w4():
+            for m in range(OUT_TILES):
+                nc.gpsimd.tensor_scalar(
+                    w4_bf[:, TILES * P * m : TILES * P * (m + 1)].rearrange("p (c t) -> p c t", t=TILES),
+                    w4_raw[:, :, P * m : P * (m + 1)].rearrange("p t c -> p c t"),
+                    1.0, 0.0, ALU.mult, ALU.add,
+                )
+
+        read_out(0)
         saturate(0)
+        read_out(2)
+        read_out(1)
         saturate(1)
         round_w2(0, 0)
         round_w2(0, 1)
@@ -416,65 +449,62 @@ def tile_list_plankton_tendency_kernel(
         release(0)
         release(1)
         quantise_w2(1, 0)
+        w3_scale_rows = order_columns("w3_scale_rows", w3_scales_raw, U8)
         grow(0, 0, (0, 1))
+        grow(2, 1, (0, 1))
+        grow(1, 4, (0,))
+        grow(3, 5, (0,))
         round_w2(2, 0)
         round_w2(2, 1)
         quantise_w2(2, 0)
-        grow(0, 0, (2,))
+        grow(0, passes=(2,))
+        grow(2, passes=(2,))
         quantise_w2(1, 1)
         quantise_w2(2, 1)
-        grow(1, 1)
+        grow(1, passes=(1, 2))
+        grow(3, passes=(1, 2))
         multiply(0)
-        grow(2, 0)
-        w3_scale_rows = order_columns("w3_scale_rows", w3_scales_raw, U8)
-        w3_codes = order_columns("w3_codes", w3_raw, U32)
-        w4_bf = held("w4_bf", [P, TILES * N], BF16)
-        for m in range(OUT_TILES):
-            nc.gpsimd.tensor_scalar(
-                w4_bf[:, TILES * P * m : TILES * P * (m + 1)].rearrange("p (c t) -> p c t", t=TILES),
-                w4_raw[:, :, P * m : P * (m + 1)].rearrange("p t c -> p c t"),
-                1.0, 0.0, ALU.mult, ALU.add,
-            )
-        saturate(2)
-        lose_unit(0, 4)
+        order_w3(0)
+        order_w3(1)
+        round_w4()
+        lose_unit(0, 0)
         multiply(1)
-        lose_unit(1, 1)
+        lose_unit(1, 4)
+        saturate(2)
         release(2)
-        grow(3, 2)
-        release(3)
-        saturate(3)
-        lose_unit(2, 5)
-        lose_unit(3, 3)
+        lose(2, 2)
         multiply(2)
-        grow(4, 0)
-        subtract_unit(0)
-        grow(5, 4)
-        subtract_unit(1)
-        lose_unit(4, 1)
+        lose(3, 1)
+        release(3)
+        read_out(3)
+        saturate(3)
+        grow(4, 3)
         multiply(3)
-        lose_unit(5, 2)
+        grow(5, 5)
+        subtract_unit(0)
+        lose(4, 0)
+        subtract_unit(1)
+        lose(5, 4)
         join_pairs(0)
-        subtract_unit(2)
+        subtract(2)
         w4_codes = held("w4_codes", [P, N], U32)
         w4_scales = held("w4_scales", [P, N], U8)
         quantise(w4_codes[:], w4_scales[:], w4_bf[:])
-        subtract_unit(3)
-        finish(0, (6, 5))
-        grow(6, 3)
+        subtract(3)
+        finish(0, (2, 6))
+        grow(6, 1)
+        grow(7, 7)
         multiply(4)
-        join_pairs(1, True)
-        grow(7, 0)
+        lose(6, 3)
         multiply(5)
-        lose(6, 4)
-        finish(1, (7, 6))
-        subtract_unit(4)
-        lose(7, 1)
-        subtract_unit(5)
-        join_pairs(2, True)
+        finish(1, (5, 6))
+        subtract(4)
+        lose(7, 0)
+        subtract(5)
         multiply(6)
-        finish(2, (2, 5))
+        finish(2, (2, 4))
         subtract(6)
         multiply(7)
-        finish_slice(6, 3, False)
+        finish_slice(6, 1, False)
         subtract(7)
-        finish_slice(7, 0, True)
+        finish_slice(7, 3, True)

@@ -219,9 +219,9 @@ def tile_list_plankton_tendency_kernel(
                 stop=stop,
             )
 
-        def unit_pass(acc, codes, scales, a, unit, order=(0, 1, 2)):
+        def unit_pass(acc, codes, scales, a, unit, order=(0, 1, 2), sliced=False):
             quarter, u = divmod(unit, 2)
-            if unit in SLICED:
+            if sliced:
                 for t in range(TILES):
                     table_pass(acc[:, SLICE * t : SLICE * (t + 1)], codes(a, t), scales(a, t), a, SLICE * unit, SLICE,
                                a == order[0] and t == 0, a == order[-1] and t == TILES - 1)
@@ -273,7 +273,7 @@ def tile_list_plankton_tendency_kernel(
             if unit not in growth:
                 growth[unit] = bank(number)
             for a in passes:
-                unit_pass(growth[unit], w2_tile, w2_scale_tile, a, unit, passes if len(passes) == PASSES else (0, 1, 2))
+                unit_pass(growth[unit], w2_tile, w2_scale_tile, a, unit, sliced=unit in SLICED)
 
         def lose(j, number):
             loss[j] = bank(number)
@@ -294,21 +294,22 @@ def tile_list_plankton_tendency_kernel(
             for a in range(PASSES):
                 unit_pass(loss[unit], w3_tile, w3_scale_tile, a, unit)
 
-        def weave(acc, unit):
-            return acc[:].rearrange("p (e c) -> p c e", e=TILES if unit in SLICED else 2)
+        def weave(acc, tiles=2):
+            return acc[:].rearrange("p (e c) -> p c e", e=tiles)
 
-        def woven(values, unit):
-            return values.rearrange("p (c e) -> p c e", e=TILES if unit in SLICED else 2)
+        def woven(values, tiles=2):
+            return values.rearrange("p (c e) -> p c e", e=tiles)
 
         magnitude, drive, root, inverse = {}, {}, {}, {}
+        last_saturated = held("last_saturated", [P, 2, HALF], F32)
 
         def read_out(quarter):
             for unit in (2 * quarter, 2 * quarter + 1):
                 magnitude[unit] = ring.tile([P, HALF], F32, name="magnitude", bufs=4)
-                nc.scalar.activation(woven(magnitude[unit][:], unit), weave(uptake[unit], unit), ACT.Abs)
+                nc.scalar.activation(woven(magnitude[unit][:]), weave(uptake[unit]), ACT.Abs)
                 if unit in COPIED:
                     drive[unit] = ring.tile([P, HALF], F32, name="drive", bufs=4)
-                    nc.scalar.copy(woven(drive[unit][:], unit), weave(uptake[unit], unit))
+                    nc.scalar.copy(woven(drive[unit][:]), weave(uptake[unit]))
 
         def saturate(quarter):
             units = (2 * quarter, 2 * quarter + 1)
@@ -319,42 +320,46 @@ def tile_list_plankton_tendency_kernel(
                 inverse[unit] = ring.tile([P, HALF], F32, name="inverse", bufs=4)
                 nc.scalar.activation(inverse[unit][:], root[unit][:], ACT.Square)
             for unit in units:
-                saturated[unit] = held(f"saturated{unit}", [P, HALF], F32)
-                if unit in COPIED:
-                    for lo in (0, QUARTER):
-                        part = slice(lo, lo + QUARTER)
-                        nc.gpsimd.tensor_tensor(saturated[unit][:, part], drive[unit][:, part],
-                                                inverse[unit][:, part], ALU.mult)
+                if unit in SLICED:
+                    saturated[unit] = last_saturated[:, unit % 2, :]
                 else:
+                    saturated[unit] = held(f"saturated{unit}", [P, HALF], F32)[:]
+                if unit not in COPIED:
                     pending[unit] = inverse[unit]
+            parts = [(unit, lo) for unit in units for lo in (0, QUARTER) if unit in COPIED]
+            if units == SLICED:
+                parts = sorted(parts, key=lambda part: part[1])
+            for unit, lo in parts:
+                part = slice(lo, lo + QUARTER)
+                nc.gpsimd.tensor_tensor(saturated[unit][:, part], drive[unit][:, part],
+                                        inverse[unit][:, part], ALU.mult)
 
         def release(unit):
-            nc.vector.tensor_tensor(woven(saturated[unit][:], unit), weave(uptake[unit], unit),
-                                    woven(pending[unit][:], unit), ALU.mult)
+            nc.vector.tensor_tensor(woven(saturated[unit]), weave(uptake[unit]),
+                                    woven(pending[unit][:]), ALU.mult)
 
         gain = [held(f"gain{quarter}", [P, 2, HALF], F32) for quarter in range(4)]
 
         def multiply(unit):
             quarter, u = divmod(unit, 2)
-            nc.vector.tensor_tensor(woven(gain[quarter][:, u, :], unit), weave(growth[unit], unit),
-                                    woven(saturated[unit][:], unit), ALU.mult)
+            if unit in SLICED:
+                nc.vector.tensor_tensor(
+                    gain[quarter][:, u, :].rearrange("p (c v e) -> p c v e", v=2, e=2),
+                    growth[unit][:].rearrange("p (v e c) -> p c v e", v=2, e=2),
+                    last_saturated[:, :, QUARTER * u : QUARTER * (u + 1)].rearrange("p v (c e) -> p c v e", e=2),
+                    ALU.mult,
+                )
+            else:
+                nc.vector.tensor_tensor(woven(gain[quarter][:, u, :]), weave(growth[unit]),
+                                        woven(saturated[unit]), ALU.mult)
 
         def subtract(j):
             quarter, side = divmod(j, 2)
             if side == 0:
                 h_bf[quarter] = ring.tile([P, TILES * QUARTER], BF16, name="h_bf", align_bytes=64, bufs=4)
             values = h_bf[quarter][:, HALF * side : HALF * (side + 1)]
-            if j in SLICED:
-                nc.vector.tensor_tensor(woven(values, j), woven(gain[quarter][:, side, :], j), weave(loss[j], j),
-                                        ALU.subtract)
-            else:
-                nc.vector.tensor_tensor(
-                    values.rearrange("p (c u e) -> p c u e", u=2, e=2),
-                    gain[quarter][:, :, QUARTER * side : QUARTER * (side + 1)].rearrange("p u (c e) -> p c u e", e=2),
-                    loss[j][:].rearrange("p (u e c) -> p c u e", u=2, e=2),
-                    ALU.subtract,
-                )
-
+            nc.vector.tensor_tensor(woven(values, TILES), woven(gain[quarter][:, side, :], TILES),
+                                    weave(loss[j], TILES), ALU.subtract)
 
         h_pairs = {}
 
@@ -362,8 +367,8 @@ def tile_list_plankton_tendency_kernel(
             quarter, u = divmod(unit, 2)
             if u == 0:
                 h_pairs[quarter] = ring.tile([P, 2, HALF], BF16, name="h_pairs", bufs=3)
-            nc.vector.tensor_tensor(woven(h_pairs[quarter][:, u, :], unit), woven(gain[quarter][:, u, :], unit),
-                                    weave(loss[unit], unit), ALU.subtract)
+            nc.vector.tensor_tensor(woven(h_pairs[quarter][:, u, :]), woven(gain[quarter][:, u, :]),
+                                    weave(loss[unit]), ALU.subtract)
 
         def join_pairs(quarter, on_scalar=False):
             h_bf[quarter] = ring.tile([P, TILES * QUARTER], BF16, name="h_bf", align_bytes=64, bufs=4)
@@ -472,9 +477,9 @@ def tile_list_plankton_tendency_kernel(
         lose_unit(1, 4)
         saturate(2)
         release(2)
-        lose(2, 2)
+        lose_unit(2, 2)
         multiply(2)
-        lose(3, 1)
+        lose_unit(3, 1)
         release(3)
         read_out(3)
         saturate(3)
@@ -482,25 +487,27 @@ def tile_list_plankton_tendency_kernel(
         multiply(3)
         grow(5, 5)
         subtract_unit(0)
-        lose(4, 0)
+        lose_unit(4, 0)
         subtract_unit(1)
-        lose(5, 4)
+        lose_unit(5, 4)
         join_pairs(0)
-        subtract(2)
+        subtract_unit(2)
         w4_codes = held("w4_codes", [P, N], U32)
         w4_scales = held("w4_scales", [P, N], U8)
         quantise(w4_codes[:], w4_scales[:], w4_bf[:])
-        subtract(3)
+        subtract_unit(3)
         finish(0, (2, 6))
         grow(6, 1)
         grow(7, 7)
         multiply(4)
+        join_pairs(1)
         lose(6, 3)
         multiply(5)
         finish(1, (5, 6))
-        subtract(4)
+        subtract_unit(4)
         lose(7, 0)
-        subtract(5)
+        subtract_unit(5)
+        join_pairs(2, True)
         multiply(6)
         finish(2, (2, 4))
         subtract(6)

from contextlib import ExitStack

import concourse.mybir as mybir

K, T, S, H, N = 1536, 2048, 1024, 512, 384
FLOPS = 2 * (3 * K * H * S + H * N * S)

F32 = mybir.dt.float32
BF16 = mybir.dt.bfloat16
I32 = mybir.dt.int32
U32 = mybir.dt.uint32
U16 = mybir.dt.uint16
U8 = mybir.dt.uint8
FP8X4 = mybir.dt.float8_e4m3fn_x4
FP4X4 = mybir.dt.float4_e2m1fn_x4
ACT = mybir.ActivationFunctionType
ALU = mybir.AluOpType

P = 128
PACK = 4
PASSES = K // (P * PACK)
QUADS = 4
RUN = 8
RUNS = P // RUN
HALF = 512
QUARTER = 256
SLICE = 128
TILES = H // P
OUT_TILES = N // P
UNITS = 8
STAGE = 4 * T

COPIED = (4, 5, 6, 7)
SLICED = (6, 7)
REACH = 128
W1_BYTES = PASSES * 2 * H
WINDOW = W1_BYTES - REACH
W2_FIRST = W1_BYTES + 4 * S
TAB0 = W2_FIRST + STAGE - REACH
W2_SECOND = TAB0 + STAGE - REACH
TAB2 = W2_SECOND + STAGE
W1_RAW = TAB2 + STAGE - REACH
TAB1 = W1_RAW + W1_BYTES
W2_LAST = TAB1 + STAGE - REACH
SPARE = W2_LAST + STAGE
OFFSET = {
    "w1_codes": 0,
    "scale_window": WINDOW,
    "v_words0": W1_BYTES,
    "tab0": TAB0,
    "v_words1": TAB0 + REACH,
    "w2_raw1": W2_SECOND,
    "tab2": TAB2,
    "drift_cols": TAB2 + REACH + 4 * TILES * N,
    "w4_raw": TAB2 + REACH,
    "saturated4": TAB2 + REACH,
    "saturated5": TAB2 + REACH + 4 * HALF,
    "w1_raw": W1_RAW,
    "last_scales": W1_RAW + REACH,
    "w1_scale_rows": W1_RAW + REACH + S,
    "w2_raw0": W2_FIRST,
    "tab1": TAB1,
    "w3_raw": TAB1,
    "w4_bf": SPARE + 16 * HALF - REACH,
    "w2_raw2": W2_LAST,
    "w2_codes1_1": W2_LAST + REACH,
    "w2_bf0_0": SPARE,
    "saturated0": SPARE,
    "saturated3": SPARE + 32 * HALF,
    "w4_codes": SPARE + 32 * HALF,
    "w2_bf0_1": SPARE + 4 * HALF,
    "w2_bf1_1": SPARE + 4 * HALF,
    "w2_bf2_0": SPARE + 8 * HALF,
    "w2_bf1_0": SPARE + 20 * HALF + 2 * N * TILES,
    "w3_scale_rows": SPARE + 20 * HALF + 2 * N * TILES,
    "w2_bf2_1": SPARE + 12 * HALF,
}


def tile_list_plankton_tendency_kernel(
    tc, tab_words, tab_scales, offs, w1_words, w1_scales, w2, w3_words, w3_scales, w4, drift, out
):
    nc = tc.nc
    with ExitStack() as ctx:
        keep = ctx.enter_context(tc.tile_pool(name="keep", bufs=1))
        shared = ctx.enter_context(tc.tile_pool(name="shared", bufs=1))
        ring = ctx.enter_context(tc.tile_pool(name="ring", bufs=2))
        psum = ctx.enter_context(tc.psum_pool(name="psum", bufs=1))

        def held(name, shape, dtype):
            if name in OFFSET:
                return shared.tile(shape, dtype, name=name, align_bytes=64, offset=OFFSET[name])
            return keep.tile(shape, dtype, name=name, align_bytes=64)

        def bank(number):
            return psum.tile([P, HALF], F32, name=f"bank{number}", tag=f"bank{number}")

        offsets = keep.tile([P, S // 16], U16, name="offsets")
        nc.sync.dma_start(offsets[:], offs)

        warm_in = held("warm_in", [P, 16], F32)
        warm_out = held("warm_out", [P, 16], F32)
        nc.vector.memset(warm_in[:], 1.0)
        nc.scalar.activation(warm_out[:], warm_in[:], ACT.Abs_reciprocal_sqrt)

        scale_window = held("scale_window", [P, T], U8)
        w1_scales_raw = held("w1_scales_raw", [P, PASSES, H], U8)
        w3_scales_raw = held("w3_scales_raw", [P, 1, H], U8)
        early_scales = held("early_scales", [P, 2, S], U8)
        nc.vector.memset(w1_scales_raw[:].bitcast(I32), 0)
        nc.vector.memset(early_scales[:].bitcast(I32), 0)
        nc.vector.memset(w3_scales_raw[:].bitcast(I32), 0)

        scale_words = tab_scales.bitcast(I32)
        for x in range(4):
            first = x // 2
            nc.sync.dma_start(
                scale_window[x:P:4, :].bitcast(I32), scale_words[first : first + 2].rearrange("a q n -> q a n")
            )

        tab = {}

        def load_tab(a):
            tab[a] = held(f"tab{a}", [P, T], I32)
            nc.sync.dma_start(tab[a][:], tab_words[a].rearrange("p t i -> p (t i)").bitcast(I32))

        w2_raw = {}

        def load_w2(a):
            w2_raw[a] = held(f"w2_raw{a}", [P, PACK, H], F32)
            rows = w2[P * PACK * a : P * PACK * (a + 1), :]
            nc.sync.dma_start(w2_raw[a][:], rows.rearrange("(p j) c -> p j c", j=PACK))

        def quadrant_rows(scales, d):
            return scales.bitcast(I32)[:, 4 * d : 4 * d + 4, :]

        def order_columns(name, raw, dtype, on_scalar=False):
            done = held(name, list(raw.shape), dtype)
            word = U32 if on_scalar else I32
            source = raw[:].bitcast(word).rearrange("p a (q t w) -> p t a q w", t=TILES, q=RUNS)
            target = done[:].bitcast(word).rearrange("p a (t q w) -> p t a q w", t=TILES, q=RUNS)
            if on_scalar:
                nc.scalar.copy(target, source)
            else:
                nc.vector.tensor_copy(target, source)
            return done

        w1_raw = held("w1_raw", [P, PASSES, 2 * H], U8)
        nc.sync.dma_start(w1_raw[:].bitcast(I32), w1_words.bitcast(I32).rearrange("a p n -> p a n"))
        load_tab(0)
        load_tab(1)

        for d in range(QUADS):
            queue = nc.gpsimd if d < 2 else nc.scalar
            queue.dma_start(
                w1_scales_raw[32 * d : 32 * d + 4, :, :].bitcast(I32),
                quadrant_rows(w1_scales, d).rearrange("a s n -> s a n"),
            )
        for d in range(QUADS):
            nc.gpsimd.dma_start(
                w3_scales_raw[32 * d + 4 : 32 * d + 16, 0, :].bitcast(I32), quadrant_rows(w3_scales, d)
            )

        gathered_scales = held("gathered_scales", [P, S], U8)
        nc.vector.tensor_copy(gathered_scales[:], scale_window[:].indirect(offsets[:]))
        for d in range(QUADS):
            nc.scalar.dma_start(
                early_scales[32 * d : 32 * d + 4, :, :].bitcast(I32),
                gathered_scales[32 * d : 32 * d + 32 : 4, :].bitcast(I32),
            )

        w1_codes = order_columns("w1_codes", w1_raw, U8)
        load_tab(2)
        last_scales = held("last_scales", [P, S], U8)
        for d in range(QUADS):
            nc.sync.dma_start(
                last_scales[32 * d : 32 * d + 4, :].bitcast(I32),
                gathered_scales[32 * d + 6 : 32 * d + 32 : 8, :].bitcast(I32),
            )
        w1_scale_rows = order_columns("w1_scale_rows", w1_scales_raw, U8, True)

        v_words = [held(f"v_words{a}", [P, S], U32) for a in range(PASSES)]

        def gather_words(a, lo, hi):
            entries = offsets[:, lo // 16 : hi // 16]
            nc.vector.tensor_copy(v_words[a][:, lo:hi], tab[a][:].bitcast(U32).indirect(entries))

        gather_words(0, 0, HALF)
        gather_words(0, HALF, S)
        load_w2(0)
        load_w2(1)
        gather_words(1, 0, HALF)
        gather_words(1, HALF, S)
        load_w2(2)
        w3_raw = held("w3_raw", [P, PASSES, H], I32)
        nc.sync.dma_start(w3_raw[:], w3_words.rearrange("a p e i -> p a (e i)").bitcast(I32))
        for quarter in range(4):
            gather_words(2, QUARTER * quarter, QUARTER * (quarter + 1))
        w4_raw = held("w4_raw", [P, TILES, N], F32)
        w4_rows = w4.rearrange("(q t i) n -> t q i n", t=TILES, i=RUN)
        for t in range(TILES):
            nc.sync.dma_start(w4_raw[:, t, :], w4_rows[t])
        drift_cols = held("drift_cols", [P, OUT_TILES], F32)
        with nc.allow_non_contiguous_dma(reason="one drift value for each partition and tile of out"):
            nc.sync.dma_start(drift_cols[:], drift.rearrange("(m p) -> p m", p=P))

        def quantise(codes, scales, values):
            nc.vector.quantize_mx(out=codes.bitcast(FP8X4), scales=scales, in_=values)

        def table_pass(acc, codes, scales, a, lo, width, start, stop):
            v_scales = last_scales[:] if a == PASSES - 1 else early_scales[:, a, :]
            nc.tensor.matmul_mx(
                out=acc,
                lhsT=codes,
                lhsT_scale=scales,
                rhs=v_words[a][:, lo : lo + width].bitcast(FP8X4),
                rhs_scale=v_scales[:, lo : lo + width],
                start=start,
                stop=stop,
            )

        def unit_pass(acc, codes, scales, a, unit, order=(0, 1, 2), sliced=False):
            quarter, u = divmod(unit, 2)
            if sliced:
                for t in range(TILES):
                    table_pass(acc[:, SLICE * t : SLICE * (t + 1)], codes(a, t), scales(a, t), a, SLICE * unit, SLICE,
                               a == order[0] and t == 0, a == order[-1] and t == TILES - 1)
                return
            for e in range(2):
                t = 2 * u + e
                table_pass(acc[:, QUARTER * e : QUARTER * (e + 1)], codes(a, t), scales(a, t),
                           a, QUARTER * quarter, QUARTER, a == order[0] and e == 0, a == order[-1] and e == 1)

        def w1_tile(a, t):
            return w1_codes[:, a, 2 * P * t : 2 * P * (t + 1)].bitcast(FP4X4)

        def w1_scale_tile(a, t):
            return w1_scale_rows[:, a, P * t : P * (t + 1)]

        uptake = [bank(unit) for unit in range(UNITS)]
        for unit in range(UNITS):
            order = (0, 1, 2) if unit < 2 else (2, 0, 1)
            for a in order:
                unit_pass(uptake[unit], w1_tile, w1_scale_tile, a, unit, order)

        pairs = [(a, u) for a in range(PASSES) for u in range(2)]
        w2_codes = {(a, u): held(f"w2_codes{a}_{u}", [P, 2 * P], U32) for a, u in pairs}
        w2_scales = {(a, u): held(f"w2_scales{a}_{u}", [P, 2 * P], U8) for a, u in pairs}
        w2_bf = {(a, u): held(f"w2_bf{a}_{u}", [P, PACK * 2 * P], BF16) for a, u in pairs}

        def round_w2(a, u, on_gpsimd=False):
            rounded = w2_bf[a, u][:].rearrange("p (t q i j) -> p t q j i", t=2, q=RUNS, j=PACK)
            source = w2_raw[a][:].rearrange("p j (q t i) -> p t q j i", t=TILES, q=RUNS)[:, 2 * u : 2 * u + 2]
            if on_gpsimd:
                for e in range(2):
                    nc.gpsimd.tensor_scalar(rounded[:, e].rearrange("p q j i -> p q i j"),
                                            source[:, e].rearrange("p q j i -> p q i j"), 1.0, 0.0, ALU.mult, ALU.add)
            else:
                nc.vector.tensor_copy(rounded, source)

        def quantise_w2(a, u):
            quantise(w2_codes[a, u][:], w2_scales[a, u][:], w2_bf[a, u][:])

        def w2_tile(a, t):
            return w2_codes[a, t // 2][:, P * (t % 2) : P * (t % 2 + 1)].bitcast(FP8X4)

        def w2_scale_tile(a, t):
            return w2_scales[a, t // 2][:, P * (t % 2) : P * (t % 2 + 1)]

        growth, loss, saturated, pending, h_bf = {}, {}, {}, {}, {}

        def grow(unit, number=None, passes=(0, 1, 2)):
            if unit not in growth:
                growth[unit] = bank(number)
            for a in passes:
                unit_pass(growth[unit], w2_tile, w2_scale_tile, a, unit, sliced=unit in SLICED)

        def lose(j, number):
            loss[j] = bank(number)
            for t in range(TILES):
                for a in range(PASSES):
                    table_pass(loss[j][:, SLICE * t : SLICE * (t + 1)],
                               w3_tile(a, t), w3_scale_tile(a, t), a, SLICE * j, SLICE,
                               a == 0, a == PASSES - 1)

        def w3_tile(a, t):
            return w3_pairs[t // 2][:, t % 2, a, :].bitcast(FP8X4)

        def w3_scale_tile(a, t):
            return w3_scale_rows[4 * (a + 1) : P, 0, P * t : P * (t + 1)]

        def lose_unit(unit, number):
            loss[unit] = bank(number)
            for a in range(PASSES):
                unit_pass(loss[unit], w3_tile, w3_scale_tile, a, unit)

        def weave(acc, tiles=2):
            return acc[:].rearrange("p (e c) -> p c e", e=tiles)

        def woven(values, tiles=2):
            return values.rearrange("p (c e) -> p c e", e=tiles)

        magnitude, drive, root, inverse = {}, {}, {}, {}
        last_saturated = held("last_saturated", [P, 2, HALF], F32)

        def read_out(quarter):
            for unit in (2 * quarter, 2 * quarter + 1):
                magnitude[unit] = ring.tile([P, HALF], F32, name="magnitude", bufs=4)
                nc.scalar.activation(woven(magnitude[unit][:]), weave(uptake[unit]), ACT.Abs)
                if unit in COPIED:
                    drive[unit] = ring.tile([P, HALF], F32, name="drive", bufs=4)
                    nc.scalar.copy(woven(drive[unit][:]), weave(uptake[unit]))

        def saturate(quarter):
            units = (2 * quarter, 2 * quarter + 1)
            for unit in units:
                root[unit] = ring.tile([P, HALF], F32, name="root", bufs=4)
                nc.scalar.activation(root[unit][:], magnitude[unit][:], ACT.Abs_reciprocal_sqrt, bias=1.0)
            for unit in units:
                inverse[unit] = ring.tile([P, HALF], F32, name="inverse", bufs=4)
                nc.scalar.activation(inverse[unit][:], root[unit][:], ACT.Square)
            for unit in units:
                if unit in SLICED:
                    saturated[unit] = last_saturated[:, unit % 2, :]
                else:
                    saturated[unit] = held(f"saturated{unit}", [P, HALF], F32)[:]
                if unit not in COPIED:
                    pending[unit] = inverse[unit]
            parts = [(unit, lo) for unit in units for lo in (0, QUARTER) if unit in COPIED]
            if units == SLICED:
                parts = sorted(parts, key=lambda part: part[1])
            for unit, lo in parts:
                part = slice(lo, lo + QUARTER)
                nc.gpsimd.tensor_tensor(saturated[unit][:, part], drive[unit][:, part],
                                        inverse[unit][:, part], ALU.mult)

        def release(unit):
            nc.vector.tensor_tensor(woven(saturated[unit]), weave(uptake[unit]),
                                    woven(pending[unit][:]), ALU.mult)

        gain = [held(f"gain{quarter}", [P, 2, HALF], F32) for quarter in range(4)]

        def multiply(unit):
            quarter, u = divmod(unit, 2)
            if unit in SLICED:
                nc.vector.tensor_tensor(
                    gain[quarter][:, u, :].rearrange("p (c v e) -> p c v e", v=2, e=2),
                    growth[unit][:].rearrange("p (v e c) -> p c v e", v=2, e=2),
                    last_saturated[:, :, QUARTER * u : QUARTER * (u + 1)].rearrange("p v (c e) -> p c v e", e=2),
                    ALU.mult,
                )
            else:
                nc.vector.tensor_tensor(woven(gain[quarter][:, u, :]), weave(growth[unit]),
                                        woven(saturated[unit]), ALU.mult)

        def subtract(j):
            quarter, side = divmod(j, 2)
            if side == 0:
                h_bf[quarter] = ring.tile([P, TILES * QUARTER], BF16, name="h_bf", align_bytes=64, bufs=4)
            values = h_bf[quarter][:, HALF * side : HALF * (side + 1)]
            nc.vector.tensor_tensor(woven(values, TILES), woven(gain[quarter][:, side, :], TILES),
                                    weave(loss[j], TILES), ALU.subtract)

        h_pairs = {}

        def subtract_unit(unit):
            quarter, u = divmod(unit, 2)
            if u == 0:
                h_pairs[quarter] = ring.tile([P, 2, HALF], BF16, name="h_pairs", bufs=3)
            nc.vector.tensor_tensor(woven(h_pairs[quarter][:, u, :]), woven(gain[quarter][:, u, :]),
                                    weave(loss[unit]), ALU.subtract)

        def join_pairs(quarter, on_scalar=False):
            h_bf[quarter] = ring.tile([P, TILES * QUARTER], BF16, name="h_bf", align_bytes=64, bufs=4)
            word = U32 if on_scalar else I32
            joined = h_bf[quarter][:].bitcast(word).rearrange("p (c u) -> p c u", u=2)
            pairs_of_tiles = h_pairs[quarter][:].bitcast(word).rearrange("p u c -> p c u")
            if on_scalar:
                nc.scalar.copy(joined, pairs_of_tiles)
            else:
                nc.vector.tensor_copy(joined, pairs_of_tiles)

        def tendencies(values, lo, width, banks, on_vector=False, by_tile=False):
            h_codes = ring.tile([P, width], U32, name="h_codes", align_bytes=64, bufs=4)
            h_scales = ring.tile([P, width], U8, name="h_scales", align_bytes=64, bufs=4)
            quantise(h_codes[:], h_scales[:], values)
            accs = [bank(number) for number in banks]
            result = ring.tile([P, OUT_TILES, width], F32, name="result", bufs=4)
            sums = []
            for m in range(OUT_TILES):
                which, at = divmod(width * m, HALF)
                sums.append(accs[which][:, at : at + width])
                nc.tensor.matmul_mx(
                    out=sums[m],
                    lhsT=w4_codes[:, P * m : P * (m + 1)].bitcast(FP8X4),
                    lhsT_scale=w4_scales[:, P * m : P * (m + 1)],
                    rhs=h_codes[:].bitcast(FP8X4),
                    rhs_scale=h_scales[:],
                    start=True,
                    stop=True,
                )
            if on_vector:
                nc.vector.tensor_tensor(
                    result[:],
                    accs[0][:, 0 : OUT_TILES * width].rearrange("p (m c) -> p m c", m=OUT_TILES),
                    drift_cols[:].unsqueeze(2).to_broadcast([P, OUT_TILES, width]),
                    ALU.add,
                )
            else:
                for m in range(OUT_TILES):
                    nc.scalar.activation(result[:, m, :], sums[m], ACT.Identity, bias=drift_cols[:, m : m + 1])
                    if by_tile:
                        nc.sync.dma_start(out[P * m : P * (m + 1), lo : lo + width], result[:, m, :])
            if not by_tile:
                nc.sync.dma_start(out[:, lo : lo + width].rearrange("(m p) s -> p m s", p=P), result[:])

        def finish(quarter, banks):
            tendencies(h_bf[quarter][:], QUARTER * quarter, QUARTER, banks, False, quarter == 2)

        def finish_slice(j, number, on_vector):
            quarter, side = divmod(j, 2)
            tendencies(h_bf[quarter][:, HALF * side : HALF * (side + 1)], SLICE * j, SLICE, (number,), on_vector)

        w3_pairs = {}

        def order_w3(u):
            w3_pairs[u] = held(f"w3_pair{u}", [P, 2, PASSES, P], U32)
            nc.vector.tensor_copy(
                w3_pairs[u][:].bitcast(I32).rearrange("p e a (q w) -> p e a q w", q=RUNS),
                w3_raw[:].rearrange("p a (q t w) -> p t a q w", t=TILES, q=RUNS)[:, 2 * u : 2 * u + 2],
            )

        w4_bf = held("w4_bf", [P, TILES * N], BF16)

        def round_w4():
            for m in range(OUT_TILES):
                nc.gpsimd.tensor_scalar(
                    w4_bf[:, TILES * P * m : TILES * P * (m + 1)].rearrange("p (c t) -> p c t", t=TILES),
                    w4_raw[:, :, P * m : P * (m + 1)].rearrange("p t c -> p c t"),
                    1.0, 0.0, ALU.mult, ALU.add,
                )

        read_out(0)
        saturate(0)
        read_out(2)
        read_out(1)
        saturate(1)
        round_w2(0, 0)
        round_w2(0, 1)
        quantise_w2(0, 0)
        round_w2(1, 0)
        quantise_w2(0, 1)
        round_w2(1, 1, True)
        release(0)
        release(1)
        quantise_w2(1, 0)
        w3_scale_rows = order_columns("w3_scale_rows", w3_scales_raw, U8)
        grow(0, 0, (0, 1))
        grow(2, 1, (0, 1))
        grow(1, 4, (0,))
        grow(3, 5, (0,))
        round_w2(2, 0)
        round_w2(2, 1)
        quantise_w2(2, 0)
        grow(0, passes=(2,))
        grow(2, passes=(2,))
        quantise_w2(1, 1)
        quantise_w2(2, 1)
        grow(1, passes=(1, 2))
        grow(3, passes=(1, 2))
        multiply(0)
        order_w3(0)
        order_w3(1)
        round_w4()
        lose_unit(0, 0)
        multiply(1)
        lose_unit(1, 4)
        saturate(2)
        release(2)
        lose_unit(2, 2)
        multiply(2)
        lose_unit(3, 1)
        release(3)
        read_out(3)
        saturate(3)
        grow(4, 3)
        multiply(3)
        grow(5, 5)
        subtract_unit(0)
        lose_unit(4, 0)
        subtract_unit(1)
        lose_unit(5, 4)
        join_pairs(0)
        subtract_unit(2)
        w4_codes = held("w4_codes", [P, N], U32)
        w4_scales = held("w4_scales", [P, N], U8)
        quantise(w4_codes[:], w4_scales[:], w4_bf[:])
        subtract_unit(3)
        finish(0, (2, 6))
        grow(6, 1)
        grow(7, 7)
        multiply(4)
        join_pairs(1)
        lose(6, 3)
        multiply(5)
        finish(1, (5, 6))
        subtract_unit(4)
        lose(7, 0)
        subtract_unit(5)
        join_pairs(2, True)
        multiply(6)
        finish(2, (2, 4))
        subtract(6)
        multiply(7)
        finish_slice(6, 1, False)
        subtract(7)
        finish_slice(7, 3, True)
